import numpy as np, ml_dtypes
CORES = [8,9,10,11,12,13]
N = 6
BF = ml_dtypes.bfloat16
def gentries(a):
    return np.ascontiguousarray(a.reshape(8, 16, -1).transpose(0, 2, 1)).reshape(8, -1)
def gtable(e):
    e = np.asarray(e); return np.ascontiguousarray(e.reshape(8, -1, 16).transpose(0, 2, 1)).reshape(128, -1).astype(np.int32)
R, H, LO, UP, SW = 448, 48, 2, 6, 3
S, M, T = LO + 1 + UP, N * R, R + (N - 1) * H
def byrank(v):
    return np.ascontiguousarray(v.reshape(8, -1, R, N).transpose(3, 0, 1, 2)).reshape(N, 8, -1)
def ships(rng, rows):
    return np.argsort(rng.random((N, 8, N - 1, rows)), axis=-1)[..., :H]
def users(rng, low):
    u = np.full((8, M), -1, np.int64)
    for g in range(8):
        for t in rng.permutation(LO):
            o = rng.permutation(M); l = low[g, t, o]; ok = l >= 0; u[g, l[ok]] = o[ok]
    return u
def grow(rng, ship, far, drop=0.05, sweep=False):
    G = np.arange(8)[:, None]; i = np.arange(M); q = i % N; n = i // N; K = (N - 1) * H
    low = np.empty((8, LO, M), np.int64); spot = np.empty((8, LO, M), np.int64); up = np.empty((8, UP, M), np.int64)
    for t in range(LO):
        e = rng.integers(0, K, (8, M))
        if sweep: e = np.where(n >= R // 2, ((n - R // 2) * LO + t) % K, e)
        b = e // H; p = b + (b >= q); k = ship[p, G, q - (q > p), e % H] * N + p
        take = (rng.random((8, M)) < far) & (k < i); own = (rng.random((8, M)) * n).astype(np.int64)
        c = np.where(take, k, own * N + q); none = (~take & (n == 0)) | (rng.random((8, M)) < drop)
        for s in range(t): none |= c == low[:, s]
        low[:, t] = np.where(none, -1 - t, c); spot[:, t] = np.where(none, rng.integers(0, T, (8, M)), np.where(take, R + e, own))
    u = users(rng, low); cand = []
    for x in (u, users(rng, low)):
        v = np.maximum(x, 0); l = low[G, rng.integers(0, LO, (8, M)), v]
        cand += [x, np.where((x >= 0) & (l > i), l, -1), np.where(x >= 0, u[G, v], -1)]
    cand = np.stack(cand); turn = rng.integers(0, UP, (8, M))
    for w in range(UP):
        c = cand[(w + turn) % UP, G, i]; other = i + 1 + (rng.random((8, M)) * (M - 1 - i)).astype(np.int64)
        good = (c > i) & (rng.random((8, M)) < 0.85)
        for s in range(w): good &= c != up[:, s]
        c = np.where(good, c, other); none = (c >= M) | (rng.random((8, M)) < 0.04)
        for s in range(w): none |= c == up[:, s]
        up[:, w] = np.where(none, M + w, c)
    return low, spot, up
def fill(rng, ship, low, spot, up):
    c = np.concatenate([low, np.broadcast_to(np.arange(M), (8, 1, M)), up], 1); real = byrank((c >= 0) & (c < M)).reshape(N, 8, 1, S, R)
    v = (0.03 + 0.09 * rng.random((N, 8, 16, S, R))) * (2 * rng.integers(0, 2, (N, 8, 16, S, R)) - 1)
    v = np.where(real, v, 0.0); v[:, :, :, LO] = 0.75 + 0.75 * rng.random((N, 8, 16, R))
    return {"val": v.reshape(N, 128, S * R).astype(BF), "col": byrank(c).astype(np.int32), "spot": np.stack([gtable(x) for x in byrank(spot)]), "ship": np.stack([gtable(x.reshape(8, -1)) for x in ship])}
def setup_inputs(rng):
    ship = ships(rng, R); return fill(rng, ship, *grow(rng, ship, 0.8))
def setup_inputs_halo(rng):
    ship = ships(rng, R // 2); return fill(rng, ship, *grow(rng, ship, 1.0, 0.0, True))
def setup_inputs_hub(rng):
    ship = rng.integers(0, 3, (N, 8, N - 1, H)); return fill(rng, ship, *grow(rng, ship, 0.95))
def setup_inputs_thin(rng):
    ship = ships(rng, R); low, spot, up = grow(rng, ship, 0.8)
    gone = rng.random((8, 1, M)) < rng.permutation(np.array([1.0, 1.0, 0.95, 0.8, 0.5, 0.5, 0.1, 0.0]))[:, None, None]
    gone = gone | (np.arange(M) % N == rng.integers(0, N))
    low = np.where(gone, -1 - np.arange(LO)[:, None], low); up = np.where(gone, M + np.arange(UP)[:, None], up)
    return fill(rng, ship, low, spot, up)
def setup_inputs_band(rng):
    ship = ships(rng, R); low, spot, up = grow(rng, ship, 0.8); n = np.arange(M) // N; q = np.arange(M) % N
    for g in range(6):
        for t in range(LO):
            b = n - (t + 1) * (g + 1); low[g, t] = np.where(b >= 0, b * N + q, -1 - t); spot[g, t] = np.where(b >= 0, b, 0)
        for w in range(UP):
            b = n + (w + 1) * (g + 1); up[g, w] = np.where(b < R, b * N + q, M + w)
    d = fill(rng, ship, low, spot, up); v = np.sign(d["val"].astype(np.float32)).reshape(N, 8, 16, S, R) * (0.125 - rng.integers(0, 4, (N, 8, 16, S, R)) * 2.0 ** -11)
    v[:, :, :, LO] = rng.choice(np.array([0.75, 0.75390625, 1.4921875, 1.5]), (N, 8, 16, R)); d["val"] = v.reshape(N, 128, S * R).astype(np.float32).astype(BF); return d
def setup_inputs_spread(rng):
    d = setup_inputs(rng); k = np.exp2(rng.integers(-6, 1, (N, 8, 1, S, R))) * (rng.random((N, 8, 1, S, R)) > 0.0625); k[:, :, :, LO] = 1
    d["val"] = (d["val"].astype(np.float32).reshape(N, 8, 16, S, R) * k).reshape(N, 128, S * R).astype(BF); return d
def check_inputs(d):
    bad = []; i = np.arange(R)[None] * N + np.arange(N)[:, None]; row = i[:, None, None]
    c = d["col"].astype(np.int64).reshape(N, 8, S, R); lo, up = c[:, :, :LO], c[:, :, LO + 1:]
    elo = lo == -1 - np.arange(LO)[:, None]; eup = up == M + np.arange(UP)[:, None]
    if not (c[:, :, LO] == i[:, None]).all(): bad.append("the diagonal's column is the row's number")
    if not (elo | ((lo >= 0) & (lo < row))).all(): bad.append("lower columns are below the row's number, or the slot is empty")
    if not (eup | ((up > row) & (up < M))).all(): bad.append("upper columns are above the row's number, or the slot is empty")
    s = np.sort(c, axis=2)
    if (s[:, :, 1:] == s[:, :, :-1]).any(): bad.append("the columns of a row differ")
    v = d["val"].astype(np.float32).reshape(N, 8, 16, S, R); e = np.concatenate([elo, np.zeros((N, 8, 1, R), bool), eup], 2)[:, :, None]
    if not ((v[:, :, :, LO] >= 0.75) & (v[:, :, :, LO] <= 1.5)).all(): bad.append("diagonals lie from 0.75 to 1.5")
    if not (np.abs(np.delete(v, LO, 3)) <= 0.125).all(): bad.append("other values are at most 0.125 in size")
    if not ((v == 0) | ~e).all(): bad.append("empty slots have the value 0")
    sh = np.stack([gentries(x) for x in d["ship"]]).astype(np.int64).reshape(N, 8, N - 1, H); sp = np.stack([gentries(x) for x in d["spot"]]).astype(np.int64)
    if not ((sh >= 0) & (sh < R)).all(): bad.append("ship names local rows")
    if not ((sp >= 0) & (sp < T)).all(): bad.append("spot holds places")
    for q in range(N):
        tab = np.concatenate([np.broadcast_to(i[q], (8, R))] + [sh[p][:, q - (q > p)] * N + p for p in range(N) if p != q], 1)
        k = np.take_along_axis(tab, np.clip(sp[q], 0, T - 1), 1).reshape(8, LO, R)
        if not ((k == lo[q]) | elo[q]).all(): bad.append("the row at a lower slot's place is its column"); break
    return bad
def reference(val, col, spot, ship):
    c = col.astype(np.int64).reshape(N, 8, S, R).transpose(1, 2, 3, 0).reshape(8, S, M)
    a = val.astype(np.float64).reshape(N, 8, 16, S, R).transpose(1, 2, 3, 4, 0).reshape(8, 16, S, M)
    y = np.empty((8, 16, S, M)); z = np.empty((8, 16, M))
    for g in range(8):
        k = np.maximum(c[g, :LO], 0)
        at = np.full((S, LO, M), UP * M, np.int64)
        for w in range(UP): at = np.where(c[g, LO + 1 + w][k][None] == c[g][:, None], w * M + k[None], at)
        x = a[g]; r = np.ones((16, M))
        for sweep in range(SW):
            u = np.concatenate([x[:, LO + 1:].reshape(16, UP * M), np.zeros((16, 1))], 1); d = np.array(a[g])
            for t in range(LO): d -= x[:, t][:, None] * u[:, at[:, t]]
            for t in range(LO): d[:, t] *= r[:, k[t]]
            r = r * (2 - x[:, LO] * r); x = d
        y[g] = x; z[g] = r
    y = y.reshape(8, 16, S, R, N).transpose(4, 0, 1, 2, 3).reshape(N, 128, S * R); z = z.reshape(8, 16, R, N).transpose(3, 0, 1, 2).reshape(N, 128, R)
    return {"y": y.astype(np.float32), "inv": z.astype(np.float32)}

@@ -1,0 +1,521 @@
+import numpy as np
+from concourse.bass import DstId, RemoteDMATransfer
+from concourse.mybir import AluOpType, ActivationFunctionType
+
+R, H, NB = 448, 48, 5
+UPW = 6 * R
+BLK = 7 * H
+TW = 7 * R + NB * BLK
+V0 = 3 * R
+NU, NP = 5, 3
+
+CFG = {
+    "modes": ["AAAAAADD", "DAAAAADD", "DAADAAAA"],
+    "order3": [2, 3, 4, 5, 0, 1, 6, 7],
+    "pieces": [3, 3],
+    "crep_act": (2, 3, 4, 5), "chunks": [[2], [3, 4], [5, 6], [7]], "ksplit": 17,
+    "ahead": 2, "r3at": 1, "rk2at": 2, "diag_pe": True, "low1": "pe",
+    "nope": (), "two": (),
+}
+
+SCRATCH = {
+    "CI": ("sbuf", [128, R], "int32"), "CT": ("sbuf", [128, R + NB * H], "float32"),
+    "shipI": ("sbuf", [128, 15], "int32"), "shipU": ("sbuf", [128, 16], "uint16"),
+    "spotI": ("sbuf", [128, 56], "int32"), "spotK": ("sbuf", [128, 56], "uint16"), "spotU": ("sbuf", [128, 56], "uint16"),
+    "CP": ("sbuf", [128, NB * H], "float32"),
+    "GK": ("sbuf", [128, 896], "float32"), "GT": ("sbuf", [128, 28, 32], "float32"), "OT": ("sbuf", [128, 14, 32], "float32"),
+    "Cn": ("sbuf", [128, 56, 8], "float32"), "Crep": ("sbuf", [128, 56, 8, 6], "float32"),
+    "EQ": ("sbuf", [128, 8 * 336], "bfloat16"), "OI": ("sbuf", [128, R], "int32"), "OFF": ("sbuf", [128, R], "uint16"),
+    "DD": ("sbuf", [128, 128], "float32"), "pI": ("sbuf", [128, 4], "int32"), "cI": ("sbuf", [128, 4], "int32"),
+    "mk": ("sbuf", [128, 4], "float32"), "LL": ("sbuf", [128, 512], "float32"), "negI": ("sbuf", [128, 128], "float32"),
+    "Ib": ("sbuf", [128, 128], "bfloat16"), "Wt": ("sbuf", [128, 768], "bfloat16"),
+    "s1": ("sbuf", [128, 56], "float32"), "s2": ("sbuf", [128, 56], "int32"), "s3": ("sbuf", [128, 56], "float32"),
+    "s4": ("sbuf", [128, 56], "float32"), "s5": ("sbuf", [128, 56], "float32"), "s6": ("sbuf", [128, 56], "float32"),
+    "s7": ("sbuf", [128, 56], "float32"), "s8": ("sbuf", [128, 56], "float32"),
+    "nAB": ("sbuf", [128, 112], "float32"), "Brep": ("sbuf", [128, 112], "float32"),
+    "VV": ("sbuf", [128, V0 + TW], "bfloat16"), "T1": ("sbuf", [128, TW], "float32"), "T2": ("sbuf", [128, TW], "float32"),
+    "PK0": ("sbuf", [128, NB * 6 * H], "bfloat16"), "PK1": ("sbuf", [128, NB * 6 * H], "float32"), "PK2": ("sbuf", [128, NB * 6 * H], "float32"),
+    "SI": ("sbuf", [128, NB, 6, 3], "int32"), "L6": ("sbuf", [128, 90], "uint16"), "LP": ("sbuf", [128, 96], "uint16"),
+    "RT1": ("sbuf", [128, R + NB * H], "float32"), "RT2": ("sbuf", [128, R + NB * H], "float32"),
+    "PR1": ("sbuf", [128, NB * H], "float32"), "PR2": ("sbuf", [128, NB * H], "float32"),
+    "RK1": ("sbuf", [128, 896], "float32"), "RK2": ("sbuf", [128, 896], "float32"),
+    "sq1": ("sbuf", [128, R], "float32"), "tw1": ("sbuf", [128, R], "float32"),
+    "sq2": ("sbuf", [128, R], "float32"), "tw2": ("sbuf", [128, R], "float32"), "R3": ("sbuf", [128, R], "float32"),
+    "XS1": ("sbuf", [128, 896], "float32"), "XS2": ("sbuf", [128, 896], "float32"),
+    "YY": ("sbuf", [128, 9 * R], "float32"),
+    "PS": ("psum", [128, 4096], "float32"),
+}
+for _i in range(NU):
+    SCRATCH["U%d" % _i] = ("sbuf", [128, 896], "float32")
+for _i in range(NP):
+    SCRATCH["P%d" % _i] = ("sbuf", [128, 896], "float32")
+
+LOADS = ["lc0", "lc1", "lship", "lspot", "lv0", "lv1", "lv2"]
+ARRIVALS = ["ac", "a0", "ar1", "a10", "a11", "a12", "ar2", "a20", "a21", "a22"]
+SEMAPHORES = ["vector", "scalar", "tensor", "pool", "sent", "stored"] + LOADS + ARRIVALS
+
+ALU = AluOpType
+ACT = ActivationFunctionType
+ALL = slice(None)
+
+
+def _mask(name, idx):
+    m = np.zeros(SCRATCH[name][1][1:], bool)
+    m[idx] = True
+    return int.from_bytes(np.packbits(m.ravel(), bitorder="little").tobytes(), "little")
+
+
+def _banks(m):
+    full = (1 << 512) - 1
+    return sum(1 << b for b in range(8) if (m >> (512 * b)) & full)
+
+
+def engine_sets(topo, src, peers):
+    eng = topo.engines(src, peers[0])
+    half = len(eng) // 2
+    quarters = [eng[0:half:2], eng[1:half:2], eng[half::2], eng[half + 1::2]]
+    near = [p for p in peers if topo.die(p) == topo.die(src)]
+    far = [p for p in peers if topo.die(p) != topo.die(src)]
+    last = ([p for p in near if p > src] + near + far)[0]
+    near, far = [p for p in near if p != last], [p for p in far if p != last]
+    order = []
+    while near or far:
+        if far:
+            order.append(far.pop())
+        if near:
+            order.append(near.pop())
+    first = [(p, sum(1 << e for e in q), len(q)) for p, q in zip(order, quarters)]
+    return first, (last, sum(1 << e for e in eng), len(eng))
+
+
+def rank_program(g, core, T, topo):
+    rank = T.rank_of(core)
+    if rank is None:
+        return
+    cores = list(T.cores)
+    peers = [c for c in cores if c != core]
+    ops = []
+
+    def A(name, *idx):
+        ix = tuple(idx) if idx else (ALL,)
+        return (T[name][(ALL,) + ix], name, _mask(name, ix))
+
+    def C(name, a, b, step=None):
+        return A(name, slice(a, b, step))
+
+    def IND(win, off):
+        return (win[0].indirect(off[0]), [win, off])
+
+    def op(q, fn, reads, writes, sem=None, count=None):
+        rd = []
+        for r in reads:
+            rd += r[1] if len(r) == 2 else [r]
+        ops.append({"q": q, "fn": fn, "r": [(x[1], x[2]) for x in rd], "w": [(x[1], x[2]) for x in writes], "sem": sem, "n": count})
+
+    def vcopy(o, i, extra=()):
+        op("vector", lambda: g.vector.tensor_copy(o[0], i[0]), [i] + list(extra), [o])
+
+    def vtt(o, a, b, f):
+        op("vector", lambda: g.vector.tensor_tensor(o[0], a[0], b[0], f), [a, b], [o])
+
+    def vts(o, a, s1, s2, f0, f1=None, extra=()):
+        if f1 is None:
+            op("vector", lambda: g.vector.tensor_scalar(o[0], a[0], s1, None, f0), [a] + list(extra), [o])
+        else:
+            op("vector", lambda: g.vector.tensor_scalar(o[0], a[0], s1, s2, f0, f1), [a] + list(extra), [o])
+
+    def vset(o, c):
+        op("vector", lambda: g.vector.memset(o[0], c), [], [o])
+
+    def vtr(o, i):
+        op("vector", lambda: g.vector.transpose(o[0], i[0]), [i], [o])
+
+    def act(o, i, f=ACT.Copy, bias=None, scale=None):
+        kw = {}
+        if bias is not None:
+            kw["bias"] = bias
+        if scale is not None:
+            kw["scale"] = scale
+        op("scalar", lambda: g.scalar.activation(o[0], i[0], f, **kw), [i], [o])
+
+    def copy_on(q, o, i):
+        if q == "vector":
+            vcopy(o, i)
+        else:
+            act(o, i)
+
+    def mm(o, l, r, start, stop):
+        op("tensor", lambda: g.tensor.matmul(o[0], l[0], r[0], start, stop), [l, r], [o])
+
+    def load(q, sem, o, src):
+        eng = g.sync if q == "sync" else g.scalar
+        op(q, lambda: eng.dma_start(o[0], src), [], [o], sem=sem, count=16)
+
+    nstore = [0]
+
+    def store(q, dst, i):
+        eng = g.sync if q == "sync" else g.scalar
+        nstore[0] += 16
+        op(q, lambda: eng.dma_start(dst, i[0]), [i], [], sem="stored", count=16)
+
+    plans = {c: engine_sets(topo, c, [p for p in cores if p != c]) for c in cores}
+    inbound = 0
+    for c in peers:
+        for p, m, n in plans[c][0] + [plans[c][1]]:
+            if p == core:
+                inbound += n
+    nsent = [0]
+
+    def exchange(sem, src_of, dst_of):
+        def slot(p):
+            q = T.rank_of(p)
+            return (q if q < rank else q - 1), (rank if rank < q else rank - 1)
+        first, last = plans[core]
+        trs, rd = [], []
+        for p, m, n in first:
+            b, bb = slot(p)
+            rid, pid, _ = topo.addr(p)
+            trs.append(RemoteDMATransfer(dst_ids=[DstId(rid=rid, pnc=pid)], dma_engine_mask=m, remote_sem=T.sem[sem],
+                                         src=src_of(b)[0], dst=dst_of(bb)[0]))
+            rd.append(src_of(b))
+            nsent[0] += n
+        op("pool", lambda: g.remote_dma_fused(trs, local_sem=T.sem["sent"]), rd, [], sem="remote")
+        p, m, n = last
+        b, bb = slot(p)
+        rid, pid, _ = topo.addr(p)
+        s, d = src_of(b), dst_of(bb)
+        nsent[0] += n
+        op("pool", lambda: g.remote_dma(d[0], s[0], T.sem[sem], T.sem["sent"], pid, rid, m), [s], [], sem="remote")
+        op("arrive", None, [], [dst_of(k) for k in range(NB)], sem=sem, count=inbound)
+
+    def blk(tab, base, b, w0, w1):
+        z = base + 7 * R + b * BLK
+        return C(tab, z + H * w0, z + H * w1)
+
+    def bank(b, a=0, n=R):
+        return C("PS", 512 * b + a, 512 * b + a + n)
+
+    XP = [64, 1088]
+
+    def xp(k, t=None):
+        return C("PS", XP[k], XP[k] + 896) if t is None else C("PS", XP[k] + R * t, XP[k] + R * (t + 1))
+
+    ship = C("shipU", 0, 15)
+
+    ev = (T.CI[0::2, :], "CI", _mask("CI", (ALL,)))
+    od = (T.CI[1::2, :], "CIodd", 1)
+    load("sync", "lship", A("shipI"), T.ship[:])
+    load("scalar", "lc1", od, T.col[:, 0:8 * R])
+    load("sync", "lc0", ev, T.col[:, R:9 * R])
+    load("scalar", "lspot", A("spotI"), T.spot[:])
+    load("sync", "lv0", C("VV", V0, V0 + 3 * R), T.val[:, V0:V0 + 3 * R])
+    load("sync", "lv1", C("VV", V0 + 3 * R, 9 * R), T.val[:, V0 + 3 * R:9 * R])
+    load("sync", "lv2", C("VV", 0, V0), T.val[:, 0:V0])
+
+    op("pool", lambda: g.iota(T.pI[:, 0:1], [[0, 1]], 0, 1), [], [C("pI", 0, 1)])
+    op("pool", lambda: g.iota(T.DD[:], [[1, 128]], 0, -1, allow_small_or_imprecise_dtypes=True), [], [A("DD")])
+    vset(C("VV", 9 * R, 10 * R), 0.0)
+    for b in range(NB):
+        vset(blk("VV", V0, b, 6, 7), 0.0)
+    vts(C("cI", 0, 1), C("pI", 0, 1), 4, 1, ALU.arith_shift_right, ALU.bitwise_and)
+    vts(A("negI"), A("DD"), 0.0, -1.0, ALU.is_equal, ALU.mult)
+    vts(C("mk", 0, 1), C("cI", 0, 1), 0.0, None, ALU.is_equal)
+    vts(C("mk", 1, 2), C("cI", 0, 1), 1.0, None, ALU.is_equal)
+    vts(A("Ib"), A("DD"), 0.0, None, ALU.is_equal)
+
+    def LL(t, gj):
+        return C("LL", (2 * t + gj) * 128, (2 * t + gj + 1) * 128)
+    for t in range(2):
+        for gj in range(2):
+            m = C("mk", t, t + 1)
+            vts(LL(t, gj), A("DD"), float(16 * (gj - t)), m[0], ALU.is_equal, ALU.mult, extra=[m])
+    for w in range(6):
+        act(C("Wt", 128 * w, 128 * (w + 1)), A("negI"), scale=float(6 - w))
+
+    vcopy(ship, A("shipI"))
+    vcopy(A("CP"), IND(A("CI"), ship), extra=[od])
+    exchange("ac", lambda b: C("CP", H * b, H * (b + 1)), lambda b: C("CT", R + H * b, R + H * (b + 1)))
+
+    for w in range(6):
+        vts(A("SI", ALL, w), A("shipI"), float(R * w), None, ALU.add)
+    vcopy(A("L6"), A("SI"))
+    act(A("PK0"), IND(C("VV", V0, V0 + UPW), A("L6")))
+    exchange("a0", lambda b: C("PK0", 6 * H * b, 6 * H * (b + 1)), lambda b: blk("VV", V0, b, 0, 6))
+    vcopy(C("CT", 0, R), A("CI"), extra=[od])
+    for t in range(2):
+        vcopy(C("spotK", t, 56, 2), C("spotI", 28 * t, 28 * (t + 1)))
+    vtr(A("OT"), C("CT", 0, R))
+    for ci in range(2):
+        for gj in range(2):
+            mm(bank(4, 112 * ci, 112), LL(ci, gj), A("OT", ALL, slice(16 * gj, 16 * gj + 16, 2)), gj == 0, gj == 1)
+    for ci in range(2):
+        for gj in range(2):
+            mm(bank(5, 14 * ci, 14), LL(ci, gj), A("OT", ALL, 16 * gj + 1), gj == 0, gj == 1)
+    sp = A("spotI")
+    vts(A("s1"), sp, -471.5, 1.0 / H, ALU.add, ALU.mult)
+    vts(A("s4"), sp, 6 * R + 6 * H + 0.25, None, ALU.add)
+    vcopy(A("s2"), A("s1"))
+    vts(A("s6"), sp, float(R), 1.0 / H - 1.0 / R, ALU.is_lt, ALU.mult)
+    vts(A("s8"), sp, float(R), float(R - H), ALU.is_lt, ALU.mult)
+    vts(A("s3"), A("s2"), -1.0, float(BLK - H), ALU.max, ALU.mult)
+    vts(A("s7"), A("s6"), -1.0 / H, None, ALU.add)
+    for ci in range(2):
+        vcopy(A("Cn", slice(ci, 28, 2)), bank(4, 112 * ci, 112))
+    for ci in range(2):
+        vcopy(A("Cn", slice(28 + ci, 56, 2), 0), bank(5, 14 * ci, 14))
+    vcopy(A("Cn", slice(28, 56), slice(1, 8)), A("Cn", slice(0, 28), slice(1, 8)))
+    vtt(A("s5"), A("s3"), A("s4"), ALU.add)
+    for w in range(6):
+        copy_on("scalar" if w in CFG["crep_act"] else "vector", A("Crep", ALL, slice(2, 8), w), A("Cn", ALL, slice(2, 8)))
+    for k in range(2):
+        vts(C("Brep", 56 * k, 56 * k + 56), A("s8"), float(H), None, ALU.add)
+    for k in range(2):
+        vtt(C("nAB", 56 * k, 56 * k + 56), A("s5"), A("s7"), ALU.mult)
+    for t in range(2):
+        mm(xp(0, t), A("Ib"), C("VV", R * t, R * (t + 1)), True, True)
+
+    ks = CFG["ksplit"]
+    act(C("GK", 0, 32 * ks), IND(A("CT"), C("spotK", 0, 2 * ks)))
+    vcopy(C("GK", 32 * ks, 2 * R), IND(A("CT"), C("spotK", 2 * ks, 56)))
+    for c0, c1 in ((ks, 28), (0, ks)):
+        vtr(A("GT", slice(c0, c1)), C("GK", 32 * c0, 32 * c1))
+        for t in range(2):
+            for gj in range(2):
+                mm(bank(2, 168 * t + 6 * c0, 6 * (c1 - c0)), LL(t, gj),
+                   A("GT", slice(c0, c1), slice(16 * gj + 4, 16 * gj + 16, 2)), gj == 0, gj == 1)
+    vcopy(A("spotU"), sp)
+    pieces, w0, l0 = {}, 0, 0
+    for i, nw in enumerate(CFG["pieces"]):
+        pieces[w0 + nw - 1] = (i, w0, nw, l0)
+        vts(C("LP", l0, l0 + 15 * nw), A("SI", ALL, slice(w0, w0 + nw)), float(-R * w0), None, ALU.add)
+        w0, l0 = w0 + nw, l0 + 15 * nw + nw % 2
+    r1 = C("RT1", 0, R)
+    act(r1, C("VV", 2 * R, 3 * R), ACT.Identity, bias=2.0, scale=-1.0)
+    act(A("PR1"), IND(r1, ship))
+    exchange("ar1", lambda b: C("PR1", H * b, H * (b + 1)), lambda b: C("RT1", R + H * b, R + H * (b + 1)))
+    act(A("sq1"), r1, ACT.Square)
+    act(A("tw1"), r1, scale=2.0)
+    for w in range(6):
+        act(A("Crep", ALL, slice(0, 2), w), A("Cn", ALL, slice(0, 2)))
+    for tab in ("T1", "T2"):
+        for z, n in [(C(tab, UPW, UPW + R), R)] + [(blk(tab, 0, b, 6, 7), H) for b in range(NB)]:
+            op("pool", lambda z=z, n=n: g.iota(z[0], [[0, n]], 0, 0, allow_small_or_imprecise_dtypes=True), [], [z])
+
+    def join(chunks, banks):
+        todo = []
+        for ch, wb in zip(chunks, banks):
+            s, n = ch[0], len(ch)
+            for x in ch:
+                vtt(C("EQ", 336 * x, 336 * (x + 1)), bank(2, 0, 336), A("Crep", ALL, x), ALU.is_equal)
+                if todo:
+                    todo.pop(0)()
+            o = bank(wb, 0, 56 * n)
+            mm(o, A("negI"), C("nAB", 0, 56 * n), True, False)
+            for w in range(6):
+                mm(o, C("Wt", 128 * w, 128 * (w + 1)), C("EQ", 336 * s + w, 336 * (s + n), 6), False, w == 5)
+            oi = C("OI", 56 * s, 56 * (s + n))
+            todo.append(lambda oi=oi, o=o, n=n: vtt(oi, o, C("Brep", 0, 56 * n), ALU.mult))
+            todo.append(lambda oi=oi, s=s, n=n: vcopy(C("OFF", 56 * s, 56 * (s + n)), oi))
+        while todo:
+            todo.pop(0)()
+
+    join(CFG["chunks"], [3, 4, 5, 6, 7])
+
+    cu, cp, cb = [0], [0], [3]
+    held = []
+
+    def sweep(k):
+        order = [2, 3, 4, 5, 6, 7, 0, 1] if k < 2 else CFG["order3"]
+        modes = dict(zip(order, CFG["modes"][k]))
+        win = [C("VV", V0, V0 + TW), A("T1"), A("T2")][k]
+        xs = ["VV", "XS1", "XS2"][k]
+        xk = [0, 1, 0][k]
+        out_tab, pk = [("T1", "PK1"), ("T2", "PK2"), (None, None)][k]
+        ub, pb, ab = {}, {}, {}
+
+        def off(s, t=None):
+            return C("OFF", 56 * s, 56 * s + 56) if t is None else C("OFF", 56 * s + 28 * t, 56 * s + 28 * t + 28)
+
+        def mul(s, t=None):
+            if s not in pb:
+                pb[s] = "P%d" % (cp[0] % NP)
+                cp[0] += 1
+            a, b = (0, 2 * R) if t is None else (R * t, R * (t + 1))
+            if modes[s] == "A":
+                vtt(C(pb[s], a, b), C(ub[s], a, b), xp(xk, t), ALU.mult)
+            else:
+                vtt(C(pb[s], a, b), IND(win, off(s, t)), C(xs, a, b), ALU.mult)
+
+        def newbank():
+            cb[0] = (cb[0] + 1) % 4
+            return 4 + cb[0]
+
+        def pe(s):
+            if s == 0:
+                ab[s] = [bank(newbank()), bank(newbank())]
+                for t in range(2):
+                    mm(ab[s][t], A("Ib"), C("VV", R * t, R * (t + 1)), True, k == 0)
+                for t in range(2):
+                    if k:
+                        mm(ab[s][t], A("negI"), C(pb[s], R * (1 - t), R * (2 - t)), False, True)
+                return
+            ab[s] = 2 * k if (s == 1 and k < 2) else newbank()
+            terms = 2 if (s == 1 and k < 2 and CFG["diag_pe"]) or (k, s) in CFG["two"] else (0 if (k, s) in CFG["nope"] else 1)
+            mm(bank(ab[s]), A("Ib"), C("VV", R * (s + 1), R * (s + 2)), True, terms == 0)
+            for t in range(terms):
+                mm(bank(ab[s]), A("negI"), C(pb[s], R * t, R * (t + 1)), False, t == terms - 1)
+
+        def finish(s, halves=False):
+            if s == 0:
+                for t in range(2):
+                    if k == 0:
+                        vtt(C("XS1", R * t, R * (t + 1)), ab[s][t], C(pb[s], R * (1 - t), R * (2 - t)), ALU.subtract)
+                    elif k == 1:
+                        vtt(C("XS2", R * t, R * (t + 1)), ab[s][t], C("RK1", R * t, R * (t + 1)), ALU.mult)
+                    else:
+                        o = C("YY", R * t, R * (t + 1))
+                        vtt(o, ab[s][t], C("RK2", R * t, R * (t + 1)), ALU.mult)
+                        store("sync", T.y[:, R * t:R * (t + 1)], o)
+                return
+            if (k, s) in CFG["two"]:
+                o = C(out_tab, R * (s - 2), R * (s - 1)) if k < 2 else C("YY", R * (s + 1), R * (s + 2))
+                gathers_upto(min(order.index(s) + 2, 5 if k < 2 else 7))
+                act(o, bank(ab[s]))
+                if k == 2:
+                    store("sync", T.y[:, R * (s + 1):R * (s + 2)], o)
+                return
+            if (k, s) in CFG["nope"]:
+                vtt(bank(ab[s]), bank(ab[s]), C(pb[s], 0, R), ALU.subtract)
+            if k < 2:
+                vtt(C(out_tab, R * (s - 2), R * (s - 1)), bank(ab[s]), C(pb[s], R, 2 * R), ALU.subtract)
+                return
+            parts = [(0, R // 2, "scalar"), (R // 2, R // 2, "sync")] if halves else [(0, R, "sync")]
+            for a, n, q in parts:
+                y0 = R * (s + 1) + a
+                o = C("YY", y0, y0 + n)
+                vtt(o, bank(ab[s], a, n), C(pb[s], R + a, R + a + n), ALU.subtract)
+                store(q, T.y[:, y0:y0 + n], o)
+
+        alist = [s for s in order if modes[s] == "A"]
+
+        def gathers_upto(i):
+            while alist and order.index(alist[0]) <= i:
+                s = alist.pop(0)
+                ub[s] = "U%d" % (cu[0] % NU)
+                cu[0] += 1
+                act(A(ub[s]), IND(win, off(s)))
+
+        def send(w):
+            if w in pieces:
+                i, w0, nw, l0 = pieces[w]
+                n, z = H * nw, NB * H * w0
+                act(C(pk, z, z + NB * n), IND(C(out_tab, R * w0, R * (w0 + nw)), C("LP", l0, l0 + 15 * nw)))
+                exchange("a%d%d" % (k + 1, i), lambda b: C(pk, z + n * b, z + n * (b + 1)), lambda b: blk(out_tab, 0, b, w0, w0 + nw))
+
+        nmain = 6 if k < 2 else 8
+        for i, s in enumerate(order[:nmain]):
+            gathers_upto(min(i + 1, nmain - 1))
+            if k == 2 and i == CFG["r3at"]:
+                held.pop(0)()
+            if k == 2 and i == CFG["rk2at"]:
+                act(A("RK2"), IND(A("RT2"), A("spotU")))
+            prev = order[i - 1] if i else None
+            if i == nmain - 1:
+                mul(s, 0); pe(s); finish(prev); mul(s, 1)
+                if k < 2:
+                    send(prev - 2)
+                finish(s, halves=True)
+                if k < 2:
+                    send(5)
+            else:
+                mul(s); pe(s)
+                if prev is not None:
+                    finish(prev)
+                    if k < 2:
+                        gathers_upto(min(i + CFG["ahead"], 5))
+                        send(prev - 2)
+        if k == 2:
+            return
+        if k == 0:
+            act(A("RK1"), IND(A("RT1"), A("spotU")))
+            join([[0], [1]], [newbank(), newbank()])
+        else:
+            held.pop(0)()
+            act(A("PR2"), IND(C("RT2", 0, R), ship))
+            exchange("ar2", lambda b: C("PR2", H * b, H * (b + 1)), lambda b: C("RT2", R + H * b, R + H * (b + 1)))
+        gathers_upto(7)
+        sq, tw, rr = [("sq1", "tw1", "RT1"), ("sq2", "tw2", "RT2")][k]
+        if k == 0 and CFG["low1"] == "pe":
+            for t in range(2):
+                mul(0, 1 - t)
+                mm(xp(1, t), A("Ib"), C("VV", R * t, R * (t + 1)), True, False)
+                mm(xp(1, t), A("negI"), C(pb[0], R * (1 - t), R * (2 - t)), False, True)
+                act(C("XS1", R * t, R * (t + 1)), xp(1, t))
+            mul(1); pe(1)
+        elif k == 0:
+            mul(0, 1); mul(0, 0); pe(0); finish(0)
+            act(xp(1), A("XS1"))
+            mul(1); pe(1)
+        else:
+            mul(0, 1); mul(0, 0); pe(0); mul(1); pe(1); finish(0)
+            act(A(sq), C(rr, 0, R), ACT.Square)
+            act(A(tw), C(rr, 0, R), scale=2.0)
+            act(xp(0), A("XS2"))
+        d = bank(ab[1])
+        rn = C("RT2", 0, R) if k == 0 else A("R3")
+
+        def rstep():
+            if not CFG["diag_pe"]:
+                vtt(d, d, C(pb[1], R, 2 * R), ALU.subtract)
+            vtt(d, d, A(sq), ALU.mult)
+            vtt(rn, A(tw), d, ALU.subtract)
+            if k == 1:
+                store("sync", T.inv[:], rn)
+        held.append(rstep)
+
+    for k in range(3):
+        sweep(k)
+
+    for o in ops:
+        o["acc"] = [(n, m, True, _banks(m) if n == "PS" else 0) for n, m in o["w"]] + [(n, m, False, _banks(m) if n == "PS" else 0) for n, m in o["r"]]
+    deps = []
+    for j, o in enumerate(ops):
+        d = []
+        for i in range(j):
+            e = ops[i]
+            if (e["q"] == "tensor" and o["q"] == "tensor") or o["q"] == "arrive" or e["sem"] in ("remote", "stored"):
+                continue
+            for n1, m1, w1, b1 in e["acc"]:
+                if any(n1 == n2 and ((b1 & b2 and e["q"] != o["q"]) or ((w1 or w2) and m1 & m2)) for n2, m2, w2, b2 in o["acc"]):
+                    d.append(i)
+                    break
+        deps.append(d)
+    needed = set()
+    for j, o in enumerate(ops):
+        o["latest"] = {ops[i]["q"]: i for i in deps[j] if ops[i]["sem"] is None}
+        needed.update(o["latest"].values())
+    cnt = {"vector": 0, "scalar": 0, "tensor": 0, "pool": 0}
+    for j, o in enumerate(ops):
+        if o["sem"] is not None:
+            o["tok"] = (o["sem"], o["n"])
+        elif j in needed:
+            cnt[o["q"]] += 1
+            o["tok"] = (o["q"], cnt[o["q"]])
+    queue = {"vector": g.vector, "scalar": g.scalar, "tensor": g.tensor, "pool": g, "sync": g.sync}
+    seen = {q: {} for q in queue}
+    for j, o in enumerate(ops):
+        if o["q"] == "arrive":
+            continue
+        want = [ops[i]["tok"] for i in o["latest"].values()] + [ops[i]["tok"] for i in deps[j] if ops[i]["sem"] is not None]
+        for s, n in want:
+            if seen[o["q"]].get(s, 0) < n:
+                queue[o["q"]].wait_ge(T.sem[s], n)
+                seen[o["q"]][s] = n
+        ins = o["fn"]()
+        if o["sem"] is None:
+            if j in needed:
+                ins.then_inc(T.sem[o["q"]], 1)
+        elif o["sem"] != "remote":
+            ins.then_inc(T.sem[o["sem"]], 16)
+    g.wait_ge(T.sem["sent"], nsent[0])
+    g.sync.wait_ge(T.sem["stored"], nstore[0])

@@ -4,43 +4,53 @@ from concourse.mybir import AluOpType, ActivationFunctionType
 
 R, H, NB = 448, 48, 5
 UPW = 6 * R
-BLK = 7 * H
+BLK = 8 * H
 TW = 7 * R + NB * BLK
 V0 = 3 * R
-NU, NP = 5, 3
+MID = -1344.0
+NU, NP = 8, 8
 
 CFG = {
-    "modes": ["AAAAAADD", "DAAAAADD", "DAADAAAA"],
+    "modes": [["AAS", "AAS", "ADS", "ADS", "ADS", "ADV"],
+              ["ADS", "ADV", "ADS", "ADS", "ADS", "ADV"],
+              ["ADS", "AAS", "ADS", "AAV", "AD", "ADS", "ADS", "ADV"]],
     "order3": [2, 3, 4, 5, 0, 1, 6, 7],
+    "diag": ["AD", "AD"],
     "pieces": [3, 3],
-    "crep_act": (2, 3, 4, 5), "chunks": [[2], [3, 4], [5, 6], [7]], "ksplit": 17,
-    "ahead": 2, "r3at": 1, "rk2at": 2, "diag_pe": True, "low1": "pe",
-    "nope": (), "two": (),
+    "chunks": [[2], [3], [4, 5], [6, 7]], "ksplit": 10,
+    "ahead": [2, 2, 2], "lag": [1, 1, 1], "joinat": 9, "chunks2": [[0, 1]], "pr2at": 1, "r2at": -1, "r3at": -1, "rk2at": -1,
+    "first": 2.3, "rows": 0.75, "perword": 0.006, "cut": [[0, 0, 0], [0, 0, 0]], "store": 0.5,
+    "banks": [[4, 5, 6, 7, 3], [4, 5, 6, 7, 0], [4, 5, 6, 7, 2, 3]], "rsq": [0, 2],
+    "cases": [(1.5, 1.0), (1.15, 1.2), (1.95, 0.8)], "seed": 1, "rounds": 2500, "nudge": 6, "give": 0.08,
 }
+FIXED = {"vector": 0.05, "scalar": 0.09, "tensor": 0.03, "pool": 0.13}
+CYCLE = {"vector": 0.00083, "scalar": 0.00083, "tensor": 0.000417, "pool": 0.00083}
+WAKE = 0.08
 
 SCRATCH = {
     "CI": ("sbuf", [128, R], "int32"), "CT": ("sbuf", [128, R + NB * H], "float32"),
     "shipI": ("sbuf", [128, 15], "int32"), "shipU": ("sbuf", [128, 16], "uint16"),
     "spotI": ("sbuf", [128, 56], "int32"), "spotK": ("sbuf", [128, 56], "uint16"), "spotU": ("sbuf", [128, 56], "uint16"),
+    "spotD": ("sbuf", [128, 56], "uint16"),
     "CP": ("sbuf", [128, NB * H], "float32"),
     "GK": ("sbuf", [128, 896], "float32"), "GT": ("sbuf", [128, 28, 32], "float32"), "OT": ("sbuf", [128, 14, 32], "float32"),
-    "Cn": ("sbuf", [128, 56, 8], "float32"), "Crep": ("sbuf", [128, 56, 8, 6], "float32"),
+    "GKh": ("sbuf", [128, 896], "float16"), "GTh": ("sbuf", [128, 28, 32], "float16"), "LLh": ("sbuf", [128, 512], "float16"),
+    "Cn": ("sbuf", [128, 56, 8], "float16"), "Crep": ("sbuf", [128, 56, 8, 6], "float16"),
     "EQ": ("sbuf", [128, 8 * 336], "bfloat16"), "OI": ("sbuf", [128, R], "int32"), "OFF": ("sbuf", [128, R], "uint16"),
     "DD": ("sbuf", [128, 128], "float32"), "pI": ("sbuf", [128, 4], "int32"), "cI": ("sbuf", [128, 4], "int32"),
-    "mk": ("sbuf", [128, 4], "float32"), "LL": ("sbuf", [128, 512], "float32"), "negI": ("sbuf", [128, 128], "float32"),
-    "Ib": ("sbuf", [128, 128], "bfloat16"), "Wt": ("sbuf", [128, 768], "bfloat16"),
+    "mk": ("sbuf", [128, 4], "float32"), "LL": ("sbuf", [128, 512], "float32"),
+    "n2I": ("sbuf", [128, 128], "float32"), "SQ": ("sbuf", [128, R], "float32"),
+    "negI": ("sbuf", [128, 128], "float32"), "posI": ("sbuf", [128, 128], "float32"),
+    "Ib": ("sbuf", [128, 128], "bfloat16"), "nIb": ("sbuf", [128, 128], "bfloat16"), "Wt": ("sbuf", [128, 768], "bfloat16"),
     "s1": ("sbuf", [128, 56], "float32"), "s2": ("sbuf", [128, 56], "int32"), "s3": ("sbuf", [128, 56], "float32"),
     "s4": ("sbuf", [128, 56], "float32"), "s5": ("sbuf", [128, 56], "float32"), "s6": ("sbuf", [128, 56], "float32"),
-    "s7": ("sbuf", [128, 56], "float32"), "s8": ("sbuf", [128, 56], "float32"),
+    "s7": ("sbuf", [128, 56], "float32"), "s8": ("sbuf", [128, 56], "float32"), "s9": ("sbuf", [128, 56], "float32"),
     "nAB": ("sbuf", [128, 112], "float32"), "Brep": ("sbuf", [128, 112], "float32"),
     "VV": ("sbuf", [128, V0 + TW], "bfloat16"), "T1": ("sbuf", [128, TW], "float32"), "T2": ("sbuf", [128, TW], "float32"),
-    "PK0": ("sbuf", [128, NB * 6 * H], "bfloat16"), "PK1": ("sbuf", [128, NB * 6 * H], "float32"), "PK2": ("sbuf", [128, NB * 6 * H], "float32"),
-    "SI": ("sbuf", [128, NB, 6, 3], "int32"), "L6": ("sbuf", [128, 90], "uint16"), "LP": ("sbuf", [128, 96], "uint16"),
-    "RT1": ("sbuf", [128, R + NB * H], "float32"), "RT2": ("sbuf", [128, R + NB * H], "float32"),
-    "PR1": ("sbuf", [128, NB * H], "float32"), "PR2": ("sbuf", [128, NB * H], "float32"),
-    "RK1": ("sbuf", [128, 896], "float32"), "RK2": ("sbuf", [128, 896], "float32"),
-    "sq1": ("sbuf", [128, R], "float32"), "tw1": ("sbuf", [128, R], "float32"),
-    "sq2": ("sbuf", [128, R], "float32"), "tw2": ("sbuf", [128, R], "float32"), "R3": ("sbuf", [128, R], "float32"),
+    "PK0": ("sbuf", [128, NB * 7 * H], "bfloat16"), "PK1": ("sbuf", [128, NB * 6 * H], "float32"), "PK2": ("sbuf", [128, NB * 6 * H], "float32"),
+    "SI": ("sbuf", [128, NB, 7, 3], "int32"), "L7": ("sbuf", [128, 106], "uint16"), "LP": ("sbuf", [128, 96], "uint16"),
+    "R1": ("sbuf", [128, R], "float32"), "RT2": ("sbuf", [128, R + NB * H], "float32"), "PR2": ("sbuf", [128, NB * H], "float32"),
+    "RK1": ("sbuf", [128, 896], "float32"), "RK2": ("sbuf", [128, 896], "float32"), "R3": ("sbuf", [128, R], "float32"),
     "XS1": ("sbuf", [128, 896], "float32"), "XS2": ("sbuf", [128, 896], "float32"),
     "YY": ("sbuf", [128, 9 * R], "float32"),
     "PS": ("psum", [128, 4096], "float32"),
@@ -51,7 +61,7 @@ for _i in range(NP):
     SCRATCH["P%d" % _i] = ("sbuf", [128, 896], "float32")
 
 LOADS = ["lc0", "lc1", "lship", "lspot", "lv0", "lv1", "lv2"]
-ARRIVALS = ["ac", "a0", "ar1", "a10", "a11", "a12", "ar2", "a20", "a21", "a22"]
+ARRIVALS = ["ac", "a0", "a10", "a11", "a12", "ar2", "a20", "a21", "a22"]
 SEMAPHORES = ["vector", "scalar", "tensor", "pool", "sent", "stored"] + LOADS + ARRIVALS
 
 ALU = AluOpType
@@ -88,6 +98,84 @@ def engine_sets(topo, src, peers):
     return first, (last, sum(1 << e for e in eng), len(eng))
 
 
+ORDER = []
+
+
+def issue_order(ops, deps, behind):
+    every = range(len(ops))
+    reach, before, after = [], [], [[] for _ in ops]
+    for j in every:
+        far = 0
+        for i in deps[j]:
+            far |= reach[i]
+        near = [i for i in deps[j] if not far >> i & 1]
+        reach.append(far | sum(1 << i for i in near))
+        before.append([(i, True) for i in near] + [(i, ops[j]["q"] == "arrive") for i in behind[j]])
+        for i, w in before[j]:
+            after[i].append((j, w))
+    cases = []
+    for rate, dma in CFG["cases"]:
+        cost = [(o["cost"] * dma if o["q"] == "arrive" else o["cost"]) + o["gathered"] * rate for o in ops]
+        cases.append((cost, [o["lag"] * dma + WAKE for o in ops]))
+    cost, lag = cases[0]
+
+    def lay(order, back):
+        end, taken = [0.0] * len(ops), {}
+        for j in order:
+            c = cost[j]
+            if back:
+                t = max([end[i] + (lag[j] if w else 0.0) for i, w in after[j]], default=lag[j])
+            else:
+                t = max([end[i] + (lag[i] if w else 0.0) for i, w in before[j]], default=0.0)
+            spans = taken.setdefault(ops[j]["q"], [])
+            k = len(spans)
+            while k and spans[k - 1][1] > t:
+                k -= 1
+            while k < len(spans) and t + c > spans[k][0] + 1e-9:
+                t = spans[k][1]
+                k += 1
+            spans.insert(k, (t, t + c))
+            end[j] = t + c
+        return end
+
+    def length(order):
+        total = 0.0
+        for cost, lag in cases:
+            end, free = [0.0] * len(ops), {}
+            for j in order:
+                q = ops[j]["q"]
+                t = max([end[i] + (lag[i] if w else 0.0) for i, w in before[j]], default=0.0)
+                end[j] = free[q] = max(t, free.get(q, 0.0)) + cost[j]
+            total += max(end[j] + lag[j] for j in every)
+        return total
+
+    def tighten(end):
+        late = lay(sorted(every, key=lambda j: (-end[j], -j)), True)
+        return lay(sorted(every, key=lambda j: (-late[j], j)), False)
+
+    def judge(end):
+        order = sorted(every, key=lambda j: (end[j] - cost[j], j))
+        return length(order), end, order
+
+    rng = np.random.default_rng(CFG["seed"])
+    best = cur = judge(tighten(lay(every, False)))
+    for it in range(CFG["rounds"]):
+        key = [cur[1][j] - cost[j] for j in every]
+        for j in rng.integers(0, len(ops), CFG["nudge"]):
+            key[j] += float(rng.normal())
+        for j in every:
+            for i, _ in before[j]:
+                if key[j] <= key[i]:
+                    key[j] = key[i] + 1e-6
+        end = lay(sorted(every, key=lambda j: (key[j], j)), False)
+        new = judge(tighten(end) if it % 3 == 0 else end)
+        if new[0] < cur[0] + CFG["give"]:
+            cur = new
+        if new[0] < best[0]:
+            best = new
+    return best[2]
+
+
 def rank_program(g, core, T, topo):
     rank = T.rank_of(core)
     if rank is None:
@@ -106,26 +194,33 @@ def rank_program(g, core, T, topo):
     def IND(win, off):
         return (win[0].indirect(off[0]), [win, off])
 
-    def op(q, fn, reads, writes, sem=None, count=None):
+    def op(q, fn, reads, writes, sem=None, count=None, rate=None, cost=None, lag=0.0):
         rd = []
         for r in reads:
             rd += r[1] if len(r) == 2 else [r]
-        ops.append({"q": q, "fn": fn, "r": [(x[1], x[2]) for x in rd], "w": [(x[1], x[2]) for x in writes], "sem": sem, "n": count})
+        gathered = 0.0
+        if cost is None:
+            n = writes[0][2].bit_count()
+            if any(len(r) == 2 for r in reads):
+                cost, gathered = 0.06, n * CYCLE[q]
+            else:
+                if rate is None:
+                    rate = 0.5 if q == "vector" and all(SCRATCH[x[1]][2].endswith("16") for x in rd[:1] + writes) else 1.0
+                cost = FIXED[q] + max(64, n * rate) * CYCLE[q]
+        ops.append({"q": q, "fn": fn, "r": [(x[1], x[2]) for x in rd], "w": [(x[1], x[2]) for x in writes], "sem": sem, "n": count,
+                    "cost": cost, "gathered": gathered, "lag": lag})
 
     def vcopy(o, i, extra=()):
         op("vector", lambda: g.vector.tensor_copy(o[0], i[0]), [i] + list(extra), [o])
 
     def vtt(o, a, b, f):
-        op("vector", lambda: g.vector.tensor_tensor(o[0], a[0], b[0], f), [a, b], [o])
+        op("vector", lambda: g.vector.tensor_tensor(o[0], a[0], b[0], f), [a, b], [o], rate=1.0 if "PS" in (a[1], b[1]) else 2.0)
 
     def vts(o, a, s1, s2, f0, f1=None, extra=()):
         if f1 is None:
             op("vector", lambda: g.vector.tensor_scalar(o[0], a[0], s1, None, f0), [a] + list(extra), [o])
         else:
             op("vector", lambda: g.vector.tensor_scalar(o[0], a[0], s1, s2, f0, f1), [a] + list(extra), [o])
-
-    def vset(o, c):
-        op("vector", lambda: g.vector.memset(o[0], c), [], [o])
 
     def vtr(o, i):
         op("vector", lambda: g.vector.transpose(o[0], i[0]), [i], [o])
@@ -138,25 +233,34 @@ def rank_program(g, core, T, topo):
             kw["scale"] = scale
         op("scalar", lambda: g.scalar.activation(o[0], i[0], f, **kw), [i], [o])
 
-    def copy_on(q, o, i):
-        if q == "vector":
-            vcopy(o, i)
-        else:
-            act(o, i)
+    def zero(z, n):
+        op("pool", lambda: g.iota(z[0], [[0, n]], 0, 0, allow_small_or_imprecise_dtypes=True), [], [z], rate=2.0)
 
-    def mm(o, l, r, start, stop):
-        op("tensor", lambda: g.tensor.matmul(o[0], l[0], r[0], start, stop), [l, r], [o])
+    groups = {b: [] for b in range(8)}
+    wide = set()
 
-    def load(q, sem, o, src):
+    def mm(o, l, r, start, full=False):
+        b = _banks(o[2]).bit_length() - 1
+        me = {"start": start, "stop": True}
+        if not start:
+            groups[b][-1]["stop"] = False
+        groups[b].append(me)
+        if start:
+            (wide.add if full else wide.discard)(b)
+        op("tensor", lambda: g.tensor.matmul(o[0], l[0], r[0], me["start"], me["stop"]), [l, r], [o])
+        ops[-1]["cost"] = FIXED["tensor"] + max(64, o[2].bit_count()) * CYCLE["tensor"] * (4 if SCRATCH[l[1]][2] == "float32" else 1)
+
+    def load(q, sem, o, src, lag):
         eng = g.sync if q == "sync" else g.scalar
-        op(q, lambda: eng.dma_start(o[0], src), [], [o], sem=sem, count=16)
+        op(q, lambda: eng.dma_start(o[0], src), [], [o], sem=sem, count=16, cost=0.06, lag=lag)
 
     nstore = [0]
 
     def store(q, dst, i):
         eng = g.sync if q == "sync" else g.scalar
         nstore[0] += 16
-        op(q, lambda: eng.dma_start(dst, i[0]), [i], [], sem="stored", count=16)
+        wire = CFG["store"] * i[2].bit_count() / R
+        op(q, lambda: eng.dma_start(dst, i[0]), [i], [], sem="stored", count=16, cost=wire if q == "sync" else 0.06, lag=1.6 if q == "sync" else 1.6 + wire)
 
     plans = {c: engine_sets(topo, c, [p for p in cores if p != c]) for c in cores}
     inbound = 0
@@ -179,323 +283,371 @@ def rank_program(g, core, T, topo):
                                          src=src_of(b)[0], dst=dst_of(bb)[0]))
             rd.append(src_of(b))
             nsent[0] += n
-        op("pool", lambda: g.remote_dma_fused(trs, local_sem=T.sem["sent"]), rd, [], sem="remote")
+        once = 0.0 if nsent[0] > 16 else CFG["first"]
+        wire = CFG["rows"] + rd[0][2].bit_count() * CFG["perword"] * (0.5 if SCRATCH[rd[0][1]][2] == "bfloat16" else 1.0)
+        op("pool", lambda: g.remote_dma_fused(trs, local_sem=T.sem["sent"]), rd, [], sem="remote", cost=0.35 + once, lag=0.5)
         p, m, n = last
         b, bb = slot(p)
         rid, pid, _ = topo.addr(p)
         s, d = src_of(b), dst_of(bb)
         nsent[0] += n
-        op("pool", lambda: g.remote_dma(d[0], s[0], T.sem[sem], T.sem["sent"], pid, rid, m), [s], [], sem="remote")
-        op("arrive", None, [], [dst_of(k) for k in range(NB)], sem=sem, count=inbound)
+        op("pool", lambda: g.remote_dma(d[0], s[0], T.sem[sem], T.sem["sent"], pid, rid, m), [s], [], sem="remote", cost=0.35, lag=0.1)
+        op("arrive", None, [], [dst_of(k) for k in range(NB)], sem=sem, count=inbound, cost=wire, lag=0.25)
 
     def blk(tab, base, b, w0, w1):
-        z = base + 7 * R + b * BLK
+        z = base + 7 * R + b * BLK + H
         return C(tab, z + H * w0, z + H * w1)
 
     def bank(b, a=0, n=R):
         return C("PS", 512 * b + a, 512 * b + a + n)
 
-    XP = [64, 1088]
-
-    def xp(k, t=None):
-        return C("PS", XP[k], XP[k] + 896) if t is None else C("PS", XP[k] + R * t, XP[k] + R * (t + 1))
+    def plane(s):
+        return C("VV", R * s, R * (s + 1))
 
     ship = C("shipU", 0, 15)
 
     ev = (T.CI[0::2, :], "CI", _mask("CI", (ALL,)))
     od = (T.CI[1::2, :], "CIodd", 1)
-    load("sync", "lship", A("shipI"), T.ship[:])
-    load("scalar", "lc1", od, T.col[:, 0:8 * R])
-    load("sync", "lc0", ev, T.col[:, R:9 * R])
-    load("scalar", "lspot", A("spotI"), T.spot[:])
-    load("sync", "lv0", C("VV", V0, V0 + 3 * R), T.val[:, V0:V0 + 3 * R])
-    load("sync", "lv1", C("VV", V0 + 3 * R, 9 * R), T.val[:, V0 + 3 * R:9 * R])
-    load("sync", "lv2", C("VV", 0, V0), T.val[:, 0:V0])
+    load("sync", "lship", A("shipI"), T.ship[:], 2.1)
+    load("scalar", "lc1", od, T.col[:, 0:8 * R], 2.0)
+    load("sync", "lc0", ev, T.col[:, R:9 * R], 2.8)
+    load("scalar", "lspot", A("spotI"), T.spot[:], 2.4)
+    load("sync", "lv0", C("VV", 2 * R, 6 * R), T.val[:, 2 * R:6 * R], 3.4)
+    load("sync", "lv1", C("VV", 6 * R, 9 * R), T.val[:, 6 * R:9 * R], 4.2)
+    load("sync", "lv2", C("VV", 0, 2 * R), T.val[:, 0:2 * R], 4.8)
 
-    op("pool", lambda: g.iota(T.pI[:, 0:1], [[0, 1]], 0, 1), [], [C("pI", 0, 1)])
-    op("pool", lambda: g.iota(T.DD[:], [[1, 128]], 0, -1, allow_small_or_imprecise_dtypes=True), [], [A("DD")])
-    vset(C("VV", 9 * R, 10 * R), 0.0)
+    op("pool", lambda: g.iota(T.pI[:, 0:1], [[0, 1]], 0, 1), [], [C("pI", 0, 1)], cost=0.13)
+    op("pool", lambda: g.iota(T.DD[:], [[1, 128]], 0, -1, allow_small_or_imprecise_dtypes=True), [], [A("DD")], rate=2.0)
+    zero(plane(9), R)
     for b in range(NB):
-        vset(blk("VV", V0, b, 6, 7), 0.0)
+        zero(blk("VV", V0, b, 6, 7), H)
     vts(C("cI", 0, 1), C("pI", 0, 1), 4, 1, ALU.arith_shift_right, ALU.bitwise_and)
     vts(A("negI"), A("DD"), 0.0, -1.0, ALU.is_equal, ALU.mult)
     vts(C("mk", 0, 1), C("cI", 0, 1), 0.0, None, ALU.is_equal)
     vts(C("mk", 1, 2), C("cI", 0, 1), 1.0, None, ALU.is_equal)
-    vts(A("Ib"), A("DD"), 0.0, None, ALU.is_equal)
 
-    def LL(t, gj):
-        return C("LL", (2 * t + gj) * 128, (2 * t + gj + 1) * 128)
+    def LL(t, gj, name="LL"):
+        return C(name, (2 * t + gj) * 128, (2 * t + gj + 1) * 128)
     for t in range(2):
         for gj in range(2):
             m = C("mk", t, t + 1)
             vts(LL(t, gj), A("DD"), float(16 * (gj - t)), m[0], ALU.is_equal, ALU.mult, extra=[m])
+    vcopy(A("LLh"), A("LL"))
+    act(A("Ib"), A("negI"), scale=-1.0)
+    act(A("nIb"), A("negI"))
+    act(A("posI"), A("negI"), scale=-1.0)
+    act(A("n2I"), A("negI"), scale=2.0)
     for w in range(6):
         act(C("Wt", 128 * w, 128 * (w + 1)), A("negI"), scale=float(6 - w))
 
     vcopy(ship, A("shipI"))
-    vcopy(A("CP"), IND(A("CI"), ship), extra=[od])
+    for w in range(7):
+        vts(A("SI", ALL, w), A("shipI"), float(R * w), None, ALU.add)
+    vts(A("CP"), IND(A("CI"), ship), MID, None, ALU.add, extra=[od])
     exchange("ac", lambda b: C("CP", H * b, H * (b + 1)), lambda b: C("CT", R + H * b, R + H * (b + 1)))
 
-    for w in range(6):
-        vts(A("SI", ALL, w), A("shipI"), float(R * w), None, ALU.add)
-    vcopy(A("L6"), A("SI"))
-    act(A("PK0"), IND(C("VV", V0, V0 + UPW), A("L6")))
-    exchange("a0", lambda b: C("PK0", 6 * H * b, 6 * H * (b + 1)), lambda b: blk("VV", V0, b, 0, 6))
-    vcopy(C("CT", 0, R), A("CI"), extra=[od])
+    vcopy(C("L7", 0, 105), A("SI"))
+    act(A("PK0"), IND(C("VV", 2 * R, 9 * R), C("L7", 0, 105)))
+    exchange("a0", lambda b: C("PK0", 7 * H * b, 7 * H * (b + 1)), lambda b: blk("VV", V0, b, -1, 6))
+    vts(C("CT", 0, R), A("CI"), MID, None, ALU.add, extra=[od])
     for t in range(2):
         vcopy(C("spotK", t, 56, 2), C("spotI", 28 * t, 28 * (t + 1)))
     vtr(A("OT"), C("CT", 0, R))
     for ci in range(2):
         for gj in range(2):
-            mm(bank(4, 112 * ci, 112), LL(ci, gj), A("OT", ALL, slice(16 * gj, 16 * gj + 16, 2)), gj == 0, gj == 1)
+            mm(bank(4, 112 * ci, 112), LL(ci, gj), A("OT", ALL, slice(16 * gj, 16 * gj + 16, 2)), gj == 0)
     for ci in range(2):
         for gj in range(2):
-            mm(bank(5, 14 * ci, 14), LL(ci, gj), A("OT", ALL, 16 * gj + 1), gj == 0, gj == 1)
+            mm(bank(5, 14 * ci, 14), LL(ci, gj), A("OT", ALL, 16 * gj + 1), gj == 0)
     sp = A("spotI")
     vts(A("s1"), sp, -471.5, 1.0 / H, ALU.add, ALU.mult)
-    vts(A("s4"), sp, 6 * R + 6 * H + 0.25, None, ALU.add)
+    vts(A("s4"), sp, 6 * R + BLK - H + 0.25, None, ALU.add)
     vcopy(A("s2"), A("s1"))
     vts(A("s6"), sp, float(R), 1.0 / H - 1.0 / R, ALU.is_lt, ALU.mult)
     vts(A("s8"), sp, float(R), float(R - H), ALU.is_lt, ALU.mult)
     vts(A("s3"), A("s2"), -1.0, float(BLK - H), ALU.max, ALU.mult)
-    vts(A("s7"), A("s6"), -1.0 / H, None, ALU.add)
+    act(A("s7"), A("s6"), ACT.Identity, bias=-1.0 / H)
+    vtt(A("s5"), A("s3"), A("s4"), ALU.add)
     for ci in range(2):
         vcopy(A("Cn", slice(ci, 28, 2)), bank(4, 112 * ci, 112))
     for ci in range(2):
         vcopy(A("Cn", slice(28 + ci, 56, 2), 0), bank(5, 14 * ci, 14))
     vcopy(A("Cn", slice(28, 56), slice(1, 8)), A("Cn", slice(0, 28), slice(1, 8)))
-    vtt(A("s5"), A("s3"), A("s4"), ALU.add)
     for w in range(6):
-        copy_on("scalar" if w in CFG["crep_act"] else "vector", A("Crep", ALL, slice(2, 8), w), A("Cn", ALL, slice(2, 8)))
+        vcopy(A("Crep", ALL, ALL, w), A("Cn"))
+    vtt(C("nAB", 0, 56), A("s5"), A("s7"), ALU.mult)
+    act(C("nAB", 56, 112), C("nAB", 0, 56))
     for k in range(2):
-        vts(C("Brep", 56 * k, 56 * k + 56), A("s8"), float(H), None, ALU.add)
-    for k in range(2):
-        vtt(C("nAB", 56 * k, 56 * k + 56), A("s5"), A("s7"), ALU.mult)
-    for t in range(2):
-        mm(xp(0, t), A("Ib"), C("VV", R * t, R * (t + 1)), True, True)
+        act(C("Brep", 56 * k, 56 * k + 56), A("s8"), ACT.Identity, bias=float(H))
+    mm(bank(0), A("nIb"), plane(0), True)
+    mm(bank(1), A("Ib"), plane(1), True)
 
     ks = CFG["ksplit"]
     act(C("GK", 0, 32 * ks), IND(A("CT"), C("spotK", 0, 2 * ks)))
-    vcopy(C("GK", 32 * ks, 2 * R), IND(A("CT"), C("spotK", 2 * ks, 56)))
-    for c0, c1 in ((ks, 28), (0, ks)):
-        vtr(A("GT", slice(c0, c1)), C("GK", 32 * c0, 32 * c1))
+    vcopy(C("GKh", 32 * ks, 2 * R), IND(A("CT"), C("spotK", 2 * ks, 56)))
+    for c0, c1, h in ((0, ks, ""), (ks, 28, "h")):
+        vtr(A("GT" + h, slice(c0, c1)), C("GK" + h, 32 * c0, 32 * c1))
         for t in range(2):
             for gj in range(2):
-                mm(bank(2, 168 * t + 6 * c0, 6 * (c1 - c0)), LL(t, gj),
-                   A("GT", slice(c0, c1), slice(16 * gj + 4, 16 * gj + 16, 2)), gj == 0, gj == 1)
-    vcopy(A("spotU"), sp)
-    pieces, w0, l0 = {}, 0, 0
-    for i, nw in enumerate(CFG["pieces"]):
-        pieces[w0 + nw - 1] = (i, w0, nw, l0)
-        vts(C("LP", l0, l0 + 15 * nw), A("SI", ALL, slice(w0, w0 + nw)), float(-R * w0), None, ALU.add)
-        w0, l0 = w0 + nw, l0 + 15 * nw + nw % 2
-    r1 = C("RT1", 0, R)
-    act(r1, C("VV", 2 * R, 3 * R), ACT.Identity, bias=2.0, scale=-1.0)
-    act(A("PR1"), IND(r1, ship))
-    exchange("ar1", lambda b: C("PR1", H * b, H * (b + 1)), lambda b: C("RT1", R + H * b, R + H * (b + 1)))
-    act(A("sq1"), r1, ACT.Square)
-    act(A("tw1"), r1, scale=2.0)
-    for w in range(6):
-        act(A("Crep", ALL, slice(0, 2), w), A("Cn", ALL, slice(0, 2)))
+                mm(bank(2, 168 * t + 6 * c0, 6 * (c1 - c0)), LL(t, gj, "LL" + h),
+                   A("GT" + h, slice(c0, c1), slice(16 * gj + 4, 16 * gj + 16, 2)), gj == 0)
+    act(A("R1"), plane(2), ACT.Identity, bias=2.0, scale=-1.0)
+    act(A("s9"), A("s8"), ACT.Identity, bias=float(R - 7 * H), scale=-7.0)
     for tab in ("T1", "T2"):
-        for z, n in [(C(tab, UPW, UPW + R), R)] + [(blk(tab, 0, b, 6, 7), H) for b in range(NB)]:
-            op("pool", lambda z=z, n=n: g.iota(z[0], [[0, n]], 0, 0, allow_small_or_imprecise_dtypes=True), [], [z])
+        zero(C(tab, UPW, UPW + R + H), R + H)
+        for b in range(NB):
+            n = H if b == NB - 1 else 2 * H
+            zero(blk(tab, 0, b, 6, 6 + n // H), n)
 
     def join(chunks, banks):
-        todo = []
         for ch, wb in zip(chunks, banks):
             s, n = ch[0], len(ch)
             for x in ch:
                 vtt(C("EQ", 336 * x, 336 * (x + 1)), bank(2, 0, 336), A("Crep", ALL, x), ALU.is_equal)
-                if todo:
-                    todo.pop(0)()
             o = bank(wb, 0, 56 * n)
-            mm(o, A("negI"), C("nAB", 0, 56 * n), True, False)
+            mm(o, A("negI"), C("nAB", 0, 56 * n), True)
             for w in range(6):
-                mm(o, C("Wt", 128 * w, 128 * (w + 1)), C("EQ", 336 * s + w, 336 * (s + n), 6), False, w == 5)
+                mm(o, C("Wt", 128 * w, 128 * (w + 1)), C("EQ", 336 * s + w, 336 * (s + n), 6), False)
             oi = C("OI", 56 * s, 56 * (s + n))
-            todo.append(lambda oi=oi, o=o, n=n: vtt(oi, o, C("Brep", 0, 56 * n), ALU.mult))
-            todo.append(lambda oi=oi, s=s, n=n: vcopy(C("OFF", 56 * s, 56 * (s + n)), oi))
-        while todo:
-            todo.pop(0)()
+            vtt(oi, o, C("Brep", 0, 56 * n), ALU.mult)
+            vcopy(C("OFF", 56 * s, 56 * (s + n)), oi)
 
-    join(CFG["chunks"], [3, 4, 5, 6, 7])
+    join(CFG["chunks"], [3, 6, 7, 3, 6])
+    pieces, w0, l0 = {}, 0, 0
+    for i, nw in enumerate(CFG["pieces"]):
+        pieces[w0 + nw - 1] = (i, w0, nw, l0)
+        w0, l0 = w0 + nw, l0 + 15 * nw + nw % 2
 
-    cu, cp, cb = [0], [0], [3]
-    held = []
+    def late_lists():
+        for i, w0, nw, l0 in pieces.values():
+            vcopy(C("LP", l0, l0 + 15 * nw), A("SI", ALL, slice(0, nw)))
+        vtt(A("s1"), A("s9"), A("s5"), ALU.add)
+        vcopy(A("spotD"), A("s1"))
+        vcopy(A("spotU"), sp)
+
+    cu, cp, cb = [0], [0], {}
+    later = {}
 
     def sweep(k):
-        order = [2, 3, 4, 5, 6, 7, 0, 1] if k < 2 else CFG["order3"]
+        order = [2, 3, 4, 5, 6, 7] if k < 2 else CFG["order3"]
         modes = dict(zip(order, CFG["modes"][k]))
+        if k < 2:
+            modes[0], modes[1] = "AD", CFG["diag"][k]
         win = [C("VV", V0, V0 + TW), A("T1"), A("T2")][k]
         xs = ["VV", "XS1", "XS2"][k]
-        xk = [0, 1, 0][k]
+        nx0 = bank([0, 1, 0][k])
         out_tab, pk = [("T1", "PK1"), ("T2", "PK2"), (None, None)][k]
         ub, pb, ab = {}, {}, {}
 
-        def off(s, t=None):
-            return C("OFF", 56 * s, 56 * s + 56) if t is None else C("OFF", 56 * s + 28 * t, 56 * s + 28 * t + 28)
+        def off(s, a, b):
+            return C("OFF", 56 * s + 28 * a, 56 * s + 28 * b)
 
-        def mul(s, t=None):
+        def newbank():
+            b = min(CFG["banks"][k], key=lambda b: cb.get(b, -1))
+            cb[b] = len(ops)
+            return b
+
+        def gather(s):
+            ts = [t for t in range(2) if modes[s][t] == "A"]
+            if ts and s not in ub:
+                ub[s] = "U%d" % (cu[0] % NU)
+                cu[0] += 1
+                act(C(ub[s], R * ts[0], R * (ts[-1] + 1)), IND(win, off(s, ts[0], ts[-1] + 1)))
+
+        def product(s, t):
             if s not in pb:
                 pb[s] = "P%d" % (cp[0] % NP)
                 cp[0] += 1
-            a, b = (0, 2 * R) if t is None else (R * t, R * (t + 1))
-            if modes[s] == "A":
-                vtt(C(pb[s], a, b), C(ub[s], a, b), xp(xk, t), ALU.mult)
+            o = C(pb[s], R * t, R * (t + 1))
+            if modes[s][t] == "A":
+                vtt(o, C(ub[s], R * t, R * (t + 1)), bank([1, 2, 1][k]), ALU.mult)
             else:
-                vtt(C(pb[s], a, b), IND(win, off(s, t)), C(xs, a, b), ALU.mult)
+                vtt(o, IND(win, off(s, t, t + 1)), C(xs, R * t, R * (t + 1)), ALU.mult)
+            return o
 
-        def newbank():
-            cb[0] = (cb[0] + 1) % 4
-            return 4 + cb[0]
+        def first(s, b, a):
+            if modes[s][0] == "A":
+                mm(bank(b), A("Ib"), a, True)
+                vtt(bank(b), C(ub[s], 0, R), nx0, ALU.mult)
+                mm(bank(b), A("Ib"), a, False)
+            else:
+                p = product(s, 0)
+                mm(bank(b), A("Ib"), a, True, True)
+                mm(bank(b), A("negI"), p, False)
 
-        def pe(s):
-            if s == 0:
-                ab[s] = [bank(newbank()), bank(newbank())]
-                for t in range(2):
-                    mm(ab[s][t], A("Ib"), C("VV", R * t, R * (t + 1)), True, k == 0)
-                for t in range(2):
-                    if k:
-                        mm(ab[s][t], A("negI"), C(pb[s], R * (1 - t), R * (2 - t)), False, True)
-                return
-            ab[s] = 2 * k if (s == 1 and k < 2) else newbank()
-            terms = 2 if (s == 1 and k < 2 and CFG["diag_pe"]) or (k, s) in CFG["two"] else (0 if (k, s) in CFG["nope"] else 1)
-            mm(bank(ab[s]), A("Ib"), C("VV", R * (s + 1), R * (s + 2)), True, terms == 0)
-            for t in range(terms):
-                mm(bank(ab[s]), A("negI"), C(pb[s], R * t, R * (t + 1)), False, t == terms - 1)
+        def products(s, b=None, second_first=False):
+            ab[s] = b or newbank()
+            if second_first:
+                p = product(s, 1)
+            first(s, ab[s], plane(s + 1))
+            if not second_first:
+                p = product(s, 1)
+            if modes[s][2:] != "V":
+                mm(bank(ab[s]), A("negI"), p, False)
 
         def finish(s, halves=False):
-            if s == 0:
-                for t in range(2):
-                    if k == 0:
-                        vtt(C("XS1", R * t, R * (t + 1)), ab[s][t], C(pb[s], R * (1 - t), R * (2 - t)), ALU.subtract)
-                    elif k == 1:
-                        vtt(C("XS2", R * t, R * (t + 1)), ab[s][t], C("RK1", R * t, R * (t + 1)), ALU.mult)
-                    else:
-                        o = C("YY", R * t, R * (t + 1))
-                        vtt(o, ab[s][t], C("RK2", R * t, R * (t + 1)), ALU.mult)
-                        store("sync", T.y[:, R * t:R * (t + 1)], o)
-                return
-            if (k, s) in CFG["two"]:
-                o = C(out_tab, R * (s - 2), R * (s - 1)) if k < 2 else C("YY", R * (s + 1), R * (s + 2))
-                gathers_upto(min(order.index(s) + 2, 5 if k < 2 else 7))
-                act(o, bank(ab[s]))
-                if k == 2:
-                    store("sync", T.y[:, R * (s + 1):R * (s + 2)], o)
-                return
-            if (k, s) in CFG["nope"]:
-                vtt(bank(ab[s]), bank(ab[s]), C(pb[s], 0, R), ALU.subtract)
-            if k < 2:
-                vtt(C(out_tab, R * (s - 2), R * (s - 1)), bank(ab[s]), C(pb[s], R, 2 * R), ALU.subtract)
-                return
             parts = [(0, R // 2, "scalar"), (R // 2, R // 2, "sync")] if halves else [(0, R, "sync")]
             for a, n, q in parts:
-                y0 = R * (s + 1) + a
-                o = C("YY", y0, y0 + n)
-                vtt(o, bank(ab[s], a, n), C(pb[s], R + a, R + a + n), ALU.subtract)
-                store(q, T.y[:, y0:y0 + n], o)
+                z = R * (s - 2) + a if k < 2 else R * (s + 1) + a
+                o = C(out_tab or "YY", z, z + n)
+                if modes[s][2] == "V":
+                    vtt(o, bank(ab[s], a, n), C(pb[s], R + a, R + a + n), ALU.subtract)
+                else:
+                    act(o, bank(ab[s], a, n))
+                if k == 2:
+                    store(q, T.y[:, z:z + n], o)
 
-        alist = [s for s in order if modes[s] == "A"]
-
-        def gathers_upto(i):
-            while alist and order.index(alist[0]) <= i:
-                s = alist.pop(0)
-                ub[s] = "U%d" % (cu[0] % NU)
-                cu[0] += 1
-                act(A(ub[s]), IND(win, off(s)))
+        def lower():
+            p = product(0, 1)
+            b0 = 1 if k == 0 else newbank()
+            mm(bank(b0), A("Ib" if k == 2 else "nIb"), plane(0), True, True)
+            mm(bank(b0), A("negI" if k == 2 else "posI"), p, False)
+            b1 = 2 if k == 0 else newbank()
+            first(0, b1, plane(1))
+            if k == 0:
+                act(C("XS1", R, 2 * R), bank(b1))
+                if any(m[0] == "D" for m in CFG["modes"][1] + CFG["diag"][1:]):
+                    act(C("XS1", 0, R), bank(1), scale=-1.0)
+            elif k == 1:
+                vtt(C("XS2", R, 2 * R), bank(b1), C("RK1", R, 2 * R), ALU.mult)
+                vtt(bank(0), bank(b0), C("RK1", 0, R), ALU.mult)
+                if any(m[0] == "D" for m in CFG["modes"][2]):
+                    act(C("XS2", 0, R), bank(0), scale=-1.0)
+                if any(m[1] == "A" for m in CFG["modes"][2]):
+                    later.setdefault((2, -1), []).append(lambda: act(bank(1), C("XS2", R, 2 * R)))
+            else:
+                for t, b in ((1, b1), (0, b0)):
+                    o = C("YY", R * t, R * (t + 1))
+                    vtt(o, bank(b), C("RK2", R * t, R * (t + 1)), ALU.mult)
+                    store("sync", T.y[:, R * t:R * (t + 1)], o)
 
         def send(w):
             if w in pieces:
                 i, w0, nw, l0 = pieces[w]
                 n, z = H * nw, NB * H * w0
-                act(C(pk, z, z + NB * n), IND(C(out_tab, R * w0, R * (w0 + nw)), C("LP", l0, l0 + 15 * nw)))
+                cut = CFG["cut"][k][i]
+                for fn, b0, b1 in ((vcopy, 0, cut), (act, cut, NB)):
+                    if b0 < b1:
+                        fn(C(pk, z + b0 * n, z + b1 * n), IND(C(out_tab, R * w0, R * (w0 + nw)), C("LP", l0 + 3 * nw * b0, l0 + 3 * nw * b1)))
                 exchange("a%d%d" % (k + 1, i), lambda b: C(pk, z + n * b, z + n * (b + 1)), lambda b: blk(out_tab, 0, b, w0, w0 + nw))
 
-        nmain = 6 if k < 2 else 8
-        for i, s in enumerate(order[:nmain]):
-            gathers_upto(min(i + 1, nmain - 1))
-            if k == 2 and i == CFG["r3at"]:
-                held.pop(0)()
-            if k == 2 and i == CFG["rk2at"]:
-                act(A("RK2"), IND(A("RT2"), A("spotU")))
-            prev = order[i - 1] if i else None
-            if i == nmain - 1:
-                mul(s, 0); pe(s); finish(prev); mul(s, 1)
+        def done(s, halves=False):
+            if s:
+                finish(s, halves)
                 if k < 2:
-                    send(prev - 2)
-                finish(s, halves=True)
-                if k < 2:
-                    send(5)
+                    send(s - 2)
+
+        lag = CFG["lag"][k]
+        for i, s in enumerate(order):
+            for x in order[i:i + 1 + CFG["ahead"][k]]:
+                gather(x)
+            for fn in later.pop((k, i), []):
+                fn()
+            if s == 0:
+                lower()
             else:
-                mul(s); pe(s)
-                if prev is not None:
-                    finish(prev)
-                    if k < 2:
-                        gathers_upto(min(i + CFG["ahead"], 5))
-                        send(prev - 2)
+                products(s, second_first=(i == 0 and k > 0))
+            if i == 0 and k == 0:
+                late_lists()
+            if k == 0 and i == CFG["joinat"]:
+                join(CFG["chunks2"], [3, 3])
+            if i >= lag:
+                done(order[i - lag])
+        for s in order[len(order) - lag:]:
+            done(s, halves=(k == 2 and s == order[-1]))
         if k == 2:
             return
+
+        def at(key, fn):
+            if CFG[key] < 0:
+                fn()
+            else:
+                later.setdefault((k + 1, CFG[key]), []).append(fn)
+
+        if k == 0 and CFG["joinat"] > 5:
+            join(CFG["chunks2"], [3, 3])
+        gather(0)
+        gather(1)
+        lower()
+        products(1, 3)
+        for fn in later.pop((k + 1, -1), []):
+            fn()
         if k == 0:
-            act(A("RK1"), IND(A("RT1"), A("spotU")))
-            join([[0], [1]], [newbank(), newbank()])
-        else:
-            held.pop(0)()
-            act(A("PR2"), IND(C("RT2", 0, R), ship))
-            exchange("ar2", lambda b: C("PR2", H * b, H * (b + 1)), lambda b: C("RT2", R + H * b, R + H * (b + 1)))
-        gathers_upto(7)
-        sq, tw, rr = [("sq1", "tw1", "RT1"), ("sq2", "tw2", "RT2")][k]
-        if k == 0 and CFG["low1"] == "pe":
             for t in range(2):
-                mul(0, 1 - t)
-                mm(xp(1, t), A("Ib"), C("VV", R * t, R * (t + 1)), True, False)
-                mm(xp(1, t), A("negI"), C(pb[0], R * (1 - t), R * (2 - t)), False, True)
-                act(C("XS1", R * t, R * (t + 1)), xp(1, t))
-            mul(1); pe(1)
-        elif k == 0:
-            mul(0, 1); mul(0, 0); pe(0); finish(0)
-            act(xp(1), A("XS1"))
-            mul(1); pe(1)
-        else:
-            mul(0, 1); mul(0, 0); pe(0); mul(1); pe(1); finish(0)
-            act(A(sq), C(rr, 0, R), ACT.Square)
-            act(A(tw), C(rr, 0, R), scale=2.0)
-            act(xp(0), A("XS2"))
-        d = bank(ab[1])
-        rn = C("RT2", 0, R) if k == 0 else A("R3")
+                act(C("RK1", R * t, R * (t + 1)), IND(C("VV", 2 * R, V0 + TW), C("spotD", 28 * t, 28 * t + 28)), ACT.Identity, bias=2.0, scale=-1.0)
+        d = bank(3)
+        r, rn = (A("R1"), C("RT2", 0, R)) if k == 0 else (C("RT2", 0, R), A("R3"))
 
         def rstep():
-            if not CFG["diag_pe"]:
-                vtt(d, d, C(pb[1], R, 2 * R), ALU.subtract)
-            vtt(d, d, A(sq), ALU.mult)
-            vtt(rn, A(tw), d, ALU.subtract)
+            if CFG["rsq"][k]:
+                e = bank(CFG["rsq"][k])
+                act(A("SQ"), r, ACT.Square)
+                mm(e, A("Ib"), plane(2), True)
+                vtt(e, d, A("SQ"), ALU.mult)
+                if k == 0:
+                    mm(e, A("Ib"), plane(2), False)
+                    mm(e, A("Ib"), plane(2), False)
+                    act(rn, e, ACT.Identity, bias=4.0, scale=-1.0)
+                else:
+                    mm(e, A("n2I"), r, False)
+                    act(rn, e, scale=-1.0)
+            else:
+                vtt(d, d, r, ALU.mult)
+                act(d, d, ACT.Identity, bias=2.0, scale=-1.0)
+                vtt(rn, d, r, ALU.mult)
             if k == 1:
                 store("sync", T.inv[:], rn)
-        held.append(rstep)
+
+        def send_r():
+            act(A("PR2"), IND(rn, ship))
+            exchange("ar2", lambda b: C("PR2", H * b, H * (b + 1)), lambda b: C("RT2", R + H * b, R + H * (b + 1)))
+
+        if k == 0:
+            at("r2at", rstep)
+            at("pr2at", send_r)
+        else:
+            at("rk2at", lambda: act(A("RK2"), IND(A("RT2"), A("spotU"))))
+            at("r3at", rstep)
 
     for k in range(3):
         sweep(k)
 
     for o in ops:
         o["acc"] = [(n, m, True, _banks(m) if n == "PS" else 0) for n, m in o["w"]] + [(n, m, False, _banks(m) if n == "PS" else 0) for n, m in o["r"]]
-    deps = []
+    deps, behind = [], []
+    users, lastdma = {}, {}
     for j, o in enumerate(ops):
-        d = []
-        for i in range(j):
-            e = ops[i]
-            if (e["q"] == "tensor" and o["q"] == "tensor") or o["q"] == "arrive" or e["sem"] in ("remote", "stored"):
-                continue
-            for n1, m1, w1, b1 in e["acc"]:
-                if any(n1 == n2 and ((b1 & b2 and e["q"] != o["q"]) or ((w1 or w2) and m1 & m2)) for n2, m2, w2, b2 in o["acc"]):
-                    d.append(i)
-                    break
-        deps.append(d)
+        d, f = set(), set()
+        for n2, m2, w2, b2 in o["acc"]:
+            for i, m1, w1, b1 in users.get(n2, ()):
+                q1 = ops[i]["q"]
+                if q1 == "tensor" and o["q"] == "tensor":
+                    if b1 & b2:
+                        f.add(i)
+                elif o["q"] != "arrive" and ((b1 & b2 and q1 != o["q"]) or ((w1 or w2) and m1 & m2)):
+                    d.add(i)
+        if o["q"] == "arrive":
+            f.update((j - 2, j - 1))
+        elif o["sem"] not in (None, "stored") or o["q"] == "pool":
+            if o["q"] in lastdma:
+                f.add(lastdma[o["q"]])
+            lastdma[o["q"]] = j
+        if o["sem"] not in ("remote", "stored"):
+            for n2, m2, w2, b2 in o["acc"]:
+                users.setdefault(n2, []).append((j, m2, w2, b2))
+        deps.append(sorted(d))
+        behind.append(sorted(f))
+    if not ORDER:
+        ORDER.extend(issue_order(ops, deps, behind))
+    order = ORDER
+    place = {j: p for p, j in enumerate(order)}
     needed = set()
     for j, o in enumerate(ops):
-        o["latest"] = {ops[i]["q"]: i for i in deps[j] if ops[i]["sem"] is None}
+        o["latest"] = {ops[i]["q"]: i for i in sorted(deps[j], key=place.get) if ops[i]["sem"] is None}
         needed.update(o["latest"].values())
     cnt = {"vector": 0, "scalar": 0, "tensor": 0, "pool": 0}
-    for j, o in enumerate(ops):
+    for j in order:
+        o = ops[j]
         if o["sem"] is not None:
             o["tok"] = (o["sem"], o["n"])
         elif j in needed:
@@ -503,7 +655,8 @@ def rank_program(g, core, T, topo):
             o["tok"] = (o["q"], cnt[o["q"]])
     queue = {"vector": g.vector, "scalar": g.scalar, "tensor": g.tensor, "pool": g, "sync": g.sync}
     seen = {q: {} for q in queue}
-    for j, o in enumerate(ops):
+    for j in order:
+        o = ops[j]
         if o["q"] == "arrive":
             continue
         want = [ops[i]["tok"] for i in o["latest"].values()] + [ops[i]["tok"] for i in deps[j] if ops[i]["sem"] is not None]

@@ -3,64 +3,65 @@ from concourse.bass import DstId, RemoteDMATransfer
 from concourse.mybir import AluOpType, ActivationFunctionType
 
 R, H, NB = 448, 48, 5
-UPW = 6 * R
 BLK = 8 * H
 TW = 7 * R + NB * BLK
-V0 = 3 * R
+Z0 = 3 * R
 MID = -1344.0
 NU, NP = 8, 8
 
 CFG = {
     "modes": [["AAS", "AAS", "ADS", "ADS", "ADS", "ADV"],
-              ["ADS", "ADV", "ADS", "ADS", "ADS", "ADV"],
-              ["ADS", "AAS", "ADS", "AAV", "AD", "ADS", "ADS", "ADV"]],
+              ["ADS", "ADS", "ADV", "ADS", "ADS", "ADV"],
+              ["ADS", "ADS", "ADS", "ADS", "AA", "ADS", "ADS", "ADV"]],
     "order3": [2, 3, 4, 5, 0, 1, 6, 7],
-    "diag": ["AD", "AD"],
-    "pieces": [3, 3],
-    "chunks": [[2], [3], [4, 5], [6, 7]], "ksplit": 10,
-    "ahead": [2, 2, 2], "lag": [1, 1, 1], "joinat": 9, "chunks2": [[0, 1]], "pr2at": 1, "r2at": -1, "r3at": -1, "rk2at": -1,
-    "first": 2.3, "rows": 0.75, "perword": 0.006, "cut": [[0, 0, 0], [0, 0, 0]], "store": 0.5,
-    "banks": [[4, 5, 6, 7, 3], [4, 5, 6, 7, 0], [4, 5, 6, 7, 2, 3]], "rsq": [0, 2],
-    "cases": [(1.5, 1.0), (1.15, 1.2), (1.95, 0.8)], "seed": 1, "rounds": 2500, "nudge": 6, "give": 0.08,
+    "diag": ["AD", "AD"], "cn": "VV", "crep1": False, "crepS": 0, "siS": 5, "hold": True,
+    "fill": [["posI"], ["sq", "rk1"], ["rk0", "x2", "lists", "n2I"]], "ahead": 2,
+    "gp": [[2, 4, 6], [3, 5], [3, 6]], "fp": [[2], [2], [2]],
+    "pieces": [2, 2, 2],
+    "cut": [[0, 0, 2], [0, 0, 2]],
+    "chunks": [[2], [3], [4, 5], [6, 7]], "turn": [(0, 8, "V"), (8, 18, "S"), (18, 28, "S")],
+    "banks": [[4, 5, 6, 7, 3, 4], [4, 5, 6, 7, 0, 4, 5], [4, 5, 6, 7, 2, 3, 4, 5, 6]], "rsq": [0, 6],
+    "first": 2.3, "rows": 0.75, "perword": 0.006, "store": 0.5,
+    "cases": [(1.5, 1.0, 1.0, 0.08), (1.15, 1.2, 0.9, 0.05), (1.95, 0.8, 1.1, 0.12), (1.4, 0.75, 1.15, 0.1)], "seed": 2, "rounds": 300, "swaps": 5000, "heat": 0.2, "nudge": 3, "give": 0.05, "sigma": 1.0, "big": 0.12,
 }
 FIXED = {"vector": 0.05, "scalar": 0.09, "tensor": 0.03, "pool": 0.13}
 CYCLE = {"vector": 0.00083, "scalar": 0.00083, "tensor": 0.000417, "pool": 0.00083}
-WAKE = 0.08
 
 SCRATCH = {
-    "CI": ("sbuf", [128, R], "int32"), "CT": ("sbuf", [128, R + NB * H], "float32"),
+    "CI": ("sbuf", [128, R + NB * H], "int32"), "CH": ("sbuf", [128, R], "float16"), "CP": ("sbuf", [128, NB * H], "int32"),
     "shipI": ("sbuf", [128, 15], "int32"), "shipU": ("sbuf", [128, 16], "uint16"),
-    "spotI": ("sbuf", [128, 56], "int32"), "spotK": ("sbuf", [128, 56], "uint16"), "spotU": ("sbuf", [128, 56], "uint16"),
-    "spotD": ("sbuf", [128, 56], "uint16"),
-    "CP": ("sbuf", [128, NB * H], "float32"),
-    "GK": ("sbuf", [128, 896], "float32"), "GT": ("sbuf", [128, 28, 32], "float32"), "OT": ("sbuf", [128, 14, 32], "float32"),
-    "GKh": ("sbuf", [128, 896], "float16"), "GTh": ("sbuf", [128, 28, 32], "float16"), "LLh": ("sbuf", [128, 512], "float16"),
-    "Cn": ("sbuf", [128, 56, 8], "float16"), "Crep": ("sbuf", [128, 56, 8, 6], "float16"),
-    "EQ": ("sbuf", [128, 8 * 336], "bfloat16"), "OI": ("sbuf", [128, R], "int32"), "OFF": ("sbuf", [128, R], "uint16"),
+    "spotI": ("sbuf", [128, 56], "int32"), "SP": ("sbuf", [128, 56], "float32"),
+    "spotK": ("sbuf", [128, 56], "uint16"), "spotU": ("sbuf", [128, 56], "uint16"), "spotD": ("sbuf", [128, 56], "uint16"),
+    "LS": ("sbuf", [128, 56], "uint16"), "OFL": ("sbuf", [128, 56], "uint16"),
+    "GK": ("sbuf", [128, 896], "float16"), "GT": ("sbuf", [128, 28, 32], "float16"), "OT": ("sbuf", [128, 14, 32], "float16"),
+    "C0": ("sbuf", [128, 28], "float16"), "Cn": ("sbuf", [128, 56, 8], "float16"), "Crep": ("sbuf", [128, 56, 8, 6], "float16"),
+    "EQ": ("sbuf", [128, 2, 224, 6], "bfloat16"), "OFF": ("sbuf", [128, 2, 224], "uint16"),
     "DD": ("sbuf", [128, 128], "float32"), "pI": ("sbuf", [128, 4], "int32"), "cI": ("sbuf", [128, 4], "int32"),
-    "mk": ("sbuf", [128, 4], "float32"), "LL": ("sbuf", [128, 512], "float32"),
-    "n2I": ("sbuf", [128, 128], "float32"), "SQ": ("sbuf", [128, R], "float32"),
-    "negI": ("sbuf", [128, 128], "float32"), "posI": ("sbuf", [128, 128], "float32"),
+    "mk": ("sbuf", [128, 4], "float32"), "LL": ("sbuf", [128, 512], "float16"), "N16": ("sbuf", [128, 56], "float32"),
+    "negI": ("sbuf", [128, 128], "float32"), "posI": ("sbuf", [128, 128], "float32"), "n2I": ("sbuf", [128, 128], "float32"),
     "Ib": ("sbuf", [128, 128], "bfloat16"), "nIb": ("sbuf", [128, 128], "bfloat16"), "Wt": ("sbuf", [128, 768], "bfloat16"),
-    "s1": ("sbuf", [128, 56], "float32"), "s2": ("sbuf", [128, 56], "int32"), "s3": ("sbuf", [128, 56], "float32"),
-    "s4": ("sbuf", [128, 56], "float32"), "s5": ("sbuf", [128, 56], "float32"), "s6": ("sbuf", [128, 56], "float32"),
-    "s7": ("sbuf", [128, 56], "float32"), "s8": ("sbuf", [128, 56], "float32"), "s9": ("sbuf", [128, 56], "float32"),
-    "nAB": ("sbuf", [128, 112], "float32"), "Brep": ("sbuf", [128, 112], "float32"),
-    "VV": ("sbuf", [128, V0 + TW], "bfloat16"), "T1": ("sbuf", [128, TW], "float32"), "T2": ("sbuf", [128, TW], "float32"),
+    "nAB": ("sbuf", [128, 2, 2, 28], "float32"), "Brep": ("sbuf", [128, 2, 2, 28], "float32"),
+    "VV": ("sbuf", [128, Z0 + TW], "bfloat16"), "T1": ("sbuf", [128, TW], "float32"), "T2": ("sbuf", [128, TW], "float32"),
+    "AS": ("sbuf", [128, 896], "bfloat16"),
     "PK0": ("sbuf", [128, NB * 7 * H], "bfloat16"), "PK1": ("sbuf", [128, NB * 6 * H], "float32"), "PK2": ("sbuf", [128, NB * 6 * H], "float32"),
-    "SI": ("sbuf", [128, NB, 7, 3], "int32"), "L7": ("sbuf", [128, 106], "uint16"), "LP": ("sbuf", [128, 96], "uint16"),
-    "R1": ("sbuf", [128, R], "float32"), "RT2": ("sbuf", [128, R + NB * H], "float32"), "PR2": ("sbuf", [128, NB * H], "float32"),
+    "SI": ("sbuf", [128, NB, 7, 3], "float32"), "L7": ("sbuf", [128, 106], "uint16"), "LP": ("sbuf", [128, 142], "uint16"),
+    "SQ": ("sbuf", [128, R], "float32"), "RT2": ("sbuf", [128, R + NB * H], "float32"), "PR2": ("sbuf", [128, NB * H], "float32"),
     "RK1": ("sbuf", [128, 896], "float32"), "RK2": ("sbuf", [128, 896], "float32"), "R3": ("sbuf", [128, R], "float32"),
-    "XS1": ("sbuf", [128, 896], "float32"), "XS2": ("sbuf", [128, 896], "float32"),
+    "X1": ("sbuf", [128, R], "float32"), "XS2": ("sbuf", [128, 896], "float32"),
     "YY": ("sbuf", [128, 9 * R], "float32"),
-    "PS": ("psum", [128, 4096], "float32"),
+    "PS": ("psum", [128, 8, 512], "float32"),
 }
+for _n in ("m", "d", "e"):
+    SCRATCH["w" + _n] = ("sbuf", [128, 28], "float32")
+for _n in ("s1", "s3", "s4", "s5", "s6", "s7", "s8", "s9", "sa", "MS", "Bm"):
+    SCRATCH[_n] = ("sbuf", [128, 56], "float32")
+SCRATCH["s2"] = ("sbuf", [128, 56], "int32")
 for _i in range(NU):
     SCRATCH["U%d" % _i] = ("sbuf", [128, 896], "float32")
 for _i in range(NP):
-    SCRATCH["P%d" % _i] = ("sbuf", [128, 896], "float32")
+    SCRATCH["P%d" % _i] = ("sbuf", [128, R], "float32")
 
-LOADS = ["lc0", "lc1", "lship", "lspot", "lv0", "lv1", "lv2"]
+LOADS = ["lc0", "lc1", "lship", "lspot", "lv0", "lv1", "lv2", "lv3"]
 ARRIVALS = ["ac", "a0", "a10", "a11", "a12", "ar2", "a20", "a21", "a22"]
 SEMAPHORES = ["vector", "scalar", "tensor", "pool", "sent", "stored"] + LOADS + ARRIVALS
 
@@ -114,9 +115,10 @@ def issue_order(ops, deps, behind):
         for i, w in before[j]:
             after[i].append((j, w))
     cases = []
-    for rate, dma in CFG["cases"]:
-        cost = [(o["cost"] * dma if o["q"] == "arrive" else o["cost"]) + o["gathered"] * rate for o in ops]
-        cases.append((cost, [o["lag"] * dma + WAKE for o in ops]))
+    for rate, dma, pe, wake in CFG["cases"]:
+        scale = {"arrive": dma, "pool": dma, "tensor": pe}
+        cost = [o["cost"] * scale.get(o["q"], 1.0) + o["gathered"] * rate for o in ops]
+        cases.append((cost, [o["lag"] * dma + wake for o in ops]))
     cost, lag = cases[0]
 
     def lay(order, back):
@@ -158,22 +160,83 @@ def issue_order(ops, deps, behind):
         return length(order), end, order
 
     rng = np.random.default_rng(CFG["seed"])
+    big = [j for j in every if cost[j] > CFG["big"]]
     best = cur = judge(tighten(lay(every, False)))
     for it in range(CFG["rounds"]):
         key = [cur[1][j] - cost[j] for j in every]
-        for j in rng.integers(0, len(ops), CFG["nudge"]):
-            key[j] += float(rng.normal())
+        for j in rng.choice(big, CFG["nudge"]):
+            key[j] += float(rng.normal()) * CFG["sigma"]
         for j in every:
             for i, _ in before[j]:
                 if key[j] <= key[i]:
                     key[j] = key[i] + 1e-6
         end = lay(sorted(every, key=lambda j: (key[j], j)), False)
         new = judge(tighten(end) if it % 3 == 0 else end)
-        if new[0] < cur[0] + CFG["give"]:
+        if new[0] < cur[0] + CFG["give"] * (1.0 - it / CFG["rounds"]):
             cur = new
         if new[0] < best[0]:
             best = new
-    return best[2]
+
+    queue = [o["q"] for o in ops]
+
+    def clock(seq):
+        prev, nxt = {}, {}
+        for s in seq.values():
+            prev.update(zip(s[1:], s))
+            nxt.update(zip(s, s[1:]))
+        left = [len(before[j]) + (j in prev) for j in every]
+        order = [j for j in every if not left[j]]
+        for j in order:
+            for i in [i for i, _ in after[j]] + ([nxt[j]] if j in nxt else []):
+                left[i] -= 1
+                if not left[i]:
+                    order.append(i)
+        if len(order) < len(ops):
+            return None
+        total, ends = 0.0, []
+        for cost, lag in cases:
+            end = [0.0] * len(ops)
+            for j in order:
+                t = end[prev[j]] if j in prev else 0.0
+                for i, w in before[j]:
+                    x = end[i] + lag[i] if w else end[i]
+                    if x > t:
+                        t = x
+                end[j] = t + cost[j]
+            total += max(end[j] + lag[j] for j in every)
+            ends.append(end)
+        return total, order, ends, prev
+
+    seq = {q: [j for j in best[2] if queue[j] == q] for q in set(queue)}
+    best = cur = clock(seq)
+    for it in range(CFG["swaps"]):
+        c = int(rng.integers(len(cases)))
+        (cost, lag), end, prev, arcs = cases[c], cur[2][c], cur[3], []
+        j = max(every, key=lambda j: end[j] + lag[j])
+        while True:
+            t = end[j] - cost[j]
+            if j in prev and end[prev[j]] > t - 1e-9:
+                arcs.append(j)
+                j = prev[j]
+                continue
+            j = next((i for i, w in before[j] if end[i] + (lag[i] if w else 0.0) > t - 1e-9), None)
+            if j is None:
+                break
+        v = arcs[int(rng.integers(len(arcs)))]
+        s = list(seq[queue[v]])
+        p, far = s.index(v), int(rng.integers(1, 4))
+        if rng.random() < 0.5:
+            s.insert(max(p - far, 0), s.pop(p))
+        else:
+            s.insert(p - 1 + far, s.pop(p - 1))
+        trial = dict(seq)
+        trial[queue[v]] = s
+        new = clock(trial)
+        if new and new[0] < cur[0] - CFG["heat"] * (1.0 - it / CFG["swaps"]) * float(np.log(rng.random())):
+            cur, seq = new, trial
+            if new[0] < best[0]:
+                best = new
+    return best[1]
 
 
 def rank_program(g, core, T, topo):
@@ -183,6 +246,8 @@ def rank_program(g, core, T, topo):
     cores = list(T.cores)
     peers = [c for c in cores if c != core]
     ops = []
+
+    hold = {}
 
     def A(name, *idx):
         ix = tuple(idx) if idx else (ALL,)
@@ -208,7 +273,7 @@ def rank_program(g, core, T, topo):
                     rate = 0.5 if q == "vector" and all(SCRATCH[x[1]][2].endswith("16") for x in rd[:1] + writes) else 1.0
                 cost = FIXED[q] + max(64, n * rate) * CYCLE[q]
         ops.append({"q": q, "fn": fn, "r": [(x[1], x[2]) for x in rd], "w": [(x[1], x[2]) for x in writes], "sem": sem, "n": count,
-                    "cost": cost, "gathered": gathered, "lag": lag})
+                    "cost": cost, "gathered": gathered, "lag": lag, "hold": hold.get(q)})
 
     def vcopy(o, i, extra=()):
         op("vector", lambda: g.vector.tensor_copy(o[0], i[0]), [i] + list(extra), [o])
@@ -225,30 +290,31 @@ def rank_program(g, core, T, topo):
     def vtr(o, i):
         op("vector", lambda: g.vector.transpose(o[0], i[0]), [i], [o])
 
-    def act(o, i, f=ACT.Copy, bias=None, scale=None):
+    def act(o, i, f=ACT.Copy, bias=None, scale=None, extra=()):
         kw = {}
         if bias is not None:
             kw["bias"] = bias
         if scale is not None:
             kw["scale"] = scale
-        op("scalar", lambda: g.scalar.activation(o[0], i[0], f, **kw), [i], [o])
+        op("scalar", lambda: g.scalar.activation(o[0], i[0], f, **kw), [i] + list(extra), [o])
 
-    def zero(z, n):
-        op("pool", lambda: g.iota(z[0], [[0, n]], 0, 0, allow_small_or_imprecise_dtypes=True), [], [z], rate=2.0)
+    def iota(z, pattern, per_partition=0):
+        op("pool", lambda: g.iota(z[0], pattern, 0, per_partition, allow_small_or_imprecise_dtypes=True), [], [z], rate=2.0)
+
+    def zero(z):
+        iota(z, [[0, z[2].bit_count()]])
 
     groups = {b: [] for b in range(8)}
-    wide = set()
 
-    def mm(o, l, r, start, full=False):
+    def mm(o, l, r, start):
         b = _banks(o[2]).bit_length() - 1
         me = {"start": start, "stop": True}
         if not start:
             groups[b][-1]["stop"] = False
         groups[b].append(me)
-        if start:
-            (wide.add if full else wide.discard)(b)
-        op("tensor", lambda: g.tensor.matmul(o[0], l[0], r[0], me["start"], me["stop"]), [l, r], [o])
-        ops[-1]["cost"] = FIXED["tensor"] + max(64, o[2].bit_count()) * CYCLE["tensor"] * (4 if SCRATCH[l[1]][2] == "float32" else 1)
+        op("tensor", lambda: g.tensor.matmul(o[0], l[0], r[0], me["start"], me["stop"]), [l, r], [o],
+           rate=4.0 if SCRATCH[l[1]][2] == "float32" else 1.0,
+           cost=FIXED["tensor"] + max(64, o[2].bit_count()) * CYCLE["tensor"] * (4 if SCRATCH[l[1]][2] == "float32" else 1))
 
     def load(q, sem, o, src, lag):
         eng = g.sync if q == "sync" else g.scalar
@@ -299,315 +365,316 @@ def rank_program(g, core, T, topo):
         return C(tab, z + H * w0, z + H * w1)
 
     def bank(b, a=0, n=R):
-        return C("PS", 512 * b + a, 512 * b + a + n)
+        return A("PS", b, slice(a, a + n))
 
     def plane(s):
+        s += s > 2
         return C("VV", R * s, R * (s + 1))
+
+    def half(name, t, n=R):
+        return C(name, n * t, n * (t + 1))
 
     ship = C("shipU", 0, 15)
 
-    ev = (T.CI[0::2, :], "CI", _mask("CI", (ALL,)))
-    od = (T.CI[1::2, :], "CIodd", 1)
-    load("sync", "lship", A("shipI"), T.ship[:], 2.1)
-    load("scalar", "lc1", od, T.col[:, 0:8 * R], 2.0)
-    load("sync", "lc0", ev, T.col[:, R:9 * R], 2.8)
-    load("scalar", "lspot", A("spotI"), T.spot[:], 2.4)
-    load("sync", "lv0", C("VV", 2 * R, 6 * R), T.val[:, 2 * R:6 * R], 3.4)
-    load("sync", "lv1", C("VV", 6 * R, 9 * R), T.val[:, 6 * R:9 * R], 4.2)
-    load("sync", "lv2", C("VV", 0, 2 * R), T.val[:, 0:2 * R], 4.8)
+    ev = (T.CI[0::2, 0:R], "CI", _mask("CI", (slice(0, R),)))
+    od = (T.CI[1::2, 0:R], "CIodd", 1)
+    load("sync", "lship", A("shipI"), T.ship[:], 1.8)
+    load("scalar", "lc1", od, T.col[:, 0:8 * R], 1.9)
+    load("sync", "lc0", ev, T.col[:, R:9 * R], 2.1)
+    load("sync", "lspot", A("spotI"), T.spot[:], 2.2)
+    load("sync", "lv0", C("VV", 4 * R, 7 * R), T.val[:, 3 * R:6 * R], 2.9)
+    load("sync", "lv1", plane(2), T.val[:, 2 * R:3 * R], 3.2)
+    load("sync", "lv2", C("VV", 7 * R, 10 * R), T.val[:, 6 * R:9 * R], 3.9)
+    load("sync", "lv3", C("VV", 0, 2 * R), T.val[:, 0:2 * R], 4.4)
 
     op("pool", lambda: g.iota(T.pI[:, 0:1], [[0, 1]], 0, 1), [], [C("pI", 0, 1)], cost=0.13)
-    op("pool", lambda: g.iota(T.DD[:], [[1, 128]], 0, -1, allow_small_or_imprecise_dtypes=True), [], [A("DD")], rate=2.0)
-    zero(plane(9), R)
+    iota(A("DD"), [[1, 128]], -1)
+    iota(A("N16"), [[0, 2], [16, 28]])
+    zero(C("VV", Z0, Z0 + R))
     for b in range(NB):
-        zero(blk("VV", V0, b, 6, 7), H)
+        zero(blk("VV", Z0, b, -1, 0))
     vts(C("cI", 0, 1), C("pI", 0, 1), 4, 1, ALU.arith_shift_right, ALU.bitwise_and)
     vts(A("negI"), A("DD"), 0.0, -1.0, ALU.is_equal, ALU.mult)
     vts(C("mk", 0, 1), C("cI", 0, 1), 0.0, None, ALU.is_equal)
     vts(C("mk", 1, 2), C("cI", 0, 1), 1.0, None, ALU.is_equal)
+    vts(C("cI", 1, 2), C("pI", 0, 1), 15, None, ALU.bitwise_and)
+    vts(C("mk", 2, 3), C("cI", 1, 2), float(R), None, ALU.add)
+    vcopy(C("mk", 3, 4), C("cI", 1, 2))
 
-    def LL(t, gj, name="LL"):
-        return C(name, (2 * t + gj) * 128, (2 * t + gj + 1) * 128)
+    def LL(t, gj):
+        return C("LL", (2 * t + gj) * 128, (2 * t + gj + 1) * 128)
     for t in range(2):
         for gj in range(2):
             m = C("mk", t, t + 1)
             vts(LL(t, gj), A("DD"), float(16 * (gj - t)), m[0], ALU.is_equal, ALU.mult, extra=[m])
-    vcopy(A("LLh"), A("LL"))
     act(A("Ib"), A("negI"), scale=-1.0)
     act(A("nIb"), A("negI"))
-    act(A("posI"), A("negI"), scale=-1.0)
-    act(A("n2I"), A("negI"), scale=2.0)
     for w in range(6):
-        act(C("Wt", 128 * w, 128 * (w + 1)), A("negI"), scale=float(6 - w))
+        act(half("Wt", w, 128), A("negI"), scale=-float(w + 1))
 
     vcopy(ship, A("shipI"))
     for w in range(7):
-        vts(A("SI", ALL, w), A("shipI"), float(R * w), None, ALU.add)
-    vts(A("CP"), IND(A("CI"), ship), MID, None, ALU.add, extra=[od])
-    exchange("ac", lambda b: C("CP", H * b, H * (b + 1)), lambda b: C("CT", R + H * b, R + H * (b + 1)))
+        if w < CFG["siS"]:
+            act(A("SI", ALL, w), A("shipI"), ACT.Identity, bias=float(R * (w + 2) if w < 6 else 0))
+        else:
+            vts(A("SI", ALL, w), A("shipI"), float(R * (w + 2) if w < 6 else 0), None, ALU.add)
+    vcopy(A("CP"), IND(C("CI", 0, R), ship), extra=[od])
+    exchange("ac", lambda b: half("CP", b, H), lambda b: C("CI", R + H * b, R + H * (b + 1)))
 
+    pieces, lists, w0, l0 = {}, {}, 0, 0
     vcopy(C("L7", 0, 105), A("SI"))
-    act(A("PK0"), IND(C("VV", 2 * R, 9 * R), C("L7", 0, 105)))
-    exchange("a0", lambda b: C("PK0", 7 * H * b, 7 * H * (b + 1)), lambda b: blk("VV", V0, b, -1, 6))
-    vts(C("CT", 0, R), A("CI"), MID, None, ALU.add, extra=[od])
-    for t in range(2):
-        vcopy(C("spotK", t, 56, 2), C("spotI", 28 * t, 28 * (t + 1)))
-    vtr(A("OT"), C("CT", 0, R))
+    act(A("PK0"), IND(C("VV", 2 * R, 10 * R), C("L7", 0, 105)))
+    exchange("a0", lambda b: half("PK0", b, 7 * H), lambda b: blk("VV", Z0, b, 0, 7))
+    for i, nw in enumerate(CFG["pieces"]):
+        if nw not in lists:
+            lists[nw], l0 = l0, l0 + 15 * nw + nw % 2
+            vts(C("LP", lists[nw], lists[nw] + 15 * nw), A("SI", ALL, slice(0, nw)), -2.0 * R, None, ALU.add)
+        pieces[w0 + nw - 1] = (i, w0, nw, lists[nw])
+        w0 += nw
+    act(A("CH"), C("CI", 0, R), ACT.Identity, bias=MID, extra=[od])
+    vtr(A("OT"), A("CH"))
     for ci in range(2):
         for gj in range(2):
             mm(bank(4, 112 * ci, 112), LL(ci, gj), A("OT", ALL, slice(16 * gj, 16 * gj + 16, 2)), gj == 0)
     for ci in range(2):
         for gj in range(2):
             mm(bank(5, 14 * ci, 14), LL(ci, gj), A("OT", ALL, 16 * gj + 1), gj == 0)
-    sp = A("spotI")
-    vts(A("s1"), sp, -471.5, 1.0 / H, ALU.add, ALU.mult)
-    vts(A("s4"), sp, 6 * R + BLK - H + 0.25, None, ALU.add)
+    for ci in range(2):
+        (act if CFG["cn"][0] == "S" else vcopy)(A("Cn", slice(ci, 28, 2)), bank(4, 112 * ci, 112))
+        (act if CFG["cn"][1] == "S" else vcopy)(C("C0", ci, 28, 2), bank(5, 14 * ci, 14))
+    c1, sp = A("Cn", slice(0, 28), 0), A("SP")
+    vtt(A("wm"), A("C0"), c1, ALU.is_gt)
+    vtt(A("wd"), half("spotI", 1, 28), half("spotI", 0, 28), ALU.subtract)
+    vtt(A("we"), A("wm"), A("wd"), ALU.mult)
+    vtt(half("SP", 0, 28), half("spotI", 1, 28), A("we"), ALU.subtract)
+    vtt(half("SP", 1, 28), half("spotI", 0, 28), A("we"), ALU.add)
+    for t in range(2):
+        vcopy(C("spotK", t, 56, 2), half("SP", t, 28))
+    if CFG["crep1"]:
+        vtt(c1, A("C0"), c1, ALU.max)
+        for w in range(6):
+            vcopy(A("Crep", slice(0, 28), ALL, w), A("Cn", slice(0, 28)))
+    else:
+        vtt(A("Cn", slice(28, 56), 0), A("C0"), c1, ALU.max)
+        vcopy(A("Cn", slice(28, 56), slice(1, 8)), A("Cn", slice(0, 28), slice(1, 8)))
+        for w in range(6):
+            (act if w < CFG["crepS"] else vcopy)(A("Crep", ALL, ALL, w), A("Cn"))
+    for t in range(2):
+        q = C("mk", 2 + t, 3 + t)
+        act(half("MS", t, 28), A("wm"), ACT.Identity, bias=q[0], scale=float(R if t else -R), extra=[q])
+    vtt(A("LS"), A("MS"), A("N16"), ALU.add)
+    act(A("AS"), IND(C("VV", 0, 2 * R), A("LS")))
+    act(A("s1"), sp, ACT.Identity, bias=-471.5 / H, scale=1.0 / H)
     vcopy(A("s2"), A("s1"))
-    vts(A("s6"), sp, float(R), 1.0 / H - 1.0 / R, ALU.is_lt, ALU.mult)
     vts(A("s8"), sp, float(R), float(R - H), ALU.is_lt, ALU.mult)
-    vts(A("s3"), A("s2"), -1.0, float(BLK - H), ALU.max, ALU.mult)
-    act(A("s7"), A("s6"), ACT.Identity, bias=-1.0 / H)
-    vtt(A("s5"), A("s3"), A("s4"), ALU.add)
-    for ci in range(2):
-        vcopy(A("Cn", slice(ci, 28, 2)), bank(4, 112 * ci, 112))
-    for ci in range(2):
-        vcopy(A("Cn", slice(28 + ci, 56, 2), 0), bank(5, 14 * ci, 14))
-    vcopy(A("Cn", slice(28, 56), slice(1, 8)), A("Cn", slice(0, 28), slice(1, 8)))
-    for w in range(6):
-        vcopy(A("Crep", ALL, ALL, w), A("Cn"))
-    vtt(C("nAB", 0, 56), A("s5"), A("s7"), ALU.mult)
-    act(C("nAB", 56, 112), C("nAB", 0, 56))
+    act(A("s3"), A("s2"), ACT.Relu, bias=float(BLK - H), scale=float(BLK - H))
+    act(A("s4"), A("s8"), ACT.Identity, bias=6 * R - BLK + H + 0.25, scale=-(6.0 * R - BLK + H) / (R - H))
+    act(A("s7"), A("s8"), ACT.Identity, bias=-1.0 / H, scale=(1.0 / H - 1.0 / R) / (R - H))
+    vtt(A("sa"), A("s3"), sp, ALU.add)
+    vtt(A("s5"), A("sa"), A("s4"), ALU.add)
+    vtt(A("nAB", ALL, 0), A("s5"), A("s7"), ALU.mult)
+    act(A("nAB", ALL, 1), A("nAB", ALL, 0))
     for k in range(2):
-        act(C("Brep", 56 * k, 56 * k + 56), A("s8"), ACT.Identity, bias=float(H))
-    mm(bank(0), A("nIb"), plane(0), True)
-    mm(bank(1), A("Ib"), plane(1), True)
+        act(A("Brep", ALL, k), A("s8"), ACT.Identity, bias=float(H))
+    mm(bank(0), A("nIb"), half("AS", 0), True)
+    mm(bank(1), A("Ib"), half("AS", 1), True)
 
-    ks = CFG["ksplit"]
-    act(C("GK", 0, 32 * ks), IND(A("CT"), C("spotK", 0, 2 * ks)))
-    vcopy(C("GKh", 32 * ks, 2 * R), IND(A("CT"), C("spotK", 2 * ks, 56)))
-    for c0, c1, h in ((0, ks, ""), (ks, 28, "h")):
-        vtr(A("GT" + h, slice(c0, c1)), C("GK" + h, 32 * c0, 32 * c1))
+    for c0, c2, who in CFG["turn"]:
+        o, i = C("GK", 32 * c0, 32 * c2), IND(A("CI"), C("spotK", 2 * c0, 2 * c2))
+        if who == "S":
+            act(o, i, ACT.Identity, bias=MID, extra=[od])
+        else:
+            vts(o, i, MID, None, ALU.add, extra=[od])
+    for c0, c2, who in CFG["turn"]:
+        vtr(A("GT", slice(c0, c2)), C("GK", 32 * c0, 32 * c2))
         for t in range(2):
             for gj in range(2):
-                mm(bank(2, 168 * t + 6 * c0, 6 * (c1 - c0)), LL(t, gj, "LL" + h),
-                   A("GT" + h, slice(c0, c1), slice(16 * gj + 4, 16 * gj + 16, 2)), gj == 0)
-    act(A("R1"), plane(2), ACT.Identity, bias=2.0, scale=-1.0)
-    act(A("s9"), A("s8"), ACT.Identity, bias=float(R - 7 * H), scale=-7.0)
+                mm(bank(2, 168 * t + 6 * c0, 6 * (c2 - c0)), LL(t, gj),
+                   A("GT", slice(c0, c2), slice(16 * gj + 4, 16 * gj + 16, 2)), gj == 0)
     for tab in ("T1", "T2"):
-        zero(C(tab, UPW, UPW + R + H), R + H)
+        zero(C(tab, 0, R))
+        zero(blk(tab, 0, 0, -1, 0))
         for b in range(NB):
-            n = H if b == NB - 1 else 2 * H
-            zero(blk(tab, 0, b, 6, 6 + n // H), n)
+            zero(blk(tab, 0, b, 6, 7 if b == NB - 1 else 8))
 
-    def join(chunks, banks):
-        for ch, wb in zip(chunks, banks):
-            s, n = ch[0], len(ch)
-            for x in ch:
-                vtt(C("EQ", 336 * x, 336 * (x + 1)), bank(2, 0, 336), A("Crep", ALL, x), ALU.is_equal)
-            o = bank(wb, 0, 56 * n)
-            mm(o, A("negI"), C("nAB", 0, 56 * n), True)
-            for w in range(6):
-                mm(o, C("Wt", 128 * w, 128 * (w + 1)), C("EQ", 336 * s + w, 336 * (s + n), 6), False)
-            oi = C("OI", 56 * s, 56 * (s + n))
-            vtt(oi, o, C("Brep", 0, 56 * n), ALU.mult)
-            vcopy(C("OFF", 56 * s, 56 * (s + n)), oi)
+    def compare(x):
+        ts = slice(0 if x else 1, 2)
+        if CFG["crep1"]:
+            for t in range(ts.start, 2):
+                vtt(A("EQ", t, slice(28 * x, 28 * x + 28)), bank(2, 168 * t, 168), A("Crep", slice(0, 28), x), ALU.is_equal)
+            return
+        vtt(A("EQ", ts, slice(28 * x, 28 * x + 28)), bank(2, 168 * ts.start, 336 - 168 * ts.start),
+            A("Crep", slice(28 * ts.start, 56), x), ALU.is_equal)
 
-    join(CFG["chunks"], [3, 6, 7, 3, 6])
-    pieces, w0, l0 = {}, 0, 0
-    for i, nw in enumerate(CFG["pieces"]):
-        pieces[w0 + nw - 1] = (i, w0, nw, l0)
-        w0, l0 = w0 + nw, l0 + 15 * nw + nw % 2
+    def address(ch, o):
+        s, n = ch[0], len(ch)
+        ts, cs = slice(0 if s else 1, 2), slice(28 * s, 28 * (s + n))
+        mm(o, A("negI"), A("nAB", ts, slice(0, n)), True)
+        for w in range(6):
+            mm(o, half("Wt", w, 128), A("EQ", ts, cs, w), False)
+        vtt(A("OFF", ts, cs), o, A("Brep", ts, slice(0, n)), ALU.mult)
 
-    def late_lists():
-        for i, w0, nw, l0 in pieces.values():
-            vcopy(C("LP", l0, l0 + 15 * nw), A("SI", ALL, slice(0, nw)))
-        vtt(A("s1"), A("s9"), A("s5"), ALU.add)
-        vcopy(A("spotD"), A("s1"))
-        vcopy(A("spotU"), sp)
+    for ch, wb in zip(CFG["chunks"], [3, 6, 7, 3, 6]):
+        for x in ch:
+            compare(x)
+        address(ch, bank(wb, 0, 56 * len(ch)))
+    act(A("s9"), A("s8"), ACT.Identity, bias=float(R + 7 * H), scale=-(R + 7.0 * H) / (R - H))
+    vtt(A("spotD"), A("s9"), A("s5"), ALU.add)
+    vcopy(A("spotU"), A("spotI"))
 
-    cu, cp, cb = [0], [0], {}
-    later = {}
+    def second_x():
+        vtt(half("XS2", 1), bank(1), half("RK1", 1), ALU.mult)
+
+    def last_lists():
+        vtt(half("OFL", 0, 28), A("OFF", 1, slice(0, 28)), A("wm"), ALU.mult)
+        vtt(half("OFL", 1, 28), A("OFF", 1, slice(0, 28)), half("OFL", 0, 28), ALU.subtract)
+
+    def first_r(t):
+        act(half("RK1", t), IND(C("VV", 2 * R, Z0 + TW), half("spotD", t, 28)), ACT.Identity, bias=2.0, scale=-1.0)
+    fill = {"rk0": lambda: first_r(0), "rk1": lambda: first_r(1), "x2": second_x, "lists": last_lists,
+            "sq": lambda: act(A("SQ"), plane(2), ACT.Square, bias=2.0, scale=-1.0),
+            "posI": lambda: act(A("posI"), A("negI"), scale=-1.0), "n2I": lambda: act(A("n2I"), A("negI"), scale=2.0)}
+    for name in CFG["fill"][0]:
+        fill[name]()
+
+    cu, cp = [0], [0]
 
     def sweep(k):
         order = [2, 3, 4, 5, 6, 7] if k < 2 else CFG["order3"]
         modes = dict(zip(order, CFG["modes"][k]))
         if k < 2:
-            modes[0], modes[1] = "AD", CFG["diag"][k]
-        win = [C("VV", V0, V0 + TW), A("T1"), A("T2")][k]
-        xs = ["VV", "XS1", "XS2"][k]
-        nx0 = bank([0, 1, 0][k])
+            modes[0], modes[1] = "-D", CFG["diag"][k]
+        win = [C("VV", Z0, Z0 + TW), A("T1"), A("T2")][k]
+        xs = [(half("AS", 0), half("AS", 1)), (A("X1"), half("AS", 1)), (half("XS2", 0), half("XS2", 1))][k]
+        nx0 = bank([0, 2, 0][k])
         out_tab, pk = [("T1", "PK1"), ("T2", "PK2"), (None, None)][k]
-        ub, pb, ab = {}, {}, {}
+        ub, pb, ab, banks = {}, {}, {}, list(CFG["banks"][k])
 
-        def off(s, a, b):
-            return C("OFF", 56 * s + 28 * a, 56 * s + 28 * b)
-
-        def newbank():
-            b = min(CFG["banks"][k], key=lambda b: cb.get(b, -1))
-            cb[b] = len(ops)
-            return b
+        def off(s, t, n=1):
+            if s == 0 and k == 2:
+                return C("OFL", 28 * t, 28 * (t + n))
+            return A("OFF", t, slice(28 * s, 28 * (s + n)))
 
         def gather(s):
-            ts = [t for t in range(2) if modes[s][t] == "A"]
-            if ts and s not in ub:
-                ub[s] = "U%d" % (cu[0] % NU)
-                cu[0] += 1
-                act(C(ub[s], R * ts[0], R * (ts[-1] + 1)), IND(win, off(s, ts[0], ts[-1] + 1)))
+            for t in range(2):
+                if modes[s][t] == "A" and (s, t) not in ub:
+                    n = 2 if s in CFG["gp"][k] and modes[s + 1][t] == "A" else 1
+                    u = "U%d" % (cu[0] % NU)
+                    cu[0] += 1
+                    act(C(u, 0, R * n), IND(win, off(s, t, n)))
+                    for i in range(n):
+                        ub[s + i, t] = half(u, i)
 
-        def product(s, t):
-            if s not in pb:
-                pb[s] = "P%d" % (cp[0] % NP)
-                cp[0] += 1
-            o = C(pb[s], R * t, R * (t + 1))
+        def product(s, t, x):
+            pb[s, t] = A("P%d" % (cp[0] % NP))
+            cp[0] += 1
             if modes[s][t] == "A":
-                vtt(o, C(ub[s], R * t, R * (t + 1)), bank([1, 2, 1][k]), ALU.mult)
+                vtt(pb[s, t], ub[s, t], bank(1), ALU.mult)
             else:
-                vtt(o, IND(win, off(s, t, t + 1)), C(xs, R * t, R * (t + 1)), ALU.mult)
-            return o
+                vtt(pb[s, t], IND(win, off(s, t)), xs[x], ALU.mult)
+            return pb[s, t]
 
-        def first(s, b, a):
+        def products(s, b):
+            ab[s], a = b, plane(s + 1)
+            mm(bank(b), A("Ib"), a, True)
             if modes[s][0] == "A":
-                mm(bank(b), A("Ib"), a, True)
-                vtt(bank(b), C(ub[s], 0, R), nx0, ALU.mult)
+                vtt(bank(b), ub[s, 0], nx0, ALU.mult)
                 mm(bank(b), A("Ib"), a, False)
             else:
-                p = product(s, 0)
-                mm(bank(b), A("Ib"), a, True, True)
+                mm(bank(b), A("negI"), product(s, 0, 0), False)
+            p = product(s, 1, 1)
+            if modes[s][2:] != "V":
                 mm(bank(b), A("negI"), p, False)
 
-        def products(s, b=None, second_first=False):
-            ab[s] = b or newbank()
-            if second_first:
-                p = product(s, 1)
-            first(s, ab[s], plane(s + 1))
-            if not second_first:
-                p = product(s, 1)
-            if modes[s][2:] != "V":
-                mm(bank(ab[s]), A("negI"), p, False)
-
-        def finish(s, halves=False):
-            parts = [(0, R // 2, "scalar"), (R // 2, R // 2, "sync")] if halves else [(0, R, "sync")]
+        def finish(s):
+            if s in CFG["fp"][k]:
+                return
+            s0 = s - 1 if s - 1 in CFG["fp"][k] else s
+            parts = [(0, R // 2, "scalar"), (R // 2, R // 2, "sync")] if k == 2 and s == order[-1] else [(0, R * (s - s0 + 1), "sync")]
             for a, n, q in parts:
-                z = R * (s - 2) + a if k < 2 else R * (s + 1) + a
+                z = R * (s0 - 1) + a if k < 2 else R * (s0 + 1) + a
                 o = C(out_tab or "YY", z, z + n)
                 if modes[s][2] == "V":
-                    vtt(o, bank(ab[s], a, n), C(pb[s], R + a, R + a + n), ALU.subtract)
+                    vtt(o, bank(ab[s], a, n), C(pb[s, 1][1], a, a + n), ALU.subtract)
+                elif s0 < s:
+                    act(o, A("PS", slice(ab[s0], ab[s] + 1), slice(0, R)))
                 else:
                     act(o, bank(ab[s], a, n))
                 if k == 2:
                     store(q, T.y[:, z:z + n], o)
-
-        def lower():
-            p = product(0, 1)
-            b0 = 1 if k == 0 else newbank()
-            mm(bank(b0), A("Ib" if k == 2 else "nIb"), plane(0), True, True)
-            mm(bank(b0), A("negI" if k == 2 else "posI"), p, False)
-            b1 = 2 if k == 0 else newbank()
-            first(0, b1, plane(1))
-            if k == 0:
-                act(C("XS1", R, 2 * R), bank(b1))
-                if any(m[0] == "D" for m in CFG["modes"][1] + CFG["diag"][1:]):
-                    act(C("XS1", 0, R), bank(1), scale=-1.0)
-            elif k == 1:
-                vtt(C("XS2", R, 2 * R), bank(b1), C("RK1", R, 2 * R), ALU.mult)
-                vtt(bank(0), bank(b0), C("RK1", 0, R), ALU.mult)
-                if any(m[0] == "D" for m in CFG["modes"][2]):
-                    act(C("XS2", 0, R), bank(0), scale=-1.0)
-                if any(m[1] == "A" for m in CFG["modes"][2]):
-                    later.setdefault((2, -1), []).append(lambda: act(bank(1), C("XS2", R, 2 * R)))
-            else:
-                for t, b in ((1, b1), (0, b0)):
-                    o = C("YY", R * t, R * (t + 1))
-                    vtt(o, bank(b), C("RK2", R * t, R * (t + 1)), ALU.mult)
-                    store("sync", T.y[:, R * t:R * (t + 1)], o)
-
-        def send(w):
-            if w in pieces:
-                i, w0, nw, l0 = pieces[w]
+            for i, w0, nw, l0 in [pieces[x - 2] for x in range(s0, s + 1) if k < 2 and x - 2 in pieces]:
                 n, z = H * nw, NB * H * w0
                 cut = CFG["cut"][k][i]
                 for fn, b0, b1 in ((vcopy, 0, cut), (act, cut, NB)):
                     if b0 < b1:
-                        fn(C(pk, z + b0 * n, z + b1 * n), IND(C(out_tab, R * w0, R * (w0 + nw)), C("LP", l0 + 3 * nw * b0, l0 + 3 * nw * b1)))
+                        fn(C(pk, z + b0 * n, z + b1 * n),
+                           IND(C(out_tab, R * (w0 + 1), R * (w0 + nw + 1)), C("LP", l0 + 3 * nw * b0, l0 + 3 * nw * b1)))
                 exchange("a%d%d" % (k + 1, i), lambda b: C(pk, z + n * b, z + n * (b + 1)), lambda b: blk(out_tab, 0, b, w0, w0 + nw))
 
-        def done(s, halves=False):
-            if s:
-                finish(s, halves)
-                if k < 2:
-                    send(s - 2)
+        def last_lower():
+            for t in range(2):
+                b, o = bank(banks.pop(0)), half("YY", t)
+                mm(b, A("Ib"), plane(t), True)
+                if modes[0][t] == "A":
+                    vtt(b, ub[0, t], bank(1), ALU.mult)
+                    mm(b, A("nIb"), plane(t), False)
+                else:
+                    mm(b, A("negI"), product(0, t, 1), False)
+                vtt(o, b, half("RK2", t), ALU.mult)
+                store("sync", T.y[:, R * t:R * (t + 1)], o)
 
-        lag = CFG["lag"][k]
         for i, s in enumerate(order):
-            for x in order[i:i + 1 + CFG["ahead"][k]]:
+            for x in order[i:i + 1 + CFG["ahead"]]:
                 gather(x)
-            for fn in later.pop((k, i), []):
-                fn()
             if s == 0:
-                lower()
+                last_lower()
             else:
-                products(s, second_first=(i == 0 and k > 0))
-            if i == 0 and k == 0:
-                late_lists()
-            if k == 0 and i == CFG["joinat"]:
-                join(CFG["chunks2"], [3, 3])
-            if i >= lag:
-                done(order[i - lag])
-        for s in order[len(order) - lag:]:
-            done(s, halves=(k == 2 and s == order[-1]))
+                products(s, banks.pop(0))
+            behind_v = max(j for j, o in enumerate(ops) if o["q"] == "vector")
+            if i and order[i - 1]:
+                finish(order[i - 1])
+        finish(order[-1])
         if k == 2:
             return
 
-        def at(key, fn):
-            if CFG[key] < 0:
-                fn()
-            else:
-                later.setdefault((k + 1, CFG[key]), []).append(fn)
-
-        if k == 0 and CFG["joinat"] > 5:
-            join(CFG["chunks2"], [3, 3])
-        gather(0)
+        if CFG["hold"]:
+            hold.update(vector=behind_v, scalar=max(j for j, o in enumerate(ops) if o["q"] == "scalar"))
+        if k == 0:
+            compare(0)
+            compare(1)
+            address([0], bank(2, 392, 28))
+            address([1], bank(2, 336, 56))
+        for name in CFG["fill"][k + 1]:
+            fill[name]()
         gather(1)
-        lower()
+        b0 = bank(2 if k == 0 else banks.pop(0))
+        mm(b0, A("nIb"), half("AS", 0), True)
+        mm(b0, A("posI"), product(0, 1, 1), False)
+        if k == 1:
+            vtt(bank(0), b0, half("RK1", 0), ALU.mult)
+        if any(m[0] == "D" for m in CFG["modes"][k + 1][:4] + CFG["modes"][k + 1][5:] + CFG["modes"][1][4:5] + CFG["diag"][k + 1:]):
+            act(A("X1") if k == 0 else half("XS2", 0), bank(2 if k == 0 else 0), scale=-1.0)
         products(1, 3)
-        for fn in later.pop((k + 1, -1), []):
-            fn()
+        if k == 1 and (any(m[1] == "A" for m in CFG["modes"][2]) or "A" in CFG["modes"][2][4]):
+            act(bank(1), half("XS2", 1))
+        e, rn = bank(CFG["rsq"][k]), (half("RT2", 0) if k == 0 else A("R3"))
+        mm(e, A("Ib"), plane(2), True)
+        vtt(e, bank(3), A("SQ"), ALU.mult)
         if k == 0:
-            for t in range(2):
-                act(C("RK1", R * t, R * (t + 1)), IND(C("VV", 2 * R, V0 + TW), C("spotD", 28 * t, 28 * t + 28)), ACT.Identity, bias=2.0, scale=-1.0)
-        d = bank(3)
-        r, rn = (A("R1"), C("RT2", 0, R)) if k == 0 else (C("RT2", 0, R), A("R3"))
-
-        def rstep():
-            if CFG["rsq"][k]:
-                e = bank(CFG["rsq"][k])
-                act(A("SQ"), r, ACT.Square)
-                mm(e, A("Ib"), plane(2), True)
-                vtt(e, d, A("SQ"), ALU.mult)
-                if k == 0:
-                    mm(e, A("Ib"), plane(2), False)
-                    mm(e, A("Ib"), plane(2), False)
-                    act(rn, e, ACT.Identity, bias=4.0, scale=-1.0)
-                else:
-                    mm(e, A("n2I"), r, False)
-                    act(rn, e, scale=-1.0)
-            else:
-                vtt(d, d, r, ALU.mult)
-                act(d, d, ACT.Identity, bias=2.0, scale=-1.0)
-                vtt(rn, d, r, ALU.mult)
-            if k == 1:
-                store("sync", T.inv[:], rn)
-
-        def send_r():
+            mm(e, A("Ib"), plane(2), False)
+            mm(e, A("Ib"), plane(2), False)
+            act(rn, e, ACT.Identity, bias=4.0, scale=-1.0)
             act(A("PR2"), IND(rn, ship))
-            exchange("ar2", lambda b: C("PR2", H * b, H * (b + 1)), lambda b: C("RT2", R + H * b, R + H * (b + 1)))
-
-        if k == 0:
-            at("r2at", rstep)
-            at("pr2at", send_r)
+            exchange("ar2", lambda b: half("PR2", b, H), lambda b: C("RT2", R + H * b, R + H * (b + 1)))
+            act(A("SQ"), rn, ACT.Square)
         else:
-            at("rk2at", lambda: act(A("RK2"), IND(A("RT2"), A("spotU"))))
-            at("r3at", rstep)
+            mm(e, A("n2I"), half("RT2", 0), False)
+            act(rn, e, scale=-1.0)
+            store("sync", T.inv[:], rn)
+            sign = [-1.0 if c == "A" else 1.0 for c in CFG["modes"][2][4]]
+            for t0, t1 in ([(0, 2)] if sign[0] == sign[1] else [(0, 1), (1, 2)]):
+                act(C("RK2", R * t0, R * t1), IND(A("RT2"), C("spotU", 28 * t0, 28 * t1)), scale=sign[t0])
+        hold.clear()
 
     for k in range(3):
         sweep(k)
@@ -626,6 +693,8 @@ def rank_program(g, core, T, topo):
                         f.add(i)
                 elif o["q"] != "arrive" and ((b1 & b2 and q1 != o["q"]) or ((w1 or w2) and m1 & m2)):
                     d.add(i)
+        if o["hold"] is not None and o["hold"] not in d:
+            f.add(o["hold"])
         if o["q"] == "arrive":
             f.update((j - 2, j - 1))
         elif o["sem"] not in (None, "stored") or o["q"] == "pool":
@@ -639,14 +708,13 @@ def rank_program(g, core, T, topo):
         behind.append(sorted(f))
     if not ORDER:
         ORDER.extend(issue_order(ops, deps, behind))
-    order = ORDER
-    place = {j: p for p, j in enumerate(order)}
+    place = {j: p for p, j in enumerate(ORDER)}
     needed = set()
     for j, o in enumerate(ops):
         o["latest"] = {ops[i]["q"]: i for i in sorted(deps[j], key=place.get) if ops[i]["sem"] is None}
         needed.update(o["latest"].values())
     cnt = {"vector": 0, "scalar": 0, "tensor": 0, "pool": 0}
-    for j in order:
+    for j in ORDER:
         o = ops[j]
         if o["sem"] is not None:
             o["tok"] = (o["sem"], o["n"])
@@ -655,7 +723,7 @@ def rank_program(g, core, T, topo):
             o["tok"] = (o["q"], cnt[o["q"]])
     queue = {"vector": g.vector, "scalar": g.scalar, "tensor": g.tensor, "pool": g, "sync": g.sync}
     seen = {q: {} for q in queue}
-    for j in order:
+    for j in ORDER:
         o = ops[j]
         if o["q"] == "arrive":
             continue

@@ -10,21 +10,21 @@ MID = -1344.0
 NU, NP = 8, 8
 
 CFG = {
-    "modes": [["AAS", "AAS", "ADS", "ADS", "ADS", "ADV"],
+    "modes": [["ADS", "ADS", "ADV", "ADS", "ADS", "ADV"],
               ["ADS", "ADS", "ADV", "ADS", "ADS", "ADV"],
-              ["ADS", "ADS", "ADS", "ADS", "AA", "ADS", "ADS", "ADV"]],
+              ["ADS", "ADS", "AAV", "ADS", "AA", "ADS", "AAV", "ADV"]],
     "order3": [2, 3, 4, 5, 0, 1, 6, 7],
-    "diag": ["AD", "AD"], "cn": "VV", "crep1": False, "crepS": 0, "siS": 5, "hold": True,
+    "low": "DD", "r3": "pe", "diag": ["AD", "AD"], "cn": "VV", "gs": "S", "abank": [2, 4, 2, 2], "x2pe": False, "onV": ["MS", "s1", "s4", "s7", "nAB", "B", "s9"], "siS": 3, "chain": True, "cut0": 0, "u16S": False, "addlag": 4.0, "addwire": 0.8, "rep": "pe", "slowval": 1.0, "rlag": 0.65, "wt": 2, "wt2": 5, "hold": False,
     "fill": [["posI"], ["sq", "rk1"], ["rk0", "x2", "lists", "n2I"]], "ahead": 2,
-    "gp": [[2, 4, 6], [3, 5], [3, 6]], "fp": [[2], [2], [2]],
+    "gp": [[2, 4, 6], [2, 4, 6], [0, 2, 4, 6]], "fp": [[2], [2], [2]],
     "pieces": [2, 2, 2],
     "cut": [[0, 0, 2], [0, 0, 2]],
-    "chunks": [[2], [3], [4, 5], [6, 7]], "turn": [(0, 8, "V"), (8, 18, "S"), (18, 28, "S")],
-    "banks": [[4, 5, 6, 7, 3, 4], [4, 5, 6, 7, 0, 4, 5], [4, 5, 6, 7, 2, 3, 4, 5, 6]], "rsq": [0, 6],
+    "chunks": [[2], [3], [4, 5], [6, 7]], "turn": [(0, 12, "V"), (12, 20, "S"), (20, 28, "S")],
+    "banks": [[4, 5, 3, 6, 7, 4], [4, 5, 0, 6, 7, 4, 5], [4, 5, 6, 7, 2, 3, 4, 5, 6]], "rsq": [0, 6],
     "first": 2.3, "rows": 0.75, "perword": 0.006, "store": 0.5,
-    "cases": [(1.5, 1.0, 1.0, 0.08), (1.15, 1.2, 0.9, 0.05), (1.95, 0.8, 1.1, 0.12), (1.4, 0.75, 1.15, 0.1)], "seed": 2, "rounds": 300, "swaps": 5000, "heat": 0.2, "nudge": 3, "give": 0.05, "sigma": 1.0, "big": 0.12,
+    "cases": [(1.35, 0.8, 1.1, 0.08), (1.1, 0.85, 1.1, 0.07), (1.9, 0.7, 1.03, 0.08), (1.3, 0.75, 1.6, 0.08), (1.5, 1.2, 1.1, 0.08), (1.3, 0.6, 1.0, 0.06)], "seed": 7, "rounds": 300, "swaps": 55000, "heat": 0.15, "land": 0.03, "pefix": 0.02, "nudge": 3, "give": 0.05, "sigma": 1.0, "big": 0.12,
 }
-FIXED = {"vector": 0.05, "scalar": 0.09, "tensor": 0.03, "pool": 0.13}
+FIXED = {"vector": 0.058, "scalar": 0.12, "tensor": 0.03, "pool": 0.13}
 CYCLE = {"vector": 0.00083, "scalar": 0.00083, "tensor": 0.000417, "pool": 0.00083}
 
 SCRATCH = {
@@ -34,18 +34,20 @@ SCRATCH = {
     "spotK": ("sbuf", [128, 56], "uint16"), "spotU": ("sbuf", [128, 56], "uint16"), "spotD": ("sbuf", [128, 56], "uint16"),
     "LS": ("sbuf", [128, 56], "uint16"), "OFL": ("sbuf", [128, 56], "uint16"),
     "GK": ("sbuf", [128, 896], "float16"), "GT": ("sbuf", [128, 28, 32], "float16"), "OT": ("sbuf", [128, 14, 32], "float16"),
-    "C0": ("sbuf", [128, 28], "float16"), "Cn": ("sbuf", [128, 56, 8], "float16"), "Crep": ("sbuf", [128, 56, 8, 6], "float16"),
+    "C0": ("sbuf", [128, 28], "float16"), "Cn": ("sbuf", [128, 56, 8], "float16"), "GS": ("sbuf", [128, 336], "float16"),
+    "Ih": ("sbuf", [128, 128], "float16"), "Crep": ("sbuf", [128, 56, 8, 6], "float16"),
     "EQ": ("sbuf", [128, 2, 224, 6], "bfloat16"), "OFF": ("sbuf", [128, 2, 224], "uint16"),
     "DD": ("sbuf", [128, 128], "float32"), "pI": ("sbuf", [128, 4], "int32"), "cI": ("sbuf", [128, 4], "int32"),
     "mk": ("sbuf", [128, 4], "float32"), "LL": ("sbuf", [128, 512], "float16"), "N16": ("sbuf", [128, 56], "float32"),
     "negI": ("sbuf", [128, 128], "float32"), "posI": ("sbuf", [128, 128], "float32"), "n2I": ("sbuf", [128, 128], "float32"),
-    "Ib": ("sbuf", [128, 128], "bfloat16"), "nIb": ("sbuf", [128, 128], "bfloat16"), "Wt": ("sbuf", [128, 768], "bfloat16"),
+    "diagI": ("sbuf", [128, 128], "float32"), "ownI": ("sbuf", [128, 128], "float32"), "nIb": ("sbuf", [128, 128], "bfloat16"), "Wt": ("sbuf", [128, 768], "bfloat16"),
     "nAB": ("sbuf", [128, 2, 2, 28], "float32"), "Brep": ("sbuf", [128, 2, 2, 28], "float32"),
     "VV": ("sbuf", [128, Z0 + TW], "bfloat16"), "T1": ("sbuf", [128, TW], "float32"), "T2": ("sbuf", [128, TW], "float32"),
     "AS": ("sbuf", [128, 896], "bfloat16"),
     "PK0": ("sbuf", [128, NB * 7 * H], "bfloat16"), "PK1": ("sbuf", [128, NB * 6 * H], "float32"), "PK2": ("sbuf", [128, NB * 6 * H], "float32"),
     "SI": ("sbuf", [128, NB, 7, 3], "float32"), "L7": ("sbuf", [128, 106], "uint16"), "LP": ("sbuf", [128, 142], "uint16"),
-    "SQ": ("sbuf", [128, R], "float32"), "RT2": ("sbuf", [128, R + NB * H], "float32"), "PR2": ("sbuf", [128, NB * H], "float32"),
+    "SQ": ("sbuf", [128, R], "float32"), "SQ2": ("sbuf", [128, R], "float32"),
+    "RT2": ("sbuf", [128, R + NB * H], "float32"), "PR2": ("sbuf", [128, NB * H], "float32"),
     "RK1": ("sbuf", [128, 896], "float32"), "RK2": ("sbuf", [128, 896], "float32"), "R3": ("sbuf", [128, R], "float32"),
     "X1": ("sbuf", [128, R], "float32"), "XS2": ("sbuf", [128, 896], "float32"),
     "YY": ("sbuf", [128, 9 * R], "float32"),
@@ -62,8 +64,10 @@ for _i in range(NP):
     SCRATCH["P%d" % _i] = ("sbuf", [128, R], "float32")
 
 LOADS = ["lc0", "lc1", "lship", "lspot", "lv0", "lv1", "lv2", "lv3"]
-ARRIVALS = ["ac", "a0", "a10", "a11", "a12", "ar2", "a20", "a21", "a22"]
-SEMAPHORES = ["vector", "scalar", "tensor", "pool", "sent", "stored"] + LOADS + ARRIVALS
+ARRIVALS = ["ac", "a0", "ar2"] + ["a%d%d" % (k, i) for k in (1, 2) for i in range(6)]
+for _n in ("00", "01", "10", "11"):
+    SCRATCH["Q" + _n] = ("sbuf", [128, 896], "float32")
+SEMAPHORES = ["pre", "add00", "add01", "add10", "add11", "vector", "scalar", "tensor", "pool", "sent", "stored"] + LOADS + ARRIVALS
 
 ALU = AluOpType
 ACT = ActivationFunctionType
@@ -179,63 +183,69 @@ def issue_order(ops, deps, behind):
 
     queue = [o["q"] for o in ops]
 
-    def clock(seq):
-        prev, nxt = {}, {}
-        for s in seq.values():
-            prev.update(zip(s[1:], s))
-            nxt.update(zip(s, s[1:]))
-        left = [len(before[j]) + (j in prev) for j in every]
-        order = [j for j in every if not left[j]]
+    waits = [[[(i, lag[i] if w else 0.0) for i, w in before[j]] for j in every] for cost, lag in cases]
+    sinks = [j for j in every if not after[j]]
+    lands = [j for j in every if queue[j] == "arrive"]
+    links = ([{i for i, _ in x} for x in before], [{i for i, _ in x} for x in after])
+
+    def clock(order, old, p0):
+        prev, last = {}, {}
         for j in order:
-            for i in [i for i, _ in after[j]] + ([nxt[j]] if j in nxt else []):
-                left[i] -= 1
-                if not left[i]:
-                    order.append(i)
-        if len(order) < len(ops):
-            return None
-        total, ends = 0.0, []
-        for cost, lag in cases:
-            end = [0.0] * len(ops)
-            for j in order:
-                t = end[prev[j]] if j in prev else 0.0
-                for i, w in before[j]:
-                    x = end[i] + lag[i] if w else end[i]
+            prev[j], last[queue[j]] = last.get(queue[j]), j
+        total, ends, rest = 0.0, [], [(j, prev[j]) for j in order[p0:]]
+        for c, (cost, lag) in enumerate(cases):
+            end, wait = list(old[c]), waits[c]
+            for j, p in rest:
+                t = 0.0 if p is None else end[p]
+                for i, x in wait[j]:
+                    x += end[i]
                     if x > t:
                         t = x
                 end[j] = t + cost[j]
-            total += max(end[j] + lag[j] for j in every)
+            total += max(end[j] + lag[j] for j in sinks) + CFG["land"] * sum(end[j] for j in lands)
             ends.append(end)
         return total, order, ends, prev
 
-    seq = {q: [j for j in best[2] if queue[j] == q] for q in set(queue)}
-    best = cur = clock(seq)
+    def shift(part, link):
+        v, moved, flagged = part[-1], {part[-1]}, set()
+        for x in reversed(part[:-1]):
+            if queue[x] in flagged or link[x] & moved:
+                if queue[x] == queue[v]:
+                    return None
+                moved.add(x)
+                flagged.add(queue[x])
+        return [x for x in part if x in moved] + [x for x in part if x not in moved]
+
+    best = cur = clock(best[2], [[0.0] * len(ops)] * len(cases), 0)
     for it in range(CFG["swaps"]):
         c = int(rng.integers(len(cases)))
-        (cost, lag), end, prev, arcs = cases[c], cur[2][c], cur[3], []
-        j = max(every, key=lambda j: end[j] + lag[j])
-        while True:
-            t = end[j] - cost[j]
-            if j in prev and end[prev[j]] > t - 1e-9:
+        (cost, lag), order, end, prev, arcs = cases[c], cur[1], cur[2][c], cur[3], []
+        j = max(sinks, key=lambda j: end[j] + lag[j]) if rng.random() < 0.7 else lands[int(rng.integers(len(lands)))]
+        while j is not None:
+            t = end[j] - cost[j] - 1e-9
+            if prev[j] is not None and end[prev[j]] > t:
                 arcs.append(j)
                 j = prev[j]
-                continue
-            j = next((i for i, w in before[j] if end[i] + (lag[i] if w else 0.0) > t - 1e-9), None)
-            if j is None:
-                break
+            else:
+                j = next((i for i, x in waits[c][j] if end[i] + x > t), None)
+        if not arcs:
+            continue
         v = arcs[int(rng.integers(len(arcs)))]
-        s = list(seq[queue[v]])
-        p, far = s.index(v), int(rng.integers(1, 4))
+        mates, far = [j for j in order if queue[j] == queue[v]], int(rng.integers(1, 5))
+        p = mates.index(v)
         if rng.random() < 0.5:
-            s.insert(max(p - far, 0), s.pop(p))
+            a, b = order.index(mates[max(p - far, 0)]), order.index(v) + 1
+            part = shift(order[a:b], links[1])
         else:
-            s.insert(p - 1 + far, s.pop(p - 1))
-        trial = dict(seq)
-        trial[queue[v]] = s
-        new = clock(trial)
-        if new and new[0] < cur[0] - CFG["heat"] * (1.0 - it / CFG["swaps"]) * float(np.log(rng.random())):
-            cur, seq = new, trial
-            if new[0] < best[0]:
-                best = new
+            a, b = order.index(mates[p - 1]), order.index(mates[min(p - 1 + far, len(mates) - 1)]) + 1
+            part = shift(order[a:b][::-1], links[0])
+            part = part and part[::-1]
+        if part:
+            new = clock(order[:a] + part + order[b:], cur[2], a)
+            if new[0] < cur[0] - CFG["heat"] * (1.0 - it / CFG["swaps"]) * float(np.log(rng.random())):
+                cur = new
+                if new[0] < best[0]:
+                    best = new
     return best[1]
 
 
@@ -247,6 +257,7 @@ def rank_program(g, core, T, topo):
     peers = [c for c in cores if c != core]
     ops = []
 
+    chain = {}
     hold = {}
 
     def A(name, *idx):
@@ -271,9 +282,11 @@ def rank_program(g, core, T, topo):
             else:
                 if rate is None:
                     rate = 0.5 if q == "vector" and all(SCRATCH[x[1]][2].endswith("16") for x in rd[:1] + writes) else 1.0
-                cost = FIXED[q] + max(64, n * rate) * CYCLE[q]
+                cost = CFG.get(q, FIXED[q]) + max(64, n * rate) * CYCLE[q]
         ops.append({"q": q, "fn": fn, "r": [(x[1], x[2]) for x in rd], "w": [(x[1], x[2]) for x in writes], "sem": sem, "n": count,
                     "cost": cost, "gathered": gathered, "lag": lag, "hold": hold.get(q)})
+        if chain.get(q):
+            hold[q] = len(ops) - 1
 
     def vcopy(o, i, extra=()):
         op("vector", lambda: g.vector.tensor_copy(o[0], i[0]), [i] + list(extra), [o])
@@ -298,8 +311,8 @@ def rank_program(g, core, T, topo):
             kw["scale"] = scale
         op("scalar", lambda: g.scalar.activation(o[0], i[0], f, **kw), [i] + list(extra), [o])
 
-    def iota(z, pattern, per_partition=0):
-        op("pool", lambda: g.iota(z[0], pattern, 0, per_partition, allow_small_or_imprecise_dtypes=True), [], [z], rate=2.0)
+    def iota(z, pattern, per_partition=0, base=0):
+        op("pool", lambda: g.iota(z[0], pattern, base, per_partition, allow_small_or_imprecise_dtypes=True), [], [z], rate=2.0)
 
     def zero(z):
         iota(z, [[0, z[2].bit_count()]])
@@ -314,7 +327,7 @@ def rank_program(g, core, T, topo):
         groups[b].append(me)
         op("tensor", lambda: g.tensor.matmul(o[0], l[0], r[0], me["start"], me["stop"]), [l, r], [o],
            rate=4.0 if SCRATCH[l[1]][2] == "float32" else 1.0,
-           cost=FIXED["tensor"] + max(64, o[2].bit_count()) * CYCLE["tensor"] * (4 if SCRATCH[l[1]][2] == "float32" else 1))
+           cost=CFG["pefix"] + max(64, o[2].bit_count()) * CYCLE["tensor"] * (4 if SCRATCH[l[1]][2] == "float32" else 1))
 
     def load(q, sem, o, src, lag):
         eng = g.sync if q == "sync" else g.scalar
@@ -351,13 +364,13 @@ def rank_program(g, core, T, topo):
             nsent[0] += n
         once = 0.0 if nsent[0] > 16 else CFG["first"]
         wire = CFG["rows"] + rd[0][2].bit_count() * CFG["perword"] * (0.5 if SCRATCH[rd[0][1]][2] == "bfloat16" else 1.0)
-        op("pool", lambda: g.remote_dma_fused(trs, local_sem=T.sem["sent"]), rd, [], sem="remote", cost=0.35 + once, lag=0.5)
+        op("pool", lambda: g.remote_dma_fused(trs, local_sem=T.sem["sent"]), rd, [], sem="remote", cost=0.35 + once, lag=CFG["rlag"])
         p, m, n = last
         b, bb = slot(p)
         rid, pid, _ = topo.addr(p)
         s, d = src_of(b), dst_of(bb)
         nsent[0] += n
-        op("pool", lambda: g.remote_dma(d[0], s[0], T.sem[sem], T.sem["sent"], pid, rid, m), [s], [], sem="remote", cost=0.35, lag=0.1)
+        op("pool", lambda: g.remote_dma(d[0], s[0], T.sem[sem], T.sem["sent"], pid, rid, m), [s], [], sem="remote", cost=0.35, lag=CFG["rlag"] - 0.4)
         op("arrive", None, [], [dst_of(k) for k in range(NB)], sem=sem, count=inbound, cost=wire, lag=0.25)
 
     def blk(tab, base, b, w0, w1):
@@ -382,23 +395,20 @@ def rank_program(g, core, T, topo):
     load("scalar", "lc1", od, T.col[:, 0:8 * R], 1.9)
     load("sync", "lc0", ev, T.col[:, R:9 * R], 2.1)
     load("sync", "lspot", A("spotI"), T.spot[:], 2.2)
-    load("sync", "lv0", C("VV", 4 * R, 7 * R), T.val[:, 3 * R:6 * R], 2.9)
-    load("sync", "lv1", plane(2), T.val[:, 2 * R:3 * R], 3.2)
-    load("sync", "lv2", C("VV", 7 * R, 10 * R), T.val[:, 6 * R:9 * R], 3.9)
-    load("sync", "lv3", C("VV", 0, 2 * R), T.val[:, 0:2 * R], 4.4)
+    load("sync", "lv0", C("VV", 4 * R, 7 * R), T.val[:, 3 * R:6 * R], 2.9 * CFG["slowval"])
+    load("sync", "lv1", plane(2), T.val[:, 2 * R:3 * R], 3.2 * CFG["slowval"])
+    load("sync", "lv2", C("VV", 7 * R, 10 * R), T.val[:, 6 * R:9 * R], 3.9 * CFG["slowval"])
+    load("sync", "lv3", C("VV", 0, 2 * R), T.val[:, 0:2 * R], 4.4 * CFG["slowval"])
 
-    op("pool", lambda: g.iota(T.pI[:, 0:1], [[0, 1]], 0, 1), [], [C("pI", 0, 1)], cost=0.13)
     iota(A("DD"), [[1, 128]], -1)
-    iota(A("N16"), [[0, 2], [16, 28]])
+    op("pool", lambda: g.iota(T.pI[:, 0:1], [[0, 1]], 0, 1), [], [C("pI", 0, 1)], cost=0.13)
+    iota(A("N16"), [[-R, 2], [16, 28]], base=R)
     zero(C("VV", Z0, Z0 + R))
-    for b in range(NB):
-        zero(blk("VV", Z0, b, -1, 0))
     vts(C("cI", 0, 1), C("pI", 0, 1), 4, 1, ALU.arith_shift_right, ALU.bitwise_and)
     vts(A("negI"), A("DD"), 0.0, -1.0, ALU.is_equal, ALU.mult)
     vts(C("mk", 0, 1), C("cI", 0, 1), 0.0, None, ALU.is_equal)
     vts(C("mk", 1, 2), C("cI", 0, 1), 1.0, None, ALU.is_equal)
     vts(C("cI", 1, 2), C("pI", 0, 1), 15, None, ALU.bitwise_and)
-    vts(C("mk", 2, 3), C("cI", 1, 2), float(R), None, ALU.add)
     vcopy(C("mk", 3, 4), C("cI", 1, 2))
 
     def LL(t, gj):
@@ -407,77 +417,107 @@ def rank_program(g, core, T, topo):
         for gj in range(2):
             m = C("mk", t, t + 1)
             vts(LL(t, gj), A("DD"), float(16 * (gj - t)), m[0], ALU.is_equal, ALU.mult, extra=[m])
-    act(A("Ib"), A("negI"), scale=-1.0)
+    def Wt(w):
+        return half("Wt", w, 128)
+    chain["scalar"] = CFG["chain"]
+    if CFG["rep"] == "pe":
+        act(A("Ih"), A("negI"), scale=-1.0)
     act(A("nIb"), A("negI"))
-    for w in range(6):
-        act(half("Wt", w, 128), A("negI"), scale=-float(w + 1))
+    act(A("ownI"), A("negI"), scale=-(6.0 * R - BLK + H) / (R - H))
+    op("vector", lambda: g.vector.memset(T.s4[:], 6 * R + 0.25), [], [A("s4")])
+    for w in range(CFG["wt"]):
+        act(Wt(w), A("negI"), scale=-float(w + 1))
 
     vcopy(ship, A("shipI"))
+    vcopy(A("CP"), IND(C("CI", 0, R), ship), extra=[od])
+    exchange("ac", lambda b: half("CP", b, H), lambda b: C("CI", R + H * b, R + H * (b + 1)))
+    for b in range(NB):
+        zero(blk("VV", Z0, b, -1, 0))
+    act(A("CH"), C("CI", 0, R), ACT.Identity, bias=MID, extra=[od])
     for w in range(7):
         if w < CFG["siS"]:
             act(A("SI", ALL, w), A("shipI"), ACT.Identity, bias=float(R * (w + 2) if w < 6 else 0))
         else:
             vts(A("SI", ALL, w), A("shipI"), float(R * (w + 2) if w < 6 else 0), None, ALU.add)
-    vcopy(A("CP"), IND(C("CI", 0, R), ship), extra=[od])
-    exchange("ac", lambda b: half("CP", b, H), lambda b: C("CI", R + H * b, R + H * (b + 1)))
 
     pieces, lists, w0, l0 = {}, {}, 0, 0
     vcopy(C("L7", 0, 105), A("SI"))
-    act(A("PK0"), IND(C("VV", 2 * R, 10 * R), C("L7", 0, 105)))
+    act(A("diagI"), A("negI"), scale=-(7.0 * R - BLK + 8 * H) / (R - H))
+    for w in range(CFG["wt"], CFG["wt2"]):
+        act(Wt(w), A("negI"), scale=-float(w + 1))
+    for fn, b0, b1 in ((act, CFG["cut0"], NB), (vcopy, 0, CFG["cut0"])):
+        if b0 < b1:
+            fn(C("PK0", 7 * H * b0, 7 * H * b1), IND(C("VV", 2 * R, 10 * R), C("L7", 21 * b0, 21 * b1)))
+    chain.clear()
+    for w in range(CFG["wt2"], 6):
+        act(Wt(w), A("negI"), scale=-float(w + 1))
+    hold.clear()
     exchange("a0", lambda b: half("PK0", b, 7 * H), lambda b: blk("VV", Z0, b, 0, 7))
     for i, nw in enumerate(CFG["pieces"]):
         if nw not in lists:
             lists[nw], l0 = l0, l0 + 15 * nw + nw % 2
-            vts(C("LP", lists[nw], lists[nw] + 15 * nw), A("SI", ALL, slice(0, nw)), -2.0 * R, None, ALU.add)
+            if CFG["u16S"]:
+                act(C("LP", lists[nw], lists[nw] + 15 * nw), A("SI", ALL, slice(0, nw)), ACT.Identity, bias=-2.0 * R)
+            else:
+                vts(C("LP", lists[nw], lists[nw] + 15 * nw), A("SI", ALL, slice(0, nw)), -2.0 * R, None, ALU.add)
         pieces[w0 + nw - 1] = (i, w0, nw, lists[nw])
         w0 += nw
-    act(A("CH"), C("CI", 0, R), ACT.Identity, bias=MID, extra=[od])
     vtr(A("OT"), A("CH"))
     for ci in range(2):
         for gj in range(2):
             mm(bank(4, 112 * ci, 112), LL(ci, gj), A("OT", ALL, slice(16 * gj, 16 * gj + 16, 2)), gj == 0)
     for ci in range(2):
         for gj in range(2):
-            mm(bank(5, 14 * ci, 14), LL(ci, gj), A("OT", ALL, 16 * gj + 1), gj == 0)
+            mm(A("PS", 5, slice(ci, 28, 2)), LL(ci, gj), A("OT", ALL, 16 * gj + 1), gj == 0)
     for ci in range(2):
         (act if CFG["cn"][0] == "S" else vcopy)(A("Cn", slice(ci, 28, 2)), bank(4, 112 * ci, 112))
-        (act if CFG["cn"][1] == "S" else vcopy)(C("C0", ci, 28, 2), bank(5, 14 * ci, 14))
     c1, sp = A("Cn", slice(0, 28), 0), A("SP")
-    vtt(A("wm"), A("C0"), c1, ALU.is_gt)
+    vtt(A("wm"), bank(5, 0, 28), c1, ALU.is_gt)
     vtt(A("wd"), half("spotI", 1, 28), half("spotI", 0, 28), ALU.subtract)
     vtt(A("we"), A("wm"), A("wd"), ALU.mult)
     vtt(half("SP", 0, 28), half("spotI", 1, 28), A("we"), ALU.subtract)
     vtt(half("SP", 1, 28), half("spotI", 0, 28), A("we"), ALU.add)
     for t in range(2):
         vcopy(C("spotK", t, 56, 2), half("SP", t, 28))
-    if CFG["crep1"]:
-        vtt(c1, A("C0"), c1, ALU.max)
-        for w in range(6):
-            vcopy(A("Crep", slice(0, 28), ALL, w), A("Cn", slice(0, 28)))
-    else:
-        vtt(A("Cn", slice(28, 56), 0), A("C0"), c1, ALU.max)
-        vcopy(A("Cn", slice(28, 56), slice(1, 8)), A("Cn", slice(0, 28), slice(1, 8)))
-        for w in range(6):
-            (act if w < CFG["crepS"] else vcopy)(A("Crep", ALL, ALL, w), A("Cn"))
+    vtt(A("Cn", slice(28, 56), 0), bank(5, 0, 28), c1, ALU.max)
+    vcopy(A("Cn", slice(28, 56), slice(1, 8)), A("Cn", slice(0, 28), slice(1, 8)))
+    own = {0: (2, 336), 1: (2, 0), 2: (0, 0), 3: (1, 0), 4: (5, 0), 5: (6, 0), 6: (7, 0), 7: (3, 0)}
+
+    def repeat(x):
+        (b, z), c0 = own[x], 0 if x else 28
+        for w in range(6 if CFG["rep"] == "pe" else 0):
+            mm(A("PS", b, slice(z + w, z + 6 * (56 - c0), 6)), A("Ih"), A("Cn", slice(c0, 56), x), True)
+    for x in range(2, 8):
+        repeat(x)
+    for w in range(0 if CFG["rep"] == "pe" else 6):
+        vcopy(A("Crep", ALL, ALL, w), A("Cn"))
+    def affine(name, o, i, scale, bias, extra=()):
+        if name in CFG["onV"]:
+            vts(o, i, scale, bias, ALU.mult, ALU.add, extra=extra)
+        else:
+            act(o, i, ACT.Identity, bias=bias, scale=scale, extra=extra)
+
     for t in range(2):
-        q = C("mk", 2 + t, 3 + t)
-        act(half("MS", t, 28), A("wm"), ACT.Identity, bias=q[0], scale=float(R if t else -R), extra=[q])
+        q = C("mk", 3, 4)
+        affine("MS", half("MS", t, 28), A("wm"), float(R if t else -R), q[0], extra=[q])
     vtt(A("LS"), A("MS"), A("N16"), ALU.add)
     act(A("AS"), IND(C("VV", 0, 2 * R), A("LS")))
-    act(A("s1"), sp, ACT.Identity, bias=-471.5 / H, scale=1.0 / H)
+    affine("s1", A("s1"), sp, 1.0 / H, -471.5 / H)
     vcopy(A("s2"), A("s1"))
     vts(A("s8"), sp, float(R), float(R - H), ALU.is_lt, ALU.mult)
-    act(A("s3"), A("s2"), ACT.Relu, bias=float(BLK - H), scale=float(BLK - H))
-    act(A("s4"), A("s8"), ACT.Identity, bias=6 * R - BLK + H + 0.25, scale=-(6.0 * R - BLK + H) / (R - H))
-    act(A("s7"), A("s8"), ACT.Identity, bias=-1.0 / H, scale=(1.0 / H - 1.0 / R) / (R - H))
-    vtt(A("sa"), A("s3"), sp, ALU.add)
-    vtt(A("s5"), A("sa"), A("s4"), ALU.add)
-    vtt(A("nAB", ALL, 0), A("s5"), A("s7"), ALU.mult)
-    act(A("nAB", ALL, 1), A("nAB", ALL, 0))
+    vts(A("s3"), A("s2"), -1.0, float(BLK - H), ALU.max, ALU.mult)
+    affine("s7", A("s7"), A("s8"), (1.0 / R - 1.0 / H) / (R - H), 1.0 / H)
+    nA = bank(4, R, 56)
+    for i, (m, x) in enumerate((("negI", A("s4")), ("negI", sp), ("ownI", A("s8")), ("negI", A("s3")))):
+        mm(nA, A(m), x, i == 0)
+    vtt(A("nAB", ALL, 0), nA, A("s7"), ALU.mult)
+    nD = bank(3, 400, 56)
+    for i, (m, x) in enumerate((("negI", sp), ("diagI", A("s8")), ("negI", A("s3")))):
+        mm(nD, A(m), x, i == 0)
+    vts(A("spotD"), nD, -1.0, 7 * R + 7 * H + 0.25, ALU.mult, ALU.add)
+    affine("nAB", A("nAB", ALL, 1), A("nAB", ALL, 0), 1.0, 0.0)
     for k in range(2):
-        act(A("Brep", ALL, k), A("s8"), ACT.Identity, bias=float(H))
-    mm(bank(0), A("nIb"), half("AS", 0), True)
-    mm(bank(1), A("Ib"), half("AS", 1), True)
+        affine("B", A("Brep", ALL, k), A("s8"), 1.0, float(H))
 
     for c0, c2, who in CFG["turn"]:
         o, i = C("GK", 32 * c0, 32 * c2), IND(A("CI"), C("spotK", 2 * c0, 2 * c2))
@@ -491,20 +531,33 @@ def rank_program(g, core, T, topo):
             for gj in range(2):
                 mm(bank(2, 168 * t + 6 * c0, 6 * (c2 - c0)), LL(t, gj),
                    A("GT", slice(c0, c2), slice(16 * gj + 4, 16 * gj + 16, 2)), gj == 0)
+    if CFG["rep"] == "pe":
+        (act if CFG["gs"] == "S" else vcopy)(A("GS"), bank(2, 0, 336))
     for tab in ("T1", "T2"):
         zero(C(tab, 0, R))
         zero(blk(tab, 0, 0, -1, 0))
         for b in range(NB):
             zero(blk(tab, 0, b, 6, 7 if b == NB - 1 else 8))
+    nadd = sum(m[2:] == "M" for m in CFG["modes"][2])
+    adds = []
+
+    def add_y(z, src, sem):
+        adds.append(sem)
+        op("pool", lambda: g.dma_start(T.y[:, z:z + 2 * R], src[0], accum_op=ALU.add), [src], [(None, "y", ((1 << 2 * R) - 1) << z)],
+           sem=sem, count=16, cost=1.0, lag=CFG["addlag"])
+        op("sync", None, [(None, "y", ((1 << R) - 1) << z)], [], sem="stored", cost=CFG["addwire"], lag=0.0)
+    if nadd:
+        op("pool", lambda: g.dma_start(T.y[:, 3 * R:(3 + nadd) * R], T.val[:, 3 * R:(3 + nadd) * R]), [],
+           [(None, "y", ((1 << nadd * R) - 1) << 3 * R)], sem="pre", count=16, cost=2.0, lag=4.0)
 
     def compare(x):
         ts = slice(0 if x else 1, 2)
-        if CFG["crep1"]:
-            for t in range(ts.start, 2):
-                vtt(A("EQ", t, slice(28 * x, 28 * x + 28)), bank(2, 168 * t, 168), A("Crep", slice(0, 28), x), ALU.is_equal)
+        if CFG["rep"] != "pe":
+            vtt(A("EQ", ts, slice(28 * x, 28 * x + 28)), bank(2, 168 * ts.start, 336 - 168 * ts.start),
+                A("Crep", slice(28 * ts.start, 56), x), ALU.is_equal)
             return
-        vtt(A("EQ", ts, slice(28 * x, 28 * x + 28)), bank(2, 168 * ts.start, 336 - 168 * ts.start),
-            A("Crep", slice(28 * ts.start, 56), x), ALU.is_equal)
+        vtt(A("EQ", ts, slice(28 * x, 28 * x + 28)), bank(own[x][0], own[x][1], 336 - 168 * ts.start),
+            C("GS", 168 * ts.start, 336), ALU.is_equal)
 
     def address(ch, o):
         s, n = ch[0], len(ch)
@@ -514,36 +567,47 @@ def rank_program(g, core, T, topo):
             mm(o, half("Wt", w, 128), A("EQ", ts, cs, w), False)
         vtt(A("OFF", ts, cs), o, A("Brep", ts, slice(0, n)), ALU.mult)
 
-    for ch, wb in zip(CFG["chunks"], [3, 6, 7, 3, 6]):
+    for ch, wb in zip(CFG["chunks"], CFG["abank"]):
         for x in ch:
             compare(x)
         address(ch, bank(wb, 0, 56 * len(ch)))
-    act(A("s9"), A("s8"), ACT.Identity, bias=float(R + 7 * H), scale=-(R + 7.0 * H) / (R - H))
-    vtt(A("spotD"), A("s9"), A("s5"), ALU.add)
-    vcopy(A("spotU"), A("spotI"))
+    repeat(0)
+    repeat(1)
+    mm(bank(0), A("nIb"), half("AS", 0), True)
+    mm(bank(1), Wt(0), half("AS", 1), True)
+    (act if CFG["u16S"] else vcopy)(A("spotU"), A("spotI"))
 
     def second_x():
-        vtt(half("XS2", 1), bank(1), half("RK1", 1), ALU.mult)
+        if CFG["x2pe"]:
+            vtt(A("SQ2"), IND(C("VV", 2 * R, Z0 + TW), half("spotD", 1, 28)), half("AS", 1), ALU.mult)
+            mm(bank(1), half("Wt", 1, 128), half("AS", 1), True)
+            mm(bank(1), A("negI"), A("SQ2"), False)
+            act(half("XS2", 1), bank(1))
+        else:
+            vtt(half("XS2", 1), bank(1), half("RK1", 1), ALU.mult)
 
     def last_lists():
         vtt(half("OFL", 0, 28), A("OFF", 1, slice(0, 28)), A("wm"), ALU.mult)
         vtt(half("OFL", 1, 28), A("OFF", 1, slice(0, 28)), half("OFL", 0, 28), ALU.subtract)
 
     def first_r(t):
-        act(half("RK1", t), IND(C("VV", 2 * R, Z0 + TW), half("spotD", t, 28)), ACT.Identity, bias=2.0, scale=-1.0)
-    fill = {"rk0": lambda: first_r(0), "rk1": lambda: first_r(1), "x2": second_x, "lists": last_lists,
+        sign = -1.0 if t else 1.0
+        act(half("RK1", t), IND(C("VV", 2 * R, Z0 + TW), half("spotD", t, 28)), ACT.Identity, bias=2.0 * sign, scale=-sign)
+    fill = {"rk": lambda: act(A("RK1"), IND(C("VV", 2 * R, Z0 + TW), A("spotD")), ACT.Identity, bias=2.0, scale=-1.0),
+            "rk0": lambda: first_r(0), "rk1": lambda: first_r(1), "x2": second_x, "lists": last_lists,
             "sq": lambda: act(A("SQ"), plane(2), ACT.Square, bias=2.0, scale=-1.0),
             "posI": lambda: act(A("posI"), A("negI"), scale=-1.0), "n2I": lambda: act(A("n2I"), A("negI"), scale=2.0)}
     for name in CFG["fill"][0]:
         fill[name]()
 
     cu, cp = [0], [0]
+    low3 = CFG["modes"][2][CFG["order3"].index(0)]
 
     def sweep(k):
         order = [2, 3, 4, 5, 6, 7] if k < 2 else CFG["order3"]
         modes = dict(zip(order, CFG["modes"][k]))
         if k < 2:
-            modes[0], modes[1] = "-D", CFG["diag"][k]
+            modes[0], modes[1] = "-" + CFG["low"][k], CFG["diag"][k]
         win = [C("VV", Z0, Z0 + TW), A("T1"), A("T2")][k]
         xs = [(half("AS", 0), half("AS", 1)), (A("X1"), half("AS", 1)), (half("XS2", 0), half("XS2", 1))][k]
         nx0 = bank([0, 2, 0][k])
@@ -556,6 +620,11 @@ def rank_program(g, core, T, topo):
             return A("OFF", t, slice(28 * s, 28 * (s + n)))
 
         def gather(s):
+            if s == 0 and k == 2 and low3 == "AA" and 0 in CFG["gp"][k] and (0, 0) not in ub:
+                u = "U%d" % (cu[0] % NU)
+                cu[0] += 1
+                act(A(u), IND(win, A("OFL")))
+                ub[0, 0], ub[0, 1] = half(u, 0), half(u, 1)
             for t in range(2):
                 if modes[s][t] == "A" and (s, t) not in ub:
                     n = 2 if s in CFG["gp"][k] and modes[s + 1][t] == "A" else 1
@@ -574,20 +643,33 @@ def rank_program(g, core, T, topo):
                 vtt(pb[s, t], IND(win, off(s, t)), xs[x], ALU.mult)
             return pb[s, t]
 
+        def added(s):
+            s0 = s - s % 2
+            for t in (1, 0):
+                o = half("Q%d%d" % (s0 // 2 - 1, t), s % 2)
+                if modes[s][t] == "A":
+                    vtt(o, ub[s, t], bank(1) if t else nx0, ALU.mult)
+                else:
+                    vtt(o, IND(win, off(s, t)), xs[t], ALU.mult)
+            if s % 2:
+                add_y(R * (s0 + 1), A("Q%d1" % (s0 // 2 - 1)), "add%d1" % (s0 // 2 - 1))
+            for x in range(nadd // 2 if s == nadd + 1 else 0):
+                add_y(R * (2 * x + 3), A("Q%d0" % x), "add%d0" % x)
+
         def products(s, b):
             ab[s], a = b, plane(s + 1)
-            mm(bank(b), A("Ib"), a, True)
+            mm(bank(b), Wt(0), a, True)
             if modes[s][0] == "A":
                 vtt(bank(b), ub[s, 0], nx0, ALU.mult)
-                mm(bank(b), A("Ib"), a, False)
+                mm(bank(b), Wt(0), a, False)
             else:
                 mm(bank(b), A("negI"), product(s, 0, 0), False)
             p = product(s, 1, 1)
             if modes[s][2:] != "V":
-                mm(bank(b), A("negI"), p, False)
+                mm(bank(b), A("posI" if k == 2 else "negI"), p, False)
 
         def finish(s):
-            if s in CFG["fp"][k]:
+            if s in CFG["fp"][k] or modes[s][2] == "M":
                 return
             s0 = s - 1 if s - 1 in CFG["fp"][k] else s
             parts = [(0, R // 2, "scalar"), (R // 2, R // 2, "sync")] if k == 2 and s == order[-1] else [(0, R * (s - s0 + 1), "sync")]
@@ -595,7 +677,7 @@ def rank_program(g, core, T, topo):
                 z = R * (s0 - 1) + a if k < 2 else R * (s0 + 1) + a
                 o = C(out_tab or "YY", z, z + n)
                 if modes[s][2] == "V":
-                    vtt(o, bank(ab[s], a, n), C(pb[s, 1][1], a, a + n), ALU.subtract)
+                    vtt(o, bank(ab[s], a, n), C(pb[s, 1][1], a, a + n), ALU.add if k == 2 else ALU.subtract)
                 elif s0 < s:
                     act(o, A("PS", slice(ab[s0], ab[s] + 1), slice(0, R)))
                 else:
@@ -614,12 +696,12 @@ def rank_program(g, core, T, topo):
         def last_lower():
             for t in range(2):
                 b, o = bank(banks.pop(0)), half("YY", t)
-                mm(b, A("Ib"), plane(t), True)
+                mm(b, Wt(0), plane(t), True)
                 if modes[0][t] == "A":
                     vtt(b, ub[0, t], bank(1), ALU.mult)
-                    mm(b, A("nIb"), plane(t), False)
+                    mm(b, Wt(0), plane(t), False)
                 else:
-                    mm(b, A("negI"), product(0, t, 1), False)
+                    mm(b, A("posI"), product(0, t, 1), False)
                 vtt(o, b, half("RK2", t), ALU.mult)
                 store("sync", T.y[:, R * t:R * (t + 1)], o)
 
@@ -628,6 +710,8 @@ def rank_program(g, core, T, topo):
                 gather(x)
             if s == 0:
                 last_lower()
+            elif modes[s][2] == "M":
+                added(s)
             else:
                 products(s, banks.pop(0))
             behind_v = max(j for j, o in enumerate(ops) if o["q"] == "vector")
@@ -642,38 +726,47 @@ def rank_program(g, core, T, topo):
         if k == 0:
             compare(0)
             compare(1)
-            address([0], bank(2, 392, 28))
-            address([1], bank(2, 336, 56))
+            address([0], bank(3, 0, 28))
+            address([1], bank(3, 32, 56))
         for name in CFG["fill"][k + 1]:
             fill[name]()
         gather(1)
+        gather(0)
         b0 = bank(2 if k == 0 else banks.pop(0))
         mm(b0, A("nIb"), half("AS", 0), True)
-        mm(b0, A("posI"), product(0, 1, 1), False)
+        if modes[0][1] == "A":
+            vtt(b0, ub[0, 1], bank(1), ALU.mult)
+            mm(b0, A("nIb"), half("AS", 0), False)
+        else:
+            mm(b0, A("posI"), product(0, 1, 1), False)
         if k == 1:
             vtt(bank(0), b0, half("RK1", 0), ALU.mult)
-        if any(m[0] == "D" for m in CFG["modes"][k + 1][:4] + CFG["modes"][k + 1][5:] + CFG["modes"][1][4:5] + CFG["diag"][k + 1:]):
+        if any(m[0] == "D" and len(m) == 3 for m in CFG["modes"][k + 1]) or any(m[0] == "D" for m in CFG["diag"][k + 1:]):
             act(A("X1") if k == 0 else half("XS2", 0), bank(2 if k == 0 else 0), scale=-1.0)
         products(1, 3)
-        if k == 1 and (any(m[1] == "A" for m in CFG["modes"][2]) or "A" in CFG["modes"][2][4]):
+        if modes[1][2:] == "V":
+            vtt(bank(3), bank(3), pb[1, 1], ALU.subtract)
+        if k == 1 and not CFG["x2pe"] and (any(m[1] == "A" for m in CFG["modes"][2]) or "A" in low3):
             act(bank(1), half("XS2", 1))
         e, rn = bank(CFG["rsq"][k]), (half("RT2", 0) if k == 0 else A("R3"))
-        mm(e, A("Ib"), plane(2), True)
+        if k == 0 or CFG["r3"] == "pe":
+            mm(e, Wt(0), plane(2), True)
         vtt(e, bank(3), A("SQ"), ALU.mult)
+        if k == 1 and CFG["r3"] != "pe":
+            act(A("SQ2"), half("RT2", 0), scale=2.0)
+            vtt(rn, A("SQ2"), e, ALU.subtract)
         if k == 0:
-            mm(e, A("Ib"), plane(2), False)
-            mm(e, A("Ib"), plane(2), False)
+            mm(e, Wt(1), plane(2), False)
             act(rn, e, ACT.Identity, bias=4.0, scale=-1.0)
             act(A("PR2"), IND(rn, ship))
             exchange("ar2", lambda b: half("PR2", b, H), lambda b: C("RT2", R + H * b, R + H * (b + 1)))
             act(A("SQ"), rn, ACT.Square)
         else:
-            mm(e, A("n2I"), half("RT2", 0), False)
-            act(rn, e, scale=-1.0)
+            if CFG["r3"] == "pe":
+                mm(e, A("n2I"), half("RT2", 0), False)
+                act(rn, e, scale=-1.0)
             store("sync", T.inv[:], rn)
-            sign = [-1.0 if c == "A" else 1.0 for c in CFG["modes"][2][4]]
-            for t0, t1 in ([(0, 2)] if sign[0] == sign[1] else [(0, 1), (1, 2)]):
-                act(C("RK2", R * t0, R * t1), IND(A("RT2"), C("spotU", 28 * t0, 28 * t1)), scale=sign[t0])
+            act(A("RK2"), IND(A("RT2"), A("spotU")))
         hold.clear()
 
     for k in range(3):
@@ -707,7 +800,7 @@ def rank_program(g, core, T, topo):
         deps.append(sorted(d))
         behind.append(sorted(f))
     if not ORDER:
-        ORDER.extend(issue_order(ops, deps, behind))
+        ORDER.extend(CFG.get("fixed") or issue_order(ops, deps, behind))
     place = {j: p for p, j in enumerate(ORDER)}
     needed = set()
     for j, o in enumerate(ops):
@@ -725,7 +818,7 @@ def rank_program(g, core, T, topo):
     seen = {q: {} for q in queue}
     for j in ORDER:
         o = ops[j]
-        if o["q"] == "arrive":
+        if o["fn"] is None:
             continue
         want = [ops[i]["tok"] for i in o["latest"].values()] + [ops[i]["tok"] for i in deps[j] if ops[i]["sem"] is not None]
         for s, n in want:
@@ -738,5 +831,7 @@ def rank_program(g, core, T, topo):
                 ins.then_inc(T.sem[o["q"]], 1)
         elif o["sem"] != "remote":
             ins.then_inc(T.sem[o["sem"]], 16)
+    for sem in adds:
+        g.wait_ge(T.sem[sem], 16)
     g.wait_ge(T.sem["sent"], nsent[0])
     g.sync.wait_ge(T.sem["stored"], nstore[0])

import numpy as np
from concourse.bass import DstId, RemoteDMATransfer
from concourse.mybir import AluOpType, ActivationFunctionType

R, H, NB = 448, 48, 5
BLK = 8 * H
TW = 7 * R + NB * BLK
Z0 = 3 * R
MID = -1344.0
NU, NP = 8, 8

CFG = {
    "modes": [["ADS", "ADS", "ADV", "ADS", "ADS", "ADV"],
              ["ADS", "ADS", "ADV", "ADS", "ADS", "ADV"],
              ["ADS", "ADS", "AAV", "ADS", "AA", "ADS", "AAV", "ADV"]],
    "order3": [2, 3, 4, 5, 0, 1, 6, 7],
    "low": "DD", "r3": "pe", "diag": ["AD", "AD"], "cn": "VV", "gs": "S", "abank": [2, 4, 2, 2], "x2pe": False, "onV": ["MS", "s1", "s4", "s7", "nAB", "B", "s9"], "siS": 3, "chain": True, "cut0": 0, "u16S": False, "addlag": 4.0, "addwire": 0.8, "rep": "pe", "slowval": 1.0, "rlag": 0.65, "wt": 2, "wt2": 5, "hold": False,
    "fill": [["posI"], ["sq", "rk1"], ["rk0", "x2", "lists", "n2I"]], "ahead": 2,
    "gp": [[2, 4, 6], [2, 4, 6], [0, 2, 4, 6]], "fp": [[2], [2], [2]],
    "pieces": [2, 2, 2],
    "cut": [[0, 0, 2], [0, 0, 2]],
    "chunks": [[2], [3], [4, 5], [6, 7]], "turn": [(0, 12, "V"), (12, 20, "S"), (20, 28, "S")],
    "banks": [[4, 5, 3, 6, 7, 4], [4, 5, 0, 6, 7, 4, 5], [4, 5, 6, 7, 2, 3, 4, 5, 6]], "rsq": [0, 6],
    "first": 2.3, "rows": 0.75, "perword": 0.006, "store": 0.5,
    "cases": [(1.35, 0.8, 1.1, 0.08), (1.1, 0.85, 1.1, 0.07), (1.9, 0.7, 1.03, 0.08), (1.3, 0.75, 1.6, 0.08), (1.5, 1.2, 1.1, 0.08), (1.3, 0.6, 1.0, 0.06)], "seed": 7, "rounds": 300, "swaps": 55000, "heat": 0.15, "land": 0.03, "pefix": 0.02, "nudge": 3, "give": 0.05, "sigma": 1.0, "big": 0.12,
}
FIXED = {"vector": 0.058, "scalar": 0.12, "tensor": 0.03, "pool": 0.13}
CYCLE = {"vector": 0.00083, "scalar": 0.00083, "tensor": 0.000417, "pool": 0.00083}

SCRATCH = {
    "CI": ("sbuf", [128, R + NB * H], "int32"), "CH": ("sbuf", [128, R], "float16"), "CP": ("sbuf", [128, NB * H], "int32"),
    "shipI": ("sbuf", [128, 15], "int32"), "shipU": ("sbuf", [128, 16], "uint16"),
    "spotI": ("sbuf", [128, 56], "int32"), "SP": ("sbuf", [128, 56], "float32"),
    "spotK": ("sbuf", [128, 56], "uint16"), "spotU": ("sbuf", [128, 56], "uint16"), "spotD": ("sbuf", [128, 56], "uint16"),
    "LS": ("sbuf", [128, 56], "uint16"), "OFL": ("sbuf", [128, 56], "uint16"),
    "GK": ("sbuf", [128, 896], "float16"), "GT": ("sbuf", [128, 28, 32], "float16"), "OT": ("sbuf", [128, 14, 32], "float16"),
    "C0": ("sbuf", [128, 28], "float16"), "Cn": ("sbuf", [128, 56, 8], "float16"), "GS": ("sbuf", [128, 336], "float16"),
    "Ih": ("sbuf", [128, 128], "float16"), "Crep": ("sbuf", [128, 56, 8, 6], "float16"),
    "EQ": ("sbuf", [128, 2, 224, 6], "bfloat16"), "OFF": ("sbuf", [128, 2, 224], "uint16"),
    "DD": ("sbuf", [128, 128], "float32"), "pI": ("sbuf", [128, 4], "int32"), "cI": ("sbuf", [128, 4], "int32"),
    "mk": ("sbuf", [128, 4], "float32"), "LL": ("sbuf", [128, 512], "float16"), "N16": ("sbuf", [128, 56], "float32"),
    "negI": ("sbuf", [128, 128], "float32"), "posI": ("sbuf", [128, 128], "float32"), "n2I": ("sbuf", [128, 128], "float32"),
    "diagI": ("sbuf", [128, 128], "float32"), "ownI": ("sbuf", [128, 128], "float32"), "nIb": ("sbuf", [128, 128], "bfloat16"), "Wt": ("sbuf", [128, 768], "bfloat16"),
    "nAB": ("sbuf", [128, 2, 2, 28], "float32"), "Brep": ("sbuf", [128, 2, 2, 28], "float32"),
    "VV": ("sbuf", [128, Z0 + TW], "bfloat16"), "T1": ("sbuf", [128, TW], "float32"), "T2": ("sbuf", [128, TW], "float32"),
    "AS": ("sbuf", [128, 896], "bfloat16"),
    "PK0": ("sbuf", [128, NB * 7 * H], "bfloat16"), "PK1": ("sbuf", [128, NB * 6 * H], "float32"), "PK2": ("sbuf", [128, NB * 6 * H], "float32"),
    "SI": ("sbuf", [128, NB, 7, 3], "float32"), "L7": ("sbuf", [128, 106], "uint16"), "LP": ("sbuf", [128, 142], "uint16"),
    "SQ": ("sbuf", [128, R], "float32"), "SQ2": ("sbuf", [128, R], "float32"),
    "RT2": ("sbuf", [128, R + NB * H], "float32"), "PR2": ("sbuf", [128, NB * H], "float32"),
    "RK1": ("sbuf", [128, 896], "float32"), "RK2": ("sbuf", [128, 896], "float32"), "R3": ("sbuf", [128, R], "float32"),
    "X1": ("sbuf", [128, R], "float32"), "XS2": ("sbuf", [128, 896], "float32"),
    "YY": ("sbuf", [128, 9 * R], "float32"),
    "PS": ("psum", [128, 8, 512], "float32"),
}
for _n in ("m", "d", "e"):
    SCRATCH["w" + _n] = ("sbuf", [128, 28], "float32")
for _n in ("s1", "s3", "s4", "s5", "s6", "s7", "s8", "s9", "sa", "MS", "Bm"):
    SCRATCH[_n] = ("sbuf", [128, 56], "float32")
SCRATCH["s2"] = ("sbuf", [128, 56], "int32")
for _i in range(NU):
    SCRATCH["U%d" % _i] = ("sbuf", [128, 896], "float32")
for _i in range(NP):
    SCRATCH["P%d" % _i] = ("sbuf", [128, R], "float32")

LOADS = ["lc0", "lc1", "lship", "lspot", "lv0", "lv1", "lv2", "lv3"]
ARRIVALS = ["ac", "a0", "ar2"] + ["a%d%d" % (k, i) for k in (1, 2) for i in range(6)]
for _n in ("00", "01", "10", "11"):
    SCRATCH["Q" + _n] = ("sbuf", [128, 896], "float32")
SEMAPHORES = ["pre", "add00", "add01", "add10", "add11", "vector", "scalar", "tensor", "pool", "sent", "stored"] + LOADS + ARRIVALS

ALU = AluOpType
ACT = ActivationFunctionType
ALL = slice(None)


def _mask(name, idx):
    m = np.zeros(SCRATCH[name][1][1:], bool)
    m[idx] = True
    return int.from_bytes(np.packbits(m.ravel(), bitorder="little").tobytes(), "little")


def _banks(m):
    full = (1 << 512) - 1
    return sum(1 << b for b in range(8) if (m >> (512 * b)) & full)


def engine_sets(topo, src, peers):
    eng = topo.engines(src, peers[0])
    half = len(eng) // 2
    quarters = [eng[0:half:2], eng[1:half:2], eng[half::2], eng[half + 1::2]]
    near = [p for p in peers if topo.die(p) == topo.die(src)]
    far = [p for p in peers if topo.die(p) != topo.die(src)]
    last = ([p for p in near if p > src] + near + far)[0]
    near, far = [p for p in near if p != last], [p for p in far if p != last]
    order = []
    while near or far:
        if far:
            order.append(far.pop())
        if near:
            order.append(near.pop())
    first = [(p, sum(1 << e for e in q), len(q)) for p, q in zip(order, quarters)]
    return first, (last, sum(1 << e for e in eng), len(eng))


ORDER = []


def issue_order(ops, deps, behind):
    every = range(len(ops))
    reach, before, after = [], [], [[] for _ in ops]
    for j in every:
        far = 0
        for i in deps[j]:
            far |= reach[i]
        near = [i for i in deps[j] if not far >> i & 1]
        reach.append(far | sum(1 << i for i in near))
        before.append([(i, True) for i in near] + [(i, ops[j]["q"] == "arrive") for i in behind[j]])
        for i, w in before[j]:
            after[i].append((j, w))
    cases = []
    for rate, dma, pe, wake in CFG["cases"]:
        scale = {"arrive": dma, "pool": dma, "tensor": pe}
        cost = [o["cost"] * scale.get(o["q"], 1.0) + o["gathered"] * rate for o in ops]
        cases.append((cost, [o["lag"] * dma + wake for o in ops]))
    cost, lag = cases[0]

    def lay(order, back):
        end, taken = [0.0] * len(ops), {}
        for j in order:
            c = cost[j]
            if back:
                t = max([end[i] + (lag[j] if w else 0.0) for i, w in after[j]], default=lag[j])
            else:
                t = max([end[i] + (lag[i] if w else 0.0) for i, w in before[j]], default=0.0)
            spans = taken.setdefault(ops[j]["q"], [])
            k = len(spans)
            while k and spans[k - 1][1] > t:
                k -= 1
            while k < len(spans) and t + c > spans[k][0] + 1e-9:
                t = spans[k][1]
                k += 1
            spans.insert(k, (t, t + c))
            end[j] = t + c
        return end

    def length(order):
        total = 0.0
        for cost, lag in cases:
            end, free = [0.0] * len(ops), {}
            for j in order:
                q = ops[j]["q"]
                t = max([end[i] + (lag[i] if w else 0.0) for i, w in before[j]], default=0.0)
                end[j] = free[q] = max(t, free.get(q, 0.0)) + cost[j]
            total += max(end[j] + lag[j] for j in every)
        return total

    def tighten(end):
        late = lay(sorted(every, key=lambda j: (-end[j], -j)), True)
        return lay(sorted(every, key=lambda j: (-late[j], j)), False)

    def judge(end):
        order = sorted(every, key=lambda j: (end[j] - cost[j], j))
        return length(order), end, order

    rng = np.random.default_rng(CFG["seed"])
    big = [j for j in every if cost[j] > CFG["big"]]
    best = cur = judge(tighten(lay(every, False)))
    for it in range(CFG["rounds"]):
        key = [cur[1][j] - cost[j] for j in every]
        for j in rng.choice(big, CFG["nudge"]):
            key[j] += float(rng.normal()) * CFG["sigma"]
        for j in every:
            for i, _ in before[j]:
                if key[j] <= key[i]:
                    key[j] = key[i] + 1e-6
        end = lay(sorted(every, key=lambda j: (key[j], j)), False)
        new = judge(tighten(end) if it % 3 == 0 else end)
        if new[0] < cur[0] + CFG["give"] * (1.0 - it / CFG["rounds"]):
            cur = new
        if new[0] < best[0]:
            best = new

    queue = [o["q"] for o in ops]

    waits = [[[(i, lag[i] if w else 0.0) for i, w in before[j]] for j in every] for cost, lag in cases]
    sinks = [j for j in every if not after[j]]
    lands = [j for j in every if queue[j] == "arrive"]
    links = ([{i for i, _ in x} for x in before], [{i for i, _ in x} for x in after])

    def clock(order, old, p0):
        prev, last = {}, {}
        for j in order:
            prev[j], last[queue[j]] = last.get(queue[j]), j
        total, ends, rest = 0.0, [], [(j, prev[j]) for j in order[p0:]]
        for c, (cost, lag) in enumerate(cases):
            end, wait = list(old[c]), waits[c]
            for j, p in rest:
                t = 0.0 if p is None else end[p]
                for i, x in wait[j]:
                    x += end[i]
                    if x > t:
                        t = x
                end[j] = t + cost[j]
            total += max(end[j] + lag[j] for j in sinks) + CFG["land"] * sum(end[j] for j in lands)
            ends.append(end)
        return total, order, ends, prev

    def shift(part, link):
        v, moved, flagged = part[-1], {part[-1]}, set()
        for x in reversed(part[:-1]):
            if queue[x] in flagged or link[x] & moved:
                if queue[x] == queue[v]:
                    return None
                moved.add(x)
                flagged.add(queue[x])
        return [x for x in part if x in moved] + [x for x in part if x not in moved]

    best = cur = clock(best[2], [[0.0] * len(ops)] * len(cases), 0)
    for it in range(CFG["swaps"]):
        c = int(rng.integers(len(cases)))
        (cost, lag), order, end, prev, arcs = cases[c], cur[1], cur[2][c], cur[3], []
        j = max(sinks, key=lambda j: end[j] + lag[j]) if rng.random() < 0.7 else lands[int(rng.integers(len(lands)))]
        while j is not None:
            t = end[j] - cost[j] - 1e-9
            if prev[j] is not None and end[prev[j]] > t:
                arcs.append(j)
                j = prev[j]
            else:
                j = next((i for i, x in waits[c][j] if end[i] + x > t), None)
        if not arcs:
            continue
        v = arcs[int(rng.integers(len(arcs)))]
        mates, far = [j for j in order if queue[j] == queue[v]], int(rng.integers(1, 5))
        p = mates.index(v)
        if rng.random() < 0.5:
            a, b = order.index(mates[max(p - far, 0)]), order.index(v) + 1
            part = shift(order[a:b], links[1])
        else:
            a, b = order.index(mates[p - 1]), order.index(mates[min(p - 1 + far, len(mates) - 1)]) + 1
            part = shift(order[a:b][::-1], links[0])
            part = part and part[::-1]
        if part:
            new = clock(order[:a] + part + order[b:], cur[2], a)
            if new[0] < cur[0] - CFG["heat"] * (1.0 - it / CFG["swaps"]) * float(np.log(rng.random())):
                cur = new
                if new[0] < best[0]:
                    best = new
    return best[1]


def rank_program(g, core, T, topo):
    rank = T.rank_of(core)
    if rank is None:
        return
    cores = list(T.cores)
    peers = [c for c in cores if c != core]
    ops = []

    chain = {}
    hold = {}

    def A(name, *idx):
        ix = tuple(idx) if idx else (ALL,)
        return (T[name][(ALL,) + ix], name, _mask(name, ix))

    def C(name, a, b, step=None):
        return A(name, slice(a, b, step))

    def IND(win, off):
        return (win[0].indirect(off[0]), [win, off])

    def op(q, fn, reads, writes, sem=None, count=None, rate=None, cost=None, lag=0.0):
        rd = []
        for r in reads:
            rd += r[1] if len(r) == 2 else [r]
        gathered = 0.0
        if cost is None:
            n = writes[0][2].bit_count()
            if any(len(r) == 2 for r in reads):
                cost, gathered = 0.06, n * CYCLE[q]
            else:
                if rate is None:
                    rate = 0.5 if q == "vector" and all(SCRATCH[x[1]][2].endswith("16") for x in rd[:1] + writes) else 1.0
                cost = CFG.get(q, FIXED[q]) + max(64, n * rate) * CYCLE[q]
        ops.append({"q": q, "fn": fn, "r": [(x[1], x[2]) for x in rd], "w": [(x[1], x[2]) for x in writes], "sem": sem, "n": count,
                    "cost": cost, "gathered": gathered, "lag": lag, "hold": hold.get(q)})
        if chain.get(q):
            hold[q] = len(ops) - 1

    def vcopy(o, i, extra=()):
        op("vector", lambda: g.vector.tensor_copy(o[0], i[0]), [i] + list(extra), [o])

    def vtt(o, a, b, f):
        op("vector", lambda: g.vector.tensor_tensor(o[0], a[0], b[0], f), [a, b], [o], rate=1.0 if "PS" in (a[1], b[1]) else 2.0)

    def vts(o, a, s1, s2, f0, f1=None, extra=()):
        if f1 is None:
            op("vector", lambda: g.vector.tensor_scalar(o[0], a[0], s1, None, f0), [a] + list(extra), [o])
        else:
            op("vector", lambda: g.vector.tensor_scalar(o[0], a[0], s1, s2, f0, f1), [a] + list(extra), [o])

    def vtr(o, i):
        op("vector", lambda: g.vector.transpose(o[0], i[0]), [i], [o])

    def act(o, i, f=ACT.Copy, bias=None, scale=None, extra=()):
        kw = {}
        if bias is not None:
            kw["bias"] = bias
        if scale is not None:
            kw["scale"] = scale
        op("scalar", lambda: g.scalar.activation(o[0], i[0], f, **kw), [i] + list(extra), [o])

    def iota(z, pattern, per_partition=0, base=0):
        op("pool", lambda: g.iota(z[0], pattern, base, per_partition, allow_small_or_imprecise_dtypes=True), [], [z], rate=2.0)

    def zero(z):
        iota(z, [[0, z[2].bit_count()]])

    groups = {b: [] for b in range(8)}

    def mm(o, l, r, start):
        b = _banks(o[2]).bit_length() - 1
        me = {"start": start, "stop": True}
        if not start:
            groups[b][-1]["stop"] = False
        groups[b].append(me)
        op("tensor", lambda: g.tensor.matmul(o[0], l[0], r[0], me["start"], me["stop"]), [l, r], [o],
           rate=4.0 if SCRATCH[l[1]][2] == "float32" else 1.0,
           cost=CFG["pefix"] + max(64, o[2].bit_count()) * CYCLE["tensor"] * (4 if SCRATCH[l[1]][2] == "float32" else 1))

    def load(q, sem, o, src, lag):
        eng = g.sync if q == "sync" else g.scalar
        op(q, lambda: eng.dma_start(o[0], src), [], [o], sem=sem, count=16, cost=0.06, lag=lag)

    nstore = [0]

    def store(q, dst, i):
        eng = g.sync if q == "sync" else g.scalar
        nstore[0] += 16
        wire = CFG["store"] * i[2].bit_count() / R
        op(q, lambda: eng.dma_start(dst, i[0]), [i], [], sem="stored", count=16, cost=wire if q == "sync" else 0.06, lag=1.6 if q == "sync" else 1.6 + wire)

    plans = {c: engine_sets(topo, c, [p for p in cores if p != c]) for c in cores}
    inbound = 0
    for c in peers:
        for p, m, n in plans[c][0] + [plans[c][1]]:
            if p == core:
                inbound += n
    nsent = [0]

    def exchange(sem, src_of, dst_of):
        def slot(p):
            q = T.rank_of(p)
            return (q if q < rank else q - 1), (rank if rank < q else rank - 1)
        first, last = plans[core]
        trs, rd = [], []
        for p, m, n in first:
            b, bb = slot(p)
            rid, pid, _ = topo.addr(p)
            trs.append(RemoteDMATransfer(dst_ids=[DstId(rid=rid, pnc=pid)], dma_engine_mask=m, remote_sem=T.sem[sem],
                                         src=src_of(b)[0], dst=dst_of(bb)[0]))
            rd.append(src_of(b))
            nsent[0] += n
        once = 0.0 if nsent[0] > 16 else CFG["first"]
        wire = CFG["rows"] + rd[0][2].bit_count() * CFG["perword"] * (0.5 if SCRATCH[rd[0][1]][2] == "bfloat16" else 1.0)
        op("pool", lambda: g.remote_dma_fused(trs, local_sem=T.sem["sent"]), rd, [], sem="remote", cost=0.35 + once, lag=CFG["rlag"])
        p, m, n = last
        b, bb = slot(p)
        rid, pid, _ = topo.addr(p)
        s, d = src_of(b), dst_of(bb)
        nsent[0] += n
        op("pool", lambda: g.remote_dma(d[0], s[0], T.sem[sem], T.sem["sent"], pid, rid, m), [s], [], sem="remote", cost=0.35, lag=CFG["rlag"] - 0.4)
        op("arrive", None, [], [dst_of(k) for k in range(NB)], sem=sem, count=inbound, cost=wire, lag=0.25)

    def blk(tab, base, b, w0, w1):
        z = base + 7 * R + b * BLK + H
        return C(tab, z + H * w0, z + H * w1)

    def bank(b, a=0, n=R):
        return A("PS", b, slice(a, a + n))

    def plane(s):
        s += s > 2
        return C("VV", R * s, R * (s + 1))

    def half(name, t, n=R):
        return C(name, n * t, n * (t + 1))

    ship = C("shipU", 0, 15)

    ev = (T.CI[0::2, 0:R], "CI", _mask("CI", (slice(0, R),)))
    od = (T.CI[1::2, 0:R], "CIodd", 1)
    load("sync", "lship", A("shipI"), T.ship[:], 1.8)
    load("scalar", "lc1", od, T.col[:, 0:8 * R], 1.9)
    load("sync", "lc0", ev, T.col[:, R:9 * R], 2.1)
    load("sync", "lspot", A("spotI"), T.spot[:], 2.2)
    load("sync", "lv0", C("VV", 4 * R, 7 * R), T.val[:, 3 * R:6 * R], 2.9 * CFG["slowval"])
    load("sync", "lv1", plane(2), T.val[:, 2 * R:3 * R], 3.2 * CFG["slowval"])
    load("sync", "lv2", C("VV", 7 * R, 10 * R), T.val[:, 6 * R:9 * R], 3.9 * CFG["slowval"])
    load("sync", "lv3", C("VV", 0, 2 * R), T.val[:, 0:2 * R], 4.4 * CFG["slowval"])

    iota(A("DD"), [[1, 128]], -1)
    op("pool", lambda: g.iota(T.pI[:, 0:1], [[0, 1]], 0, 1), [], [C("pI", 0, 1)], cost=0.13)
    iota(A("N16"), [[-R, 2], [16, 28]], base=R)
    zero(C("VV", Z0, Z0 + R))
    vts(C("cI", 0, 1), C("pI", 0, 1), 4, 1, ALU.arith_shift_right, ALU.bitwise_and)
    vts(A("negI"), A("DD"), 0.0, -1.0, ALU.is_equal, ALU.mult)
    vts(C("mk", 0, 1), C("cI", 0, 1), 0.0, None, ALU.is_equal)
    vts(C("mk", 1, 2), C("cI", 0, 1), 1.0, None, ALU.is_equal)
    vts(C("cI", 1, 2), C("pI", 0, 1), 15, None, ALU.bitwise_and)
    vcopy(C("mk", 3, 4), C("cI", 1, 2))

    def LL(t, gj):
        return C("LL", (2 * t + gj) * 128, (2 * t + gj + 1) * 128)
    for t in range(2):
        for gj in range(2):
            m = C("mk", t, t + 1)
            vts(LL(t, gj), A("DD"), float(16 * (gj - t)), m[0], ALU.is_equal, ALU.mult, extra=[m])
    def Wt(w):
        return half("Wt", w, 128)
    chain["scalar"] = CFG["chain"]
    if CFG["rep"] == "pe":
        act(A("Ih"), A("negI"), scale=-1.0)
    act(A("nIb"), A("negI"))
    act(A("ownI"), A("negI"), scale=-(6.0 * R - BLK + H) / (R - H))
    op("vector", lambda: g.vector.memset(T.s4[:], 6 * R + 0.25), [], [A("s4")])
    for w in range(CFG["wt"]):
        act(Wt(w), A("negI"), scale=-float(w + 1))

    vcopy(ship, A("shipI"))
    vcopy(A("CP"), IND(C("CI", 0, R), ship), extra=[od])
    exchange("ac", lambda b: half("CP", b, H), lambda b: C("CI", R + H * b, R + H * (b + 1)))
    for b in range(NB):
        zero(blk("VV", Z0, b, -1, 0))
    act(A("CH"), C("CI", 0, R), ACT.Identity, bias=MID, extra=[od])
    for w in range(7):
        if w < CFG["siS"]:
            act(A("SI", ALL, w), A("shipI"), ACT.Identity, bias=float(R * (w + 2) if w < 6 else 0))
        else:
            vts(A("SI", ALL, w), A("shipI"), float(R * (w + 2) if w < 6 else 0), None, ALU.add)

    pieces, lists, w0, l0 = {}, {}, 0, 0
    vcopy(C("L7", 0, 105), A("SI"))
    act(A("diagI"), A("negI"), scale=-(7.0 * R - BLK + 8 * H) / (R - H))
    for w in range(CFG["wt"], CFG["wt2"]):
        act(Wt(w), A("negI"), scale=-float(w + 1))
    for fn, b0, b1 in ((act, CFG["cut0"], NB), (vcopy, 0, CFG["cut0"])):
        if b0 < b1:
            fn(C("PK0", 7 * H * b0, 7 * H * b1), IND(C("VV", 2 * R, 10 * R), C("L7", 21 * b0, 21 * b1)))
    chain.clear()
    for w in range(CFG["wt2"], 6):
        act(Wt(w), A("negI"), scale=-float(w + 1))
    hold.clear()
    exchange("a0", lambda b: half("PK0", b, 7 * H), lambda b: blk("VV", Z0, b, 0, 7))
    for i, nw in enumerate(CFG["pieces"]):
        if nw not in lists:
            lists[nw], l0 = l0, l0 + 15 * nw + nw % 2
            if CFG["u16S"]:
                act(C("LP", lists[nw], lists[nw] + 15 * nw), A("SI", ALL, slice(0, nw)), ACT.Identity, bias=-2.0 * R)
            else:
                vts(C("LP", lists[nw], lists[nw] + 15 * nw), A("SI", ALL, slice(0, nw)), -2.0 * R, None, ALU.add)
        pieces[w0 + nw - 1] = (i, w0, nw, lists[nw])
        w0 += nw
    vtr(A("OT"), A("CH"))
    for ci in range(2):
        for gj in range(2):
            mm(bank(4, 112 * ci, 112), LL(ci, gj), A("OT", ALL, slice(16 * gj, 16 * gj + 16, 2)), gj == 0)
    for ci in range(2):
        for gj in range(2):
            mm(A("PS", 5, slice(ci, 28, 2)), LL(ci, gj), A("OT", ALL, 16 * gj + 1), gj == 0)
    for ci in range(2):
        (act if CFG["cn"][0] == "S" else vcopy)(A("Cn", slice(ci, 28, 2)), bank(4, 112 * ci, 112))
    c1, sp = A("Cn", slice(0, 28), 0), A("SP")
    vtt(A("wm"), bank(5, 0, 28), c1, ALU.is_gt)
    vtt(A("wd"), half("spotI", 1, 28), half("spotI", 0, 28), ALU.subtract)
    vtt(A("we"), A("wm"), A("wd"), ALU.mult)
    vtt(half("SP", 0, 28), half("spotI", 1, 28), A("we"), ALU.subtract)
    vtt(half("SP", 1, 28), half("spotI", 0, 28), A("we"), ALU.add)
    for t in range(2):
        vcopy(C("spotK", t, 56, 2), half("SP", t, 28))
    vtt(A("Cn", slice(28, 56), 0), bank(5, 0, 28), c1, ALU.max)
    vcopy(A("Cn", slice(28, 56), slice(1, 8)), A("Cn", slice(0, 28), slice(1, 8)))
    own = {0: (2, 336), 1: (2, 0), 2: (0, 0), 3: (1, 0), 4: (5, 0), 5: (6, 0), 6: (7, 0), 7: (3, 0)}

    def repeat(x):
        (b, z), c0 = own[x], 0 if x else 28
        for w in range(6 if CFG["rep"] == "pe" else 0):
            mm(A("PS", b, slice(z + w, z + 6 * (56 - c0), 6)), A("Ih"), A("Cn", slice(c0, 56), x), True)
    for x in range(2, 8):
        repeat(x)
    for w in range(0 if CFG["rep"] == "pe" else 6):
        vcopy(A("Crep", ALL, ALL, w), A("Cn"))
    def affine(name, o, i, scale, bias, extra=()):
        if name in CFG["onV"]:
            vts(o, i, scale, bias, ALU.mult, ALU.add, extra=extra)
        else:
            act(o, i, ACT.Identity, bias=bias, scale=scale, extra=extra)

    for t in range(2):
        q = C("mk", 3, 4)
        affine("MS", half("MS", t, 28), A("wm"), float(R if t else -R), q[0], extra=[q])
    vtt(A("LS"), A("MS"), A("N16"), ALU.add)
    act(A("AS"), IND(C("VV", 0, 2 * R), A("LS")))
    affine("s1", A("s1"), sp, 1.0 / H, -471.5 / H)
    vcopy(A("s2"), A("s1"))
    vts(A("s8"), sp, float(R), float(R - H), ALU.is_lt, ALU.mult)
    vts(A("s3"), A("s2"), -1.0, float(BLK - H), ALU.max, ALU.mult)
    affine("s7", A("s7"), A("s8"), (1.0 / R - 1.0 / H) / (R - H), 1.0 / H)
    nA = bank(4, R, 56)
    for i, (m, x) in enumerate((("negI", A("s4")), ("negI", sp), ("ownI", A("s8")), ("negI", A("s3")))):
        mm(nA, A(m), x, i == 0)
    vtt(A("nAB", ALL, 0), nA, A("s7"), ALU.mult)
    nD = bank(3, 400, 56)
    for i, (m, x) in enumerate((("negI", sp), ("diagI", A("s8")), ("negI", A("s3")))):
        mm(nD, A(m), x, i == 0)
    vts(A("spotD"), nD, -1.0, 7 * R + 7 * H + 0.25, ALU.mult, ALU.add)
    affine("nAB", A("nAB", ALL, 1), A("nAB", ALL, 0), 1.0, 0.0)
    for k in range(2):
        affine("B", A("Brep", ALL, k), A("s8"), 1.0, float(H))

    for c0, c2, who in CFG["turn"]:
        o, i = C("GK", 32 * c0, 32 * c2), IND(A("CI"), C("spotK", 2 * c0, 2 * c2))
        if who == "S":
            act(o, i, ACT.Identity, bias=MID, extra=[od])
        else:
            vts(o, i, MID, None, ALU.add, extra=[od])
    for c0, c2, who in CFG["turn"]:
        vtr(A("GT", slice(c0, c2)), C("GK", 32 * c0, 32 * c2))
        for t in range(2):
            for gj in range(2):
                mm(bank(2, 168 * t + 6 * c0, 6 * (c2 - c0)), LL(t, gj),
                   A("GT", slice(c0, c2), slice(16 * gj + 4, 16 * gj + 16, 2)), gj == 0)
    if CFG["rep"] == "pe":
        (act if CFG["gs"] == "S" else vcopy)(A("GS"), bank(2, 0, 336))
    for tab in ("T1", "T2"):
        zero(C(tab, 0, R))
        zero(blk(tab, 0, 0, -1, 0))
        for b in range(NB):
            zero(blk(tab, 0, b, 6, 7 if b == NB - 1 else 8))
    nadd = sum(m[2:] == "M" for m in CFG["modes"][2])
    adds = []

    def add_y(z, src, sem):
        adds.append(sem)
        op("pool", lambda: g.dma_start(T.y[:, z:z + 2 * R], src[0], accum_op=ALU.add), [src], [(None, "y", ((1 << 2 * R) - 1) << z)],
           sem=sem, count=16, cost=1.0, lag=CFG["addlag"])
        op("sync", None, [(None, "y", ((1 << R) - 1) << z)], [], sem="stored", cost=CFG["addwire"], lag=0.0)
    if nadd:
        op("pool", lambda: g.dma_start(T.y[:, 3 * R:(3 + nadd) * R], T.val[:, 3 * R:(3 + nadd) * R]), [],
           [(None, "y", ((1 << nadd * R) - 1) << 3 * R)], sem="pre", count=16, cost=2.0, lag=4.0)

    def compare(x):
        ts = slice(0 if x else 1, 2)
        if CFG["rep"] != "pe":
            vtt(A("EQ", ts, slice(28 * x, 28 * x + 28)), bank(2, 168 * ts.start, 336 - 168 * ts.start),
                A("Crep", slice(28 * ts.start, 56), x), ALU.is_equal)
            return
        vtt(A("EQ", ts, slice(28 * x, 28 * x + 28)), bank(own[x][0], own[x][1], 336 - 168 * ts.start),
            C("GS", 168 * ts.start, 336), ALU.is_equal)

    def address(ch, o):
        s, n = ch[0], len(ch)
        ts, cs = slice(0 if s else 1, 2), slice(28 * s, 28 * (s + n))
        mm(o, A("negI"), A("nAB", ts, slice(0, n)), True)
        for w in range(6):
            mm(o, half("Wt", w, 128), A("EQ", ts, cs, w), False)
        vtt(A("OFF", ts, cs), o, A("Brep", ts, slice(0, n)), ALU.mult)

    for ch, wb in zip(CFG["chunks"], CFG["abank"]):
        for x in ch:
            compare(x)
        address(ch, bank(wb, 0, 56 * len(ch)))
    repeat(0)
    repeat(1)
    mm(bank(0), A("nIb"), half("AS", 0), True)
    mm(bank(1), Wt(0), half("AS", 1), True)
    (act if CFG["u16S"] else vcopy)(A("spotU"), A("spotI"))

    def second_x():
        if CFG["x2pe"]:
            vtt(A("SQ2"), IND(C("VV", 2 * R, Z0 + TW), half("spotD", 1, 28)), half("AS", 1), ALU.mult)
            mm(bank(1), half("Wt", 1, 128), half("AS", 1), True)
            mm(bank(1), A("negI"), A("SQ2"), False)
            act(half("XS2", 1), bank(1))
        else:
            vtt(half("XS2", 1), bank(1), half("RK1", 1), ALU.mult)

    def last_lists():
        vtt(half("OFL", 0, 28), A("OFF", 1, slice(0, 28)), A("wm"), ALU.mult)
        vtt(half("OFL", 1, 28), A("OFF", 1, slice(0, 28)), half("OFL", 0, 28), ALU.subtract)

    def first_r(t):
        sign = -1.0 if t else 1.0
        act(half("RK1", t), IND(C("VV", 2 * R, Z0 + TW), half("spotD", t, 28)), ACT.Identity, bias=2.0 * sign, scale=-sign)
    fill = {"rk": lambda: act(A("RK1"), IND(C("VV", 2 * R, Z0 + TW), A("spotD")), ACT.Identity, bias=2.0, scale=-1.0),
            "rk0": lambda: first_r(0), "rk1": lambda: first_r(1), "x2": second_x, "lists": last_lists,
            "sq": lambda: act(A("SQ"), plane(2), ACT.Square, bias=2.0, scale=-1.0),
            "posI": lambda: act(A("posI"), A("negI"), scale=-1.0), "n2I": lambda: act(A("n2I"), A("negI"), scale=2.0)}
    for name in CFG["fill"][0]:
        fill[name]()

    cu, cp = [0], [0]
    low3 = CFG["modes"][2][CFG["order3"].index(0)]

    def sweep(k):
        order = [2, 3, 4, 5, 6, 7] if k < 2 else CFG["order3"]
        modes = dict(zip(order, CFG["modes"][k]))
        if k < 2:
            modes[0], modes[1] = "-" + CFG["low"][k], CFG["diag"][k]
        win = [C("VV", Z0, Z0 + TW), A("T1"), A("T2")][k]
        xs = [(half("AS", 0), half("AS", 1)), (A("X1"), half("AS", 1)), (half("XS2", 0), half("XS2", 1))][k]
        nx0 = bank([0, 2, 0][k])
        out_tab, pk = [("T1", "PK1"), ("T2", "PK2"), (None, None)][k]
        ub, pb, ab, banks = {}, {}, {}, list(CFG["banks"][k])

        def off(s, t, n=1):
            if s == 0 and k == 2:
                return C("OFL", 28 * t, 28 * (t + n))
            return A("OFF", t, slice(28 * s, 28 * (s + n)))

        def gather(s):
            if s == 0 and k == 2 and low3 == "AA" and 0 in CFG["gp"][k] and (0, 0) not in ub:
                u = "U%d" % (cu[0] % NU)
                cu[0] += 1
                act(A(u), IND(win, A("OFL")))
                ub[0, 0], ub[0, 1] = half(u, 0), half(u, 1)
            for t in range(2):
                if modes[s][t] == "A" and (s, t) not in ub:
                    n = 2 if s in CFG["gp"][k] and modes[s + 1][t] == "A" else 1
                    u = "U%d" % (cu[0] % NU)
                    cu[0] += 1
                    act(C(u, 0, R * n), IND(win, off(s, t, n)))
                    for i in range(n):
                        ub[s + i, t] = half(u, i)

        def product(s, t, x):
            pb[s, t] = A("P%d" % (cp[0] % NP))
            cp[0] += 1
            if modes[s][t] == "A":
                vtt(pb[s, t], ub[s, t], bank(1), ALU.mult)
            else:
                vtt(pb[s, t], IND(win, off(s, t)), xs[x], ALU.mult)
            return pb[s, t]

        def added(s):
            s0 = s - s % 2
            for t in (1, 0):
                o = half("Q%d%d" % (s0 // 2 - 1, t), s % 2)
                if modes[s][t] == "A":
                    vtt(o, ub[s, t], bank(1) if t else nx0, ALU.mult)
                else:
                    vtt(o, IND(win, off(s, t)), xs[t], ALU.mult)
            if s % 2:
                add_y(R * (s0 + 1), A("Q%d1" % (s0 // 2 - 1)), "add%d1" % (s0 // 2 - 1))
            for x in range(nadd // 2 if s == nadd + 1 else 0):
                add_y(R * (2 * x + 3), A("Q%d0" % x), "add%d0" % x)

        def products(s, b):
            ab[s], a = b, plane(s + 1)
            mm(bank(b), Wt(0), a, True)
            if modes[s][0] == "A":
                vtt(bank(b), ub[s, 0], nx0, ALU.mult)
                mm(bank(b), Wt(0), a, False)
            else:
                mm(bank(b), A("negI"), product(s, 0, 0), False)
            p = product(s, 1, 1)
            if modes[s][2:] != "V":
                mm(bank(b), A("posI" if k == 2 else "negI"), p, False)

        def finish(s):
            if s in CFG["fp"][k] or modes[s][2] == "M":
                return
            s0 = s - 1 if s - 1 in CFG["fp"][k] else s
            parts = [(0, R // 2, "scalar"), (R // 2, R // 2, "sync")] if k == 2 and s == order[-1] else [(0, R * (s - s0 + 1), "sync")]
            for a, n, q in parts:
                z = R * (s0 - 1) + a if k < 2 else R * (s0 + 1) + a
                o = C(out_tab or "YY", z, z + n)
                if modes[s][2] == "V":
                    vtt(o, bank(ab[s], a, n), C(pb[s, 1][1], a, a + n), ALU.add if k == 2 else ALU.subtract)
                elif s0 < s:
                    act(o, A("PS", slice(ab[s0], ab[s] + 1), slice(0, R)))
                else:
                    act(o, bank(ab[s], a, n))
                if k == 2:
                    store(q, T.y[:, z:z + n], o)
            for i, w0, nw, l0 in [pieces[x - 2] for x in range(s0, s + 1) if k < 2 and x - 2 in pieces]:
                n, z = H * nw, NB * H * w0
                cut = CFG["cut"][k][i]
                for fn, b0, b1 in ((vcopy, 0, cut), (act, cut, NB)):
                    if b0 < b1:
                        fn(C(pk, z + b0 * n, z + b1 * n),
                           IND(C(out_tab, R * (w0 + 1), R * (w0 + nw + 1)), C("LP", l0 + 3 * nw * b0, l0 + 3 * nw * b1)))
                exchange("a%d%d" % (k + 1, i), lambda b: C(pk, z + n * b, z + n * (b + 1)), lambda b: blk(out_tab, 0, b, w0, w0 + nw))

        def last_lower():
            for t in range(2):
                b, o = bank(banks.pop(0)), half("YY", t)
                mm(b, Wt(0), plane(t), True)
                if modes[0][t] == "A":
                    vtt(b, ub[0, t], bank(1), ALU.mult)
                    mm(b, Wt(0), plane(t), False)
                else:
                    mm(b, A("posI"), product(0, t, 1), False)
                vtt(o, b, half("RK2", t), ALU.mult)
                store("sync", T.y[:, R * t:R * (t + 1)], o)

        for i, s in enumerate(order):
            for x in order[i:i + 1 + CFG["ahead"]]:
                gather(x)
            if s == 0:
                last_lower()
            elif modes[s][2] == "M":
                added(s)
            else:
                products(s, banks.pop(0))
            behind_v = max(j for j, o in enumerate(ops) if o["q"] == "vector")
            if i and order[i - 1]:
                finish(order[i - 1])
        finish(order[-1])
        if k == 2:
            return

        if CFG["hold"]:
            hold.update(vector=behind_v, scalar=max(j for j, o in enumerate(ops) if o["q"] == "scalar"))
        if k == 0:
            compare(0)
            compare(1)
            address([0], bank(3, 0, 28))
            address([1], bank(3, 32, 56))
        for name in CFG["fill"][k + 1]:
            fill[name]()
        gather(1)
        gather(0)
        b0 = bank(2 if k == 0 else banks.pop(0))
        mm(b0, A("nIb"), half("AS", 0), True)
        if modes[0][1] == "A":
            vtt(b0, ub[0, 1], bank(1), ALU.mult)
            mm(b0, A("nIb"), half("AS", 0), False)
        else:
            mm(b0, A("posI"), product(0, 1, 1), False)
        if k == 1:
            vtt(bank(0), b0, half("RK1", 0), ALU.mult)
        if any(m[0] == "D" and len(m) == 3 for m in CFG["modes"][k + 1]) or any(m[0] == "D" for m in CFG["diag"][k + 1:]):
            act(A("X1") if k == 0 else half("XS2", 0), bank(2 if k == 0 else 0), scale=-1.0)
        products(1, 3)
        if modes[1][2:] == "V":
            vtt(bank(3), bank(3), pb[1, 1], ALU.subtract)
        if k == 1 and not CFG["x2pe"] and (any(m[1] == "A" for m in CFG["modes"][2]) or "A" in low3):
            act(bank(1), half("XS2", 1))
        e, rn = bank(CFG["rsq"][k]), (half("RT2", 0) if k == 0 else A("R3"))
        if k == 0 or CFG["r3"] == "pe":
            mm(e, Wt(0), plane(2), True)
        vtt(e, bank(3), A("SQ"), ALU.mult)
        if k == 1 and CFG["r3"] != "pe":
            act(A("SQ2"), half("RT2", 0), scale=2.0)
            vtt(rn, A("SQ2"), e, ALU.subtract)
        if k == 0:
            mm(e, Wt(1), plane(2), False)
            act(rn, e, ACT.Identity, bias=4.0, scale=-1.0)
            act(A("PR2"), IND(rn, ship))
            exchange("ar2", lambda b: half("PR2", b, H), lambda b: C("RT2", R + H * b, R + H * (b + 1)))
            act(A("SQ"), rn, ACT.Square)
        else:
            if CFG["r3"] == "pe":
                mm(e, A("n2I"), half("RT2", 0), False)
                act(rn, e, scale=-1.0)
            store("sync", T.inv[:], rn)
            act(A("RK2"), IND(A("RT2"), A("spotU")))
        hold.clear()

    for k in range(3):
        sweep(k)

    for o in ops:
        o["acc"] = [(n, m, True, _banks(m) if n == "PS" else 0) for n, m in o["w"]] + [(n, m, False, _banks(m) if n == "PS" else 0) for n, m in o["r"]]
    deps, behind = [], []
    users, lastdma = {}, {}
    for j, o in enumerate(ops):
        d, f = set(), set()
        for n2, m2, w2, b2 in o["acc"]:
            for i, m1, w1, b1 in users.get(n2, ()):
                q1 = ops[i]["q"]
                if q1 == "tensor" and o["q"] == "tensor":
                    if b1 & b2:
                        f.add(i)
                elif o["q"] != "arrive" and ((b1 & b2 and q1 != o["q"]) or ((w1 or w2) and m1 & m2)):
                    d.add(i)
        if o["hold"] is not None and o["hold"] not in d:
            f.add(o["hold"])
        if o["q"] == "arrive":
            f.update((j - 2, j - 1))
        elif o["sem"] not in (None, "stored") or o["q"] == "pool":
            if o["q"] in lastdma:
                f.add(lastdma[o["q"]])
            lastdma[o["q"]] = j
        if o["sem"] not in ("remote", "stored"):
            for n2, m2, w2, b2 in o["acc"]:
                users.setdefault(n2, []).append((j, m2, w2, b2))
        deps.append(sorted(d))
        behind.append(sorted(f))
    if not ORDER:
        ORDER.extend(CFG.get("fixed") or issue_order(ops, deps, behind))
    place = {j: p for p, j in enumerate(ORDER)}
    needed = set()
    for j, o in enumerate(ops):
        o["latest"] = {ops[i]["q"]: i for i in sorted(deps[j], key=place.get) if ops[i]["sem"] is None}
        needed.update(o["latest"].values())
    cnt = {"vector": 0, "scalar": 0, "tensor": 0, "pool": 0}
    for j in ORDER:
        o = ops[j]
        if o["sem"] is not None:
            o["tok"] = (o["sem"], o["n"])
        elif j in needed:
            cnt[o["q"]] += 1
            o["tok"] = (o["q"], cnt[o["q"]])
    queue = {"vector": g.vector, "scalar": g.scalar, "tensor": g.tensor, "pool": g, "sync": g.sync}
    seen = {q: {} for q in queue}
    for j in ORDER:
        o = ops[j]
        if o["fn"] is None:
            continue
        want = [ops[i]["tok"] for i in o["latest"].values()] + [ops[i]["tok"] for i in deps[j] if ops[i]["sem"] is not None]
        for s, n in want:
            if seen[o["q"]].get(s, 0) < n:
                queue[o["q"]].wait_ge(T.sem[s], n)
                seen[o["q"]][s] = n
        ins = o["fn"]()
        if o["sem"] is None:
            if j in needed:
                ins.then_inc(T.sem[o["q"]], 1)
        elif o["sem"] != "remote":
            ins.then_inc(T.sem[o["sem"]], 16)
    for sem in adds:
        g.wait_ge(T.sem[sem], 16)
    g.wait_ge(T.sem["sent"], nsent[0])
    g.sync.wait_ge(T.sem["stored"], nstore[0])
